import numpy as np
import ml_dtypes


def mxq(x, axis, fmt="e4m3"):
    dtype, down = {"e4m3": (ml_dtypes.float8_e4m3fn, 7), "e5m2": (ml_dtypes.float8_e5m2, 14)}[fmt]
    v = np.moveaxis(np.asarray(x, np.float32).astype(ml_dtypes.bfloat16).astype(np.float64), axis, -1)
    blocks = v.reshape(v.shape[:-1] + (-1, 32))
    amax = np.abs(blocks).max(-1, keepdims=True)
    byte = np.maximum(np.where(amax > 0, np.frexp(amax)[1] - 1 + 127, 0) - down, 1)
    scale = np.exp2(byte - 127.0)
    codes = (blocks / scale).astype(np.float32).astype(dtype).astype(np.float64)
    return np.moveaxis((codes * scale).reshape(v.shape), -1, axis)


WIDE = False


def mx_kscale(k):
    if not WIDE:
        return np.ones(k)
    levels = np.array([10, -10, 5, -5, 0])
    if k % 512:
        return np.exp2(np.random.permutation(np.resize(levels, k // 32))).repeat(32)
    a = np.empty((k // 512, 16))
    for p in range(k // 512):
        a[p, :8] = np.random.permutation(np.resize(levels, 8))
        for g in range(8):
            far = levels[np.abs(levels - a[p, g]) >= 10]
            a[p, g + 8] = far[np.random.randint(len(far))]
    return np.exp2(a.ravel()).repeat(32)


BF16 = ml_dtypes.bfloat16


def bf(x):
    return np.asarray(x, np.float32).astype(BF16)


def f64(x):
    return np.asarray(x).astype(np.float64)


E2M1 = np.array([0.0, 0.5, 1.0, 1.5, 2.0, 3.0, 4.0, 6.0, -0.0, -0.5, -1.0, -1.5, -2.0, -3.0, -4.0, -6.0])


def pack_weight(w, fmt):
    k, n = w.shape
    w = f64(bf(w)).reshape(k // 32, 32, n)
    amax = np.abs(w).max(1)
    if fmt == "e4m3":
        byte = np.frexp(amax)[1] - 1 + 127 - 7
    else:
        mant, ex = np.frexp(amax / 6.0)
        byte = np.where(mant > 0.5, ex, ex - 1) + 127
    byte = np.clip(np.where(amax > 0, byte, 1), 1, 254)
    scaled = (w * np.exp2(127.0 - byte)[:, None, :]).reshape(k, n).astype(np.float32)
    by_word = np.ascontiguousarray(scaled.reshape(k // 512, 128, 4, n).transpose(0, 1, 3, 2))
    if fmt == "e4m3":
        words = by_word.astype(ml_dtypes.float8_e4m3fn).view(np.uint8)
    else:
        c = by_word.astype(ml_dtypes.float4_e2m1fn).view(np.uint8) & 0xF
        words = c[..., 0::2] | (c[..., 1::2] << 4)
    return np.ascontiguousarray(words), np.ascontiguousarray(byte.astype(np.uint8).reshape(k // 512, 16, n))


def unpack_weight(words, scales, fmt):
    g, p, n, _ = words.shape
    if fmt == "e4m3":
        vals = np.ascontiguousarray(words).view(ml_dtypes.float8_e4m3fn).astype(np.float64)
    else:
        nib = np.empty((g, p, n, 4), np.uint8)
        nib[..., 0::2] = words & 0xF
        nib[..., 1::2] = words >> 4
        vals = E2M1[nib]
    vals = vals * np.repeat(np.exp2(scales.astype(np.float64) - 127.0), 8, axis=1)[..., None]
    return vals.transpose(0, 1, 3, 2).reshape(g * 512, n)


N, D, K = 2048, 1024, 512


def scale_rows(gain, m):
    return gain[:, None] * m


def draw0():
    s = mx_kscale(D)
    u = mx_kscale(N)
    x = bf(np.random.standard_normal((N, D)) * s)
    p_words, p_scales = pack_weight(np.random.standard_normal((D, D)) / np.sqrt(D) / s[:, None], "e4m3")
    beta_words, beta_scales = pack_weight(np.random.standard_normal((D, K)) / np.sqrt(D) / s[:, None], "e4m3")
    return {
        "x": x,
        "p_words": p_words,
        "p_scales": p_scales,
        "beta_words": beta_words,
        "beta_scales": beta_scales,
        "r": bf(np.random.uniform(0.5, 1.5, N) * u),
        "t": bf((1.0 + 0.3 * np.random.standard_normal(N)) / u),
        "v": bf(np.random.standard_normal((D, K)) / np.sqrt(D)),
        "psi": bf(np.random.uniform(0.05, 0.2, D)),
    }


def core(x, p_words, p_scales, beta_words, beta_scales, r, t, v, psi):
    n_cases = x.shape[0]
    xq = mxq(f64(x), 1, "e4m3")
    e0 = xq @ unpack_weight(p_words, p_scales, "e4m3")
    e = scale_rows(f64(r), e0)
    z0 = xq @ unpack_weight(beta_words, beta_scales, "e4m3")
    z = scale_rows(f64(t), z0)
    c = mxq(e, 0, "e4m3").T @ mxq(z, 0, "e4m3")
    return (c / n_cases - f64(v)) / f64(psi)[:, None]


def e4m3fn_bytes(y):
    return np.clip(np.asarray(y, np.float64), -448.0, 448.0).astype(np.float32).astype(ml_dtypes.float8_e4m3fn).view(np.uint8)


def e4m3fn_values(b):
    return np.asarray(b, np.uint8).view(ml_dtypes.float8_e4m3fn).astype(np.float64)


def setup_inputs():
    d = draw0()
    x0 = np.asarray(d['x']).astype(np.float64)
    s = (np.max(np.abs(x0), axis=(0,), keepdims=True) / 448.0).astype(np.float32)
    out = {}
    for k, v in d.items():
        if k == 'x':
            out['x_bytes'] = e4m3fn_bytes(x0 / s.astype(np.float64))
            out['x_scale'] = s
        else:
            out[k] = v
    return out


def reference(x_bytes, x_scale, p_words, p_scales, beta_words, beta_scales, r, t, v, psi):
    return core(e4m3fn_values(x_bytes) * x_scale.astype(np.float64), p_words, p_scales, beta_words, beta_scales, r, t, v, psi)

@@ -1,0 +1,433 @@
+from contextlib import ExitStack
+
+import concourse.mybir as mybir
+from concourse.masks import make_identity
+
+N, D, K = 2048, 1024, 512
+FLOPS = 2 * N * D * (D + K) + 2 * N * D * K
+
+F32 = mybir.dt.float32
+BF16 = mybir.dt.bfloat16
+U32 = mybir.dt.uint32
+I32 = mybir.dt.int32
+U8 = mybir.dt.uint8
+FP8 = mybir.dt.float8_e4m3fn
+X4 = mybir.dt.float8_e4m3fn_x4
+MULT = mybir.AluOpType.mult
+SUBTRACT = mybir.AluOpType.subtract
+COPY = mybir.ActivationFunctionType.Copy
+ENGINE = mybir.EngineType
+
+P = 128
+PACK = 4
+GROUPS = N // (P * PACK)
+HALVES = D // (P * PACK)
+TILES = GROUPS * PACK
+STEPS = TILES // 2
+HALF = D // 2
+CHUNKS = HALF // P
+OUT_TILES = D // P
+
+LATE_TILES = 8
+R, T = 0, 1
+
+
+def tile_factoranalysisemloadinggradient_w8_kernel(
+    tc, x_bytes, x_scale, p_words, p_scales, beta_words, beta_scales, r, t, v, psi, out
+):
+    nc = tc.nc
+    with ExitStack() as ctx:
+        keep = ctx.enter_context(tc.tile_pool(name="keep", bufs=1))
+        widened_pool = ctx.enter_context(tc.tile_pool(name="widened_pool", bufs=8))
+        woven_pool = ctx.enter_context(tc.tile_pool(name="woven_pool", bufs=3))
+        narrow_pool = ctx.enter_context(tc.tile_pool(name="narrow_pool", bufs=2))
+        result_pool = ctx.enter_context(tc.tile_pool(name="result_pool", bufs=8))
+        banks = ctx.enter_context(tc.psum_pool(name="banks", bufs=8))
+
+        scale_cols = keep.tile([P, HALVES, PACK], F32, name="scale_cols")
+        nc.scalar.dma_start(out=scale_cols[:], in_=x_scale.rearrange("o (j p c) -> p (o j) c", p=P, c=PACK))
+
+        x_cases = x_bytes.rearrange("(g m c) k -> g m c k", m=P, c=PACK)
+        x_raw = []
+        for g in range(GROUPS):
+            x_raw.append(keep.tile([P, PACK, D], U8, name="x_raw%d" % g))
+
+        def load_x(g, lo, hi):
+            nc.sync.dma_start(out=x_raw[g][:, lo:hi, :], in_=x_cases[g][:, lo:hi, :])
+
+        w_scales = keep.tile([P, D + K], U8, name="w_scales", align_bytes=64)
+        nc.vector.memset(w_scales[:].bitcast(I32), 0)
+
+        def load_scales(scales, width, col):
+            rows_in = scales.bitcast(I32)
+            for q in range(4):
+                nc.sync.dma_start(
+                    out=w_scales[32 * q : 32 * q + 4 * HALVES, col : col + width].bitcast(I32),
+                    in_=rows_in[:, 4 * q : 4 * q + 4, :],
+                )
+
+        zeros = keep.tile([P, K], BF16, name="zeros")
+        nc.gpsimd.memset(zeros[:], 0.0)
+        ident = keep.tile([P, P], F32, name="ident")
+        make_identity(nc, ident[:])
+
+        beta_codes = keep.tile([P, HALVES, K * PACK], U8, name="beta_codes", align_bytes=64)
+        p_codes = []
+        for h in range(2):
+            p_codes.append(keep.tile([P, HALVES, HALF * PACK], U8, name="p_codes%d" % h, align_bytes=64))
+        p_rows = p_words.rearrange("g p n c -> p g (n c)")
+        x_scale_row = x_scale.rearrange("o k -> (o k)")
+        x_scales = keep.tile([P, D], F32, name="x_scales")
+        rt_in = keep.tile([P, 2, GROUPS, PACK], BF16, name="rt_in")
+        psi_in = keep.tile([P, OUT_TILES, 2], BF16, name="psi_in")
+        v_in = keep.tile([P, OUT_TILES, K], BF16, name="v_in")
+
+        load_x(0, 0, 1)
+        load_x(0, 1, PACK)
+        load_scales(beta_scales, K, D)
+        nc.sync.dma_start(out=beta_codes[:], in_=beta_words.rearrange("g p n c -> p g (n c)"))
+        nc.sync.dma_start(out=p_codes[0][:], in_=p_rows[:, :, 0 : HALF * PACK])
+        with nc.allow_non_contiguous_dma(reason="vectors of one value a case or a row, laid on the partitions"):
+            nc.sync.dma_start(out=rt_in[:, T, :, :], in_=t.rearrange("(g m c) -> m g c", m=P, c=PACK))
+            nc.sync.dma_start(out=rt_in[:, R, :, :], in_=r.rearrange("(g m c) -> m g c", m=P, c=PACK))
+        load_scales(p_scales, D, 0)
+        load_x(1, 0, 2)
+        load_x(1, 2, PACK)
+        nc.sync.dma_start(out=x_scales[:], in_=x_scale_row.partition_broadcast(P))
+        nc.sync.dma_start(out=p_codes[1][:], in_=p_rows[:, :, HALF * PACK : D * PACK])
+        load_x(2, 0, PACK)
+        load_x(3, 0, PACK)
+        with nc.allow_non_contiguous_dma(reason="vectors of one value a case or a row, laid on the partitions"):
+            nc.sync.dma_start(out=psi_in[:, :, 0:1], in_=psi.rearrange("(m p o) -> p m o", p=P, o=1))
+        nc.sync.dma_start(out=v_in[:], in_=v.rearrange("(m p) k -> p m k", p=P))
+
+        rt = keep.tile([P, 2, TILES], F32, name="rt")
+        inv_psi = keep.tile([P, OUT_TILES], F32, name="inv_psi")
+        gain = keep.tile([P, OUT_TILES], F32, name="gain")
+        v_scaled = keep.tile([P, 2, K], F32, name="v_scaled")
+
+        x_codes, x_code_scales, z_codes, z_code_scales, e_codes, e_code_scales = [], [], [], [], [], []
+        for s in range(STEPS):
+            x_codes.append(keep.tile([P, 2, HALVES * P], U32, name="x_codes%d" % s, align_bytes=64))
+            x_code_scales.append(keep.tile([P, 2, HALVES * P], U8, name="x_code_scales%d" % s, align_bytes=64))
+        for g in range(GROUPS):
+            z_codes.append(keep.tile([P, K], U32, name="z_codes%d" % g, align_bytes=64))
+            z_code_scales.append(keep.tile([P, K], U8, name="z_code_scales%d" % g, align_bytes=64))
+            e_codes.append(keep.tile([P, D], U32, name="e_codes%d" % g, align_bytes=64))
+            e_code_scales.append(keep.tile([P, D], U8, name="e_code_scales%d" % g, align_bytes=64))
+
+        widened, transposed, woven_x = {}, {}, {}
+        idle_bank = banks.tile([P, K], F32, name="bank")
+
+        def keep_busy(count):
+            for n in range(count):
+                nc.tensor.matmul(out=idle_bank[:], lhsT=zeros[:, 0:P], rhs=zeros[:], start=True, stop=True)
+
+        def widen(i, copy):
+            g, c = divmod(i, PACK)
+            widened[i] = widened_pool.tile([P, D], BF16, name="widened")
+            for j in range(HALVES):
+                cols = slice(j * HALF, (j + 1) * HALF)
+                copy(out=widened[i][:, cols], in_=x_raw[g][:, c, cols].bitcast(FP8))
+
+        def widen_and_scale(i):
+            g, c = divmod(i, PACK)
+            widened[i] = widened_pool.tile([P, D], BF16, name="widened")
+            nc.vector.tensor_tensor(
+                out=widened[i][:], in0=x_raw[g][:, c, :].bitcast(FP8), in1=x_scales[:], op=MULT
+            )
+
+        def transpose(i):
+            words = widened[i][:].bitcast(F32)
+            bank = banks.tile([P, HALVES, 2, P], F32, name="bank")
+            transposed[i] = bank
+            for j in range(HALVES):
+                for u in range(2):
+                    nc.tensor.transpose(bank[:, j, u, :], words[:, 256 * j + u : 256 * (j + 1) : 2], ident[:])
+
+        def woven_tile(i):
+            s, h = divmod(i, 2)
+            if h == 0:
+                woven_x[s] = woven_pool.tile([P, 2, HALVES * P * PACK], BF16, name="woven_x", align_bytes=64)
+            return woven_x[s][:, h, :]
+
+        def scale_out(i):
+            woven = woven_tile(i)
+            for j in range(HALVES):
+                scales = scale_cols[:, j, :].rearrange("p (u e) -> p u e", e=2)
+                nc.vector.tensor_tensor(
+                    out=woven[:, j * P * PACK : (j + 1) * P * PACK].rearrange("p (m u e) -> p m u e", u=2, e=2),
+                    in0=transposed[i][:, j, :, :].bitcast(BF16).rearrange("p u (m e) -> p m u e", e=2),
+                    in1=scales.unsqueeze(1).to_broadcast([P, P, 2, 2]),
+                    op=MULT,
+                )
+
+        def copy_out(i):
+            nc.scalar.copy(
+                out=woven_tile(i).bitcast(F32).rearrange("p (j m u) -> p j m u", j=HALVES, u=2),
+                in_=transposed[i][:].rearrange("p j u m -> p j m u"),
+            )
+
+        def quantize_x(i):
+            s, h = divmod(i, 2)
+            nc.vector.quantize_mx(
+                out=x_codes[s][:, h, :].bitcast(X4), scales=x_code_scales[s][:, h, :], in_=woven_x[s][:, h, :]
+            )
+
+        def quantize_x_pair(s):
+            nc.vector.quantize_mx(
+                out=x_codes[s][:].rearrange("p h w -> p (h w)").bitcast(X4),
+                scales=x_code_scales[s][:].rearrange("p h w -> p (h w)"),
+                in_=woven_x[s][:].rearrange("p h w -> p (h w)"),
+            )
+
+        def multiply(bank, i, codes, first, scale_col, width):
+            s, h = divmod(i, 2)
+            for j in range(HALVES):
+                cols = slice(j * P, (j + 1) * P)
+                nc.tensor.matmul_mx(
+                    out=bank,
+                    lhsT=x_codes[s][:, h, cols].bitcast(X4),
+                    lhsT_scale=x_code_scales[s][:, h, cols],
+                    rhs=codes[:, j, first * PACK : (first + width) * PACK].bitcast(X4),
+                    rhs_scale=w_scales[4 * j : P, scale_col : scale_col + width],
+                    start=(j == 0),
+                    stop=(j == HALVES - 1),
+                )
+
+        products, planes, woven = {}, {}, {}
+
+        def multiply_wide(kind, i):
+            bank = banks.tile([P, K], F32, name="bank")
+            products[kind, i] = bank
+            if kind == "z":
+                multiply(bank[:], i, beta_codes, 0, D, K)
+            else:
+                multiply(bank[:], i, p_codes[0], 0, 0, HALF)
+
+        def scale_wide(kind, i):
+            g, c = divmod(i, PACK)
+            if c == 0:
+                planes[kind, g] = keep.tile([P, PACK, K], BF16, name="%s_planes%d" % (kind, g))
+                woven[kind, g] = keep.tile([P, K, PACK], BF16, name="%s_woven%d" % (kind, g), align_bytes=64)
+            factor = T if kind == "z" else R
+            nc.scalar.activation(
+                out=planes[kind, g][:, c, :], in_=products[kind, i][:], func=COPY, scale=rt[:, factor, i : i + 1]
+            )
+
+        def weave(kind, g, lo, hi, copy):
+            copy(
+                out=woven[kind, g][:, lo:hi, :].rearrange("p (b n) c -> p b c n", n=4),
+                in_=planes[kind, g][:, :, lo:hi].rearrange("p c (b n) -> p b c n", n=4),
+            )
+
+        def quantize_wide(kind, g):
+            codes, scales = (z_codes, z_code_scales) if kind == "z" else (e_codes, e_code_scales)
+            nc.vector.quantize_mx(
+                out=codes[g][:, 0:K].bitcast(X4),
+                scales=scales[g][:, 0:K],
+                in_=woven[kind, g][:].rearrange("p n c -> p (n c)"),
+            )
+
+        narrow = {}
+
+        def multiply_narrow(g, chunk):
+            bank = banks.tile([P, PACK, P], F32, name="bank")
+            products[g, chunk] = bank
+            for c in range(PACK):
+                multiply(bank[:, c, :], g * PACK + c, p_codes[1], P * chunk, HALF + P * chunk, P)
+
+        def scale_narrow(g, chunk):
+            if chunk == 0:
+                narrow[g] = narrow_pool.tile([P, CHUNKS, P, PACK], BF16, name="narrow", align_bytes=64)
+            factors = rt[:, R, g * PACK : (g + 1) * PACK]
+            nc.vector.tensor_tensor(
+                out=narrow[g][:, chunk, :, :],
+                in0=products[g, chunk][:].rearrange("p c n -> p n c"),
+                in1=factors.unsqueeze(1).to_broadcast([P, P, PACK]),
+                op=MULT,
+            )
+
+        def quantize_narrow(g, lo, hi):
+            cols = slice(HALF + P * lo, HALF + P * hi)
+            nc.vector.quantize_mx(
+                out=e_codes[g][:, cols].bitcast(X4),
+                scales=e_code_scales[g][:, cols],
+                in_=narrow[g][:, lo:hi, :, :].rearrange("p b n c -> p (b n c)"),
+            )
+
+        sums = {}
+
+        def contract(m, groups, lo=0, hi=K):
+            if (m, lo) not in sums:
+                bank = banks.tile([P, K], F32, name="bank")
+                sums[m, lo] = bank
+            cols = slice(P * m, P * (m + 1))
+            for g in groups:
+                nc.tensor.matmul_mx(
+                    out=sums[m, lo][:, 0 : hi - lo],
+                    lhsT=e_codes[g][:, cols].bitcast(X4),
+                    lhsT_scale=e_code_scales[g][:, cols],
+                    rhs=z_codes[g][:, lo:hi].bitcast(X4),
+                    rhs_scale=z_code_scales[g][:, lo:hi],
+                    start=(g == 0),
+                    stop=(g == GROUPS - 1),
+                )
+
+        def finish(m):
+            difference = woven_pool.tile([P, K], F32, name="difference")
+            nc.vector.scalar_tensor_tensor(
+                out=difference[:], in0=sums[m, 0][:], scalar=1.0 / N, in1=v_in[:, m, :], op0=MULT, op1=SUBTRACT
+            )
+            result = result_pool.tile([P, K], F32, name="result")
+            nc.scalar.activation(out=result[:], in_=difference[:], func=COPY, scale=inv_psi[:, m : m + 1])
+            nc.sync.dma_start(out=out[P * m : P * (m + 1), :], in_=result[:])
+
+        def scale_v(m):
+            nc.scalar.activation(
+                out=v_scaled[:, m - 2, :], in_=v_in[:, m, :], func=COPY, scale=inv_psi[:, m : m + 1]
+            )
+
+        def finish_last(m, lo=0, hi=K):
+            result = result_pool.tile([P, K], F32, name="result")
+            nc.vector.scalar_tensor_tensor(
+                out=result[:, lo:hi],
+                in0=sums[m, lo][:, 0 : hi - lo],
+                scalar=gain[:, m : m + 1],
+                in1=v_scaled[:, m - 2, lo:hi],
+                op0=MULT,
+                op1=SUBTRACT,
+            )
+            nc.sync.dma_start(out=out[P * m : P * (m + 1), lo:hi], in_=result[:, lo:hi])
+
+        vector, scalar = nc.vector.tensor_copy, nc.scalar.copy
+        every = range(GROUPS)
+        last = GROUPS - 1
+        ctx.enter_context(tc.manual_schedule(engines={ENGINE.PE, ENGINE.Activation, ENGINE.DVE}))
+
+        keep_busy(5)
+        widen(0, vector)
+        widen(1, scalar)
+        transpose(0)
+        keep_busy(1)
+        transpose(1)
+        scale_out(0)
+        quantize_x(0)
+        widen(2, scalar)
+        multiply_wide("z", 0)
+        transpose(2)
+        scale_out(1)
+        quantize_x(1)
+        nc.vector.tensor_copy(
+            out=rt[:].rearrange("p w i -> p (w i)"), in_=rt_in[:].rearrange("p w g c -> p (w g c)")
+        )
+        widen(3, scalar)
+        scale_out(2)
+        scale_wide("z", 0)
+        multiply_wide("z", 1)
+        transpose(3)
+        widen(4, scalar)
+        scale_out(3)
+        scale_wide("z", 1)
+        widen(5, scalar)
+        quantize_x_pair(1)
+        for i in (0, 1):
+            multiply_wide("e", i)
+            scale_wide("e", i)
+
+        for s in range(1, STEPS):
+            g, h = divmod(s, 2)
+            a = 2 * s
+            if s == 1:
+                for i in range(6, LATE_TILES):
+                    widen(i, scalar)
+            ahead = (0, 2, 2, 4, 0, 4, 0, 0)[s]
+            for i in range(a + 2, a + 2 + ahead):
+                transpose(i)
+            for i in range(a + 2, a + 2 + ahead):
+                if i < LATE_TILES:
+                    scale_out(i)
+                else:
+                    copy_out(i)
+            if s == 1:
+                quantize_x_pair(2)
+            for i in range(a + 6, min(a + 8, TILES)):
+                widen_and_scale(i)
+            for kind in ("z", "e"):
+                if s == STEPS - 1 and kind == "e":
+                    multiply_narrow(g - 1, 2)
+                    multiply_narrow(g - 1, 3)
+                for i in (a, a + 1):
+                    multiply_wide(kind, i)
+                for i in (a, a + 1):
+                    scale_wide(kind, i)
+                if s == STEPS - 1 and kind == "z":
+                    weave("z", last, 256, 512, scalar)
+            if s == 6:
+                weave("z", 2, 0, 512, scalar)
+            elif 2 <= s <= 5:
+                weave("z", g - 1, 256 * h, 256 * h + 256, scalar)
+            if s == 4:
+                weave("e", 0, 0, 512, vector)
+            if s == 5:
+                quantize_wide("e", 0)
+            if s == 6:
+                weave("e", 1, 0, 512, vector)
+            if 1 < s < STEPS - 1:
+                quantize_x_pair(s + 1)
+            if s == STEPS - 1:
+                quantize_wide("e", 1)
+            if g > 0:
+                if s < STEPS - 1:
+                    multiply_narrow(g - 1, 2 * h)
+                    multiply_narrow(g - 1, 2 * h + 1)
+                if h == 0 and g > 1:
+                    quantize_wide("z", g - 2)
+                    quantize_narrow(g - 2, 0, CHUNKS)
+                scale_narrow(g - 1, 2 * h)
+                scale_narrow(g - 1, 2 * h + 1)
+            if s == 4:
+                nc.vector.reciprocal(out=inv_psi[:], in_=psi_in[:, :, 0])
+            if s == 5:
+                nc.vector.tensor_scalar(out=gain[:], in0=inv_psi[:], scalar1=1.0 / N, scalar2=None, op0=MULT)
+
+        contract(4, (0, 1))
+        for chunk in range(CHUNKS):
+            multiply_narrow(last, chunk)
+        weave("e", 2, 0, 512, scalar)
+        weave("z", last, 0, 256, vector)
+        quantize_wide("z", last - 1)
+        quantize_narrow(last - 1, 0, CHUNKS)
+        scale_narrow(last, 0)
+        quantize_wide("z", last)
+        weave("e", last, 0, 256, scalar)
+        scale_narrow(last, 1)
+        scale_narrow(last, 2)
+        quantize_narrow(last, 0, 2)
+        scale_narrow(last, 3)
+        quantize_wide("e", 2)
+        quantize_narrow(last, 2, 4)
+        contract(4, (2,))
+        contract(5, (0, 1, 2))
+        contract(6, (0, 1, 2))
+        for m in (4, 5, 6):
+            contract(m, (last,))
+        scale_v(2)
+        scale_v(3)
+        finish(4)
+        finish(5)
+        weave("e", last, 256, 512, vector)
+        quantize_wide("e", last)
+        contract(7, every)
+        finish(6)
+        contract(0, every)
+        finish(7)
+        contract(1, every)
+        finish(0)
+        contract(2, every)
+        finish(1)
+        contract(3, every, 0, 256)
+        finish_last(2)
+        contract(3, every, 256, 512)
+        finish_last(3, 0, 256)
+        finish_last(3, 256, 512)

@@ -25,10 +25,10 @@ HALVES = D // (P * PACK)
 TILES = GROUPS * PACK
 STEPS = TILES // 2
 HALF = D // 2
-CHUNKS = HALF // P
 OUT_TILES = D // P
+BANKS = 8
 
-LATE_TILES = 8
+LATE_TILES = 4
 R, T = 0, 1
 
 
@@ -38,25 +38,25 @@ def tile_factoranalysisemloadinggradient_w8_kernel(
     nc = tc.nc
     with ExitStack() as ctx:
         keep = ctx.enter_context(tc.tile_pool(name="keep", bufs=1))
-        widened_pool = ctx.enter_context(tc.tile_pool(name="widened_pool", bufs=8))
+        widened_pool = ctx.enter_context(tc.tile_pool(name="widened_pool", bufs=6))
         woven_pool = ctx.enter_context(tc.tile_pool(name="woven_pool", bufs=3))
-        narrow_pool = ctx.enter_context(tc.tile_pool(name="narrow_pool", bufs=2))
-        result_pool = ctx.enter_context(tc.tile_pool(name="result_pool", bufs=8))
-        banks = ctx.enter_context(tc.psum_pool(name="banks", bufs=8))
+        result_pool = ctx.enter_context(tc.tile_pool(name="result_pool", bufs=6))
+        psum = ctx.enter_context(tc.psum_pool(name="psum", bufs=1))
+        ctx.enter_context(tc.manual_schedule(engines={ENGINE.PE, ENGINE.Activation, ENGINE.DVE, ENGINE.SP}))
 
-        scale_cols = keep.tile([P, HALVES, PACK], F32, name="scale_cols")
-        nc.scalar.dma_start(out=scale_cols[:], in_=x_scale.rearrange("o (j p c) -> p (o j) c", p=P, c=PACK))
+        taken = []
 
-        x_cases = x_bytes.rearrange("(g m c) k -> g m c k", m=P, c=PACK)
-        x_raw = []
-        for g in range(GROUPS):
-            x_raw.append(keep.tile([P, PACK, D], U8, name="x_raw%d" % g))
-
-        def load_x(g, lo, hi):
-            nc.sync.dma_start(out=x_raw[g][:, lo:hi, :], in_=x_cases[g][:, lo:hi, :])
+        def next_bank(shape):
+            taken.append(len(taken) % BANKS)
+            return psum.tile(shape, F32, name="bank%d" % taken[-1])
 
         w_scales = keep.tile([P, D + K], U8, name="w_scales", align_bytes=64)
         nc.vector.memset(w_scales[:].bitcast(I32), 0)
+
+        zeros = keep.tile([P, P], BF16, name="zeros")
+        nc.gpsimd.memset(zeros[:], 0.0)
+        ident = keep.tile([P, P], F32, name="ident")
+        make_identity(nc, ident[:])
 
         def load_scales(scales, width, col):
             rows_in = scales.bitcast(I32)
@@ -66,45 +66,50 @@ def tile_factoranalysisemloadinggradient_w8_kernel(
                     in_=rows_in[:, 4 * q : 4 * q + 4, :],
                 )
 
-        zeros = keep.tile([P, K], BF16, name="zeros")
-        nc.gpsimd.memset(zeros[:], 0.0)
-        ident = keep.tile([P, P], F32, name="ident")
-        make_identity(nc, ident[:])
+        x_cases = x_bytes.rearrange("(g m c) k -> g m c k", m=P, c=PACK)
+        x_raw = {}
 
+        def load_x(first, count):
+            g, c = divmod(first, PACK)
+            raw = keep.tile([P, count, D], U8, name="x_raw%d" % first)
+            nc.sync.dma_start(out=raw[:], in_=x_cases[g][:, c : c + count, :])
+            for n in range(count):
+                x_raw[first + n] = raw[:, n, :]
+
+        scale_cols = keep.tile([P, HALVES, PACK], F32, name="scale_cols")
         beta_codes = keep.tile([P, HALVES, K * PACK], U8, name="beta_codes", align_bytes=64)
         p_codes = []
         for h in range(2):
             p_codes.append(keep.tile([P, HALVES, HALF * PACK], U8, name="p_codes%d" % h, align_bytes=64))
         p_rows = p_words.rearrange("g p n c -> p g (n c)")
-        x_scale_row = x_scale.rearrange("o k -> (o k)")
-        x_scales = keep.tile([P, D], F32, name="x_scales")
-        rt_in = keep.tile([P, 2, GROUPS, PACK], BF16, name="rt_in")
+        rt_rows = keep.tile([P, P * PACK], BF16, name="rt_rows")
+        nc.vector.memset(rt_rows[:], 0.0)
         psi_in = keep.tile([P, OUT_TILES, 2], BF16, name="psi_in")
         v_in = keep.tile([P, OUT_TILES, K], BF16, name="v_in")
 
-        load_x(0, 0, 1)
-        load_x(0, 1, PACK)
+        nc.scalar.dma_start(out=scale_cols[:], in_=x_scale.rearrange("o (j p c) -> p (o j) c", p=P, c=PACK))
+        load_x(0, 1)
+        load_x(1, 1)
         load_scales(beta_scales, K, D)
+        load_x(2, 2)
         nc.sync.dma_start(out=beta_codes[:], in_=beta_words.rearrange("g p n c -> p g (n c)"))
-        nc.sync.dma_start(out=p_codes[0][:], in_=p_rows[:, :, 0 : HALF * PACK])
-        with nc.allow_non_contiguous_dma(reason="vectors of one value a case or a row, laid on the partitions"):
-            nc.sync.dma_start(out=rt_in[:, T, :, :], in_=t.rearrange("(g m c) -> m g c", m=P, c=PACK))
-            nc.sync.dma_start(out=rt_in[:, R, :, :], in_=r.rearrange("(g m c) -> m g c", m=P, c=PACK))
+        nc.sync.dma_start(out=rt_rows[T * GROUPS : (T + 1) * GROUPS, :], in_=t.rearrange("(g n) -> g n", g=GROUPS))
+        nc.sync.dma_start(out=rt_rows[R * GROUPS : (R + 1) * GROUPS, :], in_=r.rearrange("(g n) -> g n", g=GROUPS))
         load_scales(p_scales, D, 0)
-        load_x(1, 0, 2)
-        load_x(1, 2, PACK)
-        nc.sync.dma_start(out=x_scales[:], in_=x_scale_row.partition_broadcast(P))
+        nc.sync.dma_start(out=p_codes[0][:], in_=p_rows[:, :, 0 : HALF * PACK])
+        load_x(4, 2)
+        load_x(6, 2)
+        load_x(8, 4)
+        load_x(12, 4)
         nc.sync.dma_start(out=p_codes[1][:], in_=p_rows[:, :, HALF * PACK : D * PACK])
-        load_x(2, 0, PACK)
-        load_x(3, 0, PACK)
         with nc.allow_non_contiguous_dma(reason="vectors of one value a case or a row, laid on the partitions"):
             nc.sync.dma_start(out=psi_in[:, :, 0:1], in_=psi.rearrange("(m p o) -> p m o", p=P, o=1))
         nc.sync.dma_start(out=v_in[:], in_=v.rearrange("(m p) k -> p m k", p=P))
 
+        x_scales = keep.tile([P, D], F32, name="x_scales")
         rt = keep.tile([P, 2, TILES], F32, name="rt")
         inv_psi = keep.tile([P, OUT_TILES], F32, name="inv_psi")
         gain = keep.tile([P, OUT_TILES], F32, name="gain")
-        v_scaled = keep.tile([P, 2, K], F32, name="v_scaled")
 
         x_codes, x_code_scales, z_codes, z_code_scales, e_codes, e_code_scales = [], [], [], [], [], []
         for s in range(STEPS):
@@ -113,51 +118,84 @@ def tile_factoranalysisemloadinggradient_w8_kernel(
         for g in range(GROUPS):
             z_codes.append(keep.tile([P, K], U32, name="z_codes%d" % g, align_bytes=64))
             z_code_scales.append(keep.tile([P, K], U8, name="z_code_scales%d" % g, align_bytes=64))
-            e_codes.append(keep.tile([P, D], U32, name="e_codes%d" % g, align_bytes=64))
-            e_code_scales.append(keep.tile([P, D], U8, name="e_code_scales%d" % g, align_bytes=64))
+        for m in range(OUT_TILES):
+            e_codes.append(keep.tile([P, GROUPS * P], U32, name="e_codes%d" % m, align_bytes=64))
+            e_code_scales.append(keep.tile([P, GROUPS * P], U8, name="e_code_scales%d" % m, align_bytes=64))
 
-        widened, transposed, woven_x = {}, {}, {}
-        idle_bank = banks.tile([P, K], F32, name="bank")
+        idle_bank = next_bank([P, K])
 
         def keep_busy(count):
             for n in range(count):
-                nc.tensor.matmul(out=idle_bank[:], lhsT=zeros[:, 0:P], rhs=zeros[:], start=True, stop=True)
+                nc.tensor.matmul(
+                    out=idle_bank[:].rearrange("p (a n) -> p a n", n=P),
+                    lhsT=zeros[:],
+                    rhs=zeros[:].unsqueeze(1).to_broadcast([P, K // P, P]),
+                    start=True,
+                    stop=True,
+                )
 
-        def widen(i, copy):
-            g, c = divmod(i, PACK)
-            widened[i] = widened_pool.tile([P, D], BF16, name="widened")
-            for j in range(HALVES):
-                cols = slice(j * HALF, (j + 1) * HALF)
-                copy(out=widened[i][:, cols], in_=x_raw[g][:, c, cols].bitcast(FP8))
+        spread = {}
 
-        def widen_and_scale(i):
-            g, c = divmod(i, PACK)
-            widened[i] = widened_pool.tile([P, D], BF16, name="widened")
-            nc.vector.tensor_tensor(
-                out=widened[i][:], in0=x_raw[g][:, c, :].bitcast(FP8), in1=x_scales[:], op=MULT
+        def spread_scales(j):
+            spread[j] = next_bank([P, PACK, P])
+            for c in range(PACK):
+                nc.tensor.transpose(spread[j][:, c, :], scale_cols[:, j, c : c + 1].to_broadcast([P, P]), ident[:])
+
+        def copy_scales(j):
+            nc.scalar.activation(
+                out=x_scales[:, j * HALF : (j + 1) * HALF].rearrange("p (q c) -> p q c", c=PACK),
+                in_=spread[j][:].rearrange("p c q -> p q c"),
+                func=COPY,
             )
 
-        def transpose(i):
+        def turn_rt():
+            spread["rt"] = next_bank([P, 2, P])
+            for u in range(2):
+                nc.tensor.transpose(spread["rt"][:, u, :], rt_rows[:].bitcast(F32)[:, u : 2 * P : 2], ident[:])
+
+        def copy_rt():
+            nc.scalar.copy(
+                out=rt[:].rearrange("p w (g u e) -> p u (w g) e", u=2, e=2),
+                in_=spread["rt"][:, :, 0 : 2 * GROUPS].bitcast(BF16).rearrange("p u (k e) -> p u k e", e=2),
+            )
+
+        widened, transposed, woven_x = {}, {}, {}
+
+        def widen(i, copy, halves=range(HALVES)):
+            if i not in widened:
+                widened[i] = widened_pool.tile([P, D], BF16, name="widened")
+            for j in halves:
+                cols = slice(j * HALF, (j + 1) * HALF)
+                copy(out=widened[i][:, cols], in_=x_raw[i][:, cols].bitcast(FP8))
+
+        def widen_and_scale(i, lo=0, hi=D):
+            if i not in widened:
+                widened[i] = widened_pool.tile([P, D], BF16, name="widened")
+            nc.vector.tensor_tensor(
+                out=widened[i][:, lo:hi], in0=x_raw[i][:, lo:hi].bitcast(FP8), in1=x_scales[:, lo:hi], op=MULT
+            )
+
+        def transpose(i, halves=range(HALVES)):
             words = widened[i][:].bitcast(F32)
-            bank = banks.tile([P, HALVES, 2, P], F32, name="bank")
-            transposed[i] = bank
-            for j in range(HALVES):
+            bank = next_bank([P, HALVES, 2, P])
+            for j in halves:
+                transposed[i, j] = bank
                 for u in range(2):
                     nc.tensor.transpose(bank[:, j, u, :], words[:, 256 * j + u : 256 * (j + 1) : 2], ident[:])
 
         def woven_tile(i):
             s, h = divmod(i, 2)
-            if h == 0:
+            if s not in woven_x:
                 woven_x[s] = woven_pool.tile([P, 2, HALVES * P * PACK], BF16, name="woven_x", align_bytes=64)
             return woven_x[s][:, h, :]
 
-        def scale_out(i):
+        def scale_out(i, halves=range(HALVES)):
             woven = woven_tile(i)
-            for j in range(HALVES):
+            for j in halves:
                 scales = scale_cols[:, j, :].rearrange("p (u e) -> p u e", e=2)
                 nc.vector.tensor_tensor(
                     out=woven[:, j * P * PACK : (j + 1) * P * PACK].rearrange("p (m u e) -> p m u e", u=2, e=2),
-                    in0=transposed[i][:, j, :, :].bitcast(BF16).rearrange("p u (m e) -> p m u e", e=2),
+                    in0=transposed[i, j][:, j, :, :].bitcast(BF16).rearrange("p u (m e) -> p m u e", e=2),
                     in1=scales.unsqueeze(1).to_broadcast([P, P, 2, 2]),
                     op=MULT,
                 )
@@ -165,13 +203,15 @@ def tile_factoranalysisemloadinggradient_w8_kernel(
         def copy_out(i):
             nc.scalar.copy(
                 out=woven_tile(i).bitcast(F32).rearrange("p (j m u) -> p j m u", j=HALVES, u=2),
-                in_=transposed[i][:].rearrange("p j u m -> p j m u"),
+                in_=transposed[i, 0][:].rearrange("p j u m -> p j m u"),
             )
 
-        def quantize_x(i):
+        def quantize_x(i, lo=0, hi=HALVES):
             s, h = divmod(i, 2)
             nc.vector.quantize_mx(
-                out=x_codes[s][:, h, :].bitcast(X4), scales=x_code_scales[s][:, h, :], in_=woven_x[s][:, h, :]
+                out=x_codes[s][:, h, lo * P : hi * P].bitcast(X4),
+                scales=x_code_scales[s][:, h, lo * P : hi * P],
+                in_=woven_x[s][:, h, lo * P * PACK : hi * P * PACK],
             )
 
         def quantize_x_pair(s):
@@ -195,239 +235,244 @@ def tile_factoranalysisemloadinggradient_w8_kernel(
                     stop=(j == HALVES - 1),
                 )
 
-        products, planes, woven = {}, {}, {}
+        products, woven_z, woven_e = {}, {}, {}
+        z_planes = []
+        for g in range(GROUPS):
+            z_planes.append(keep.tile([P, PACK, K], BF16, name="z_planes%d" % g))
+        e_planes = keep.tile([P, GROUPS, PACK, HALF], BF16, name="e_planes")
 
         def multiply_wide(kind, i):
-            bank = banks.tile([P, K], F32, name="bank")
-            products[kind, i] = bank
+            products[kind, i] = next_bank([P, K])
             if kind == "z":
-                multiply(bank[:], i, beta_codes, 0, D, K)
+                multiply(products[kind, i][:], i, beta_codes, 0, D, K)
             else:
-                multiply(bank[:], i, p_codes[0], 0, 0, HALF)
+                multiply(products[kind, i][:], i, p_codes[0], 0, 0, HALF)
 
         def scale_wide(kind, i):
             g, c = divmod(i, PACK)
-            if c == 0:
-                planes[kind, g] = keep.tile([P, PACK, K], BF16, name="%s_planes%d" % (kind, g))
-                woven[kind, g] = keep.tile([P, K, PACK], BF16, name="%s_woven%d" % (kind, g), align_bytes=64)
-            factor = T if kind == "z" else R
-            nc.scalar.activation(
-                out=planes[kind, g][:, c, :], in_=products[kind, i][:], func=COPY, scale=rt[:, factor, i : i + 1]
-            )
+            plane, factor = (z_planes[g][:, c, :], T) if kind == "z" else (e_planes[:, g, c, :], R)
+            nc.scalar.activation(out=plane, in_=products[kind, i][:], func=COPY, scale=rt[:, factor, i : i + 1])
 
-        def weave(kind, g, lo, hi, copy):
+        def wide(i):
+            for kind in ("z", "e"):
+                multiply_wide(kind, i)
+                scale_wide(kind, i)
+
+        def weave_z(g, lo, hi, copy):
+            if g not in woven_z:
+                woven_z[g] = woven_pool.tile([P, K, PACK], BF16, name="woven_z", bufs=3, align_bytes=64)
             copy(
-                out=woven[kind, g][:, lo:hi, :].rearrange("p (b n) c -> p b c n", n=4),
-                in_=planes[kind, g][:, :, lo:hi].rearrange("p c (b n) -> p b c n", n=4),
+                out=woven_z[g][:, lo:hi, :].rearrange("p (b n) c -> p b c n", n=4),
+                in_=z_planes[g][:, :, lo:hi].rearrange("p c (b n) -> p b c n", n=4),
             )
 
-        def quantize_wide(kind, g):
-            codes, scales = (z_codes, z_code_scales) if kind == "z" else (e_codes, e_code_scales)
+        def quantize_z(g):
             nc.vector.quantize_mx(
-                out=codes[g][:, 0:K].bitcast(X4),
-                scales=scales[g][:, 0:K],
-                in_=woven[kind, g][:].rearrange("p n c -> p (n c)"),
+                out=z_codes[g][:].bitcast(X4), scales=z_code_scales[g][:], in_=woven_z[g][:].rearrange("p n c -> p (n c)")
             )
 
-        narrow = {}
+        def woven_chunk(m):
+            if m not in woven_e:
+                woven_e[m] = woven_pool.tile([P, GROUPS, P, PACK], BF16, name="woven_e", bufs=4, align_bytes=64)
+            return woven_e[m]
 
-        def multiply_narrow(g, chunk):
-            bank = banks.tile([P, PACK, P], F32, name="bank")
-            products[g, chunk] = bank
+        def weave_e(m):
+            nc.scalar.copy(
+                out=woven_chunk(m)[:].rearrange("p g (b n) c -> p g b c n", n=4),
+                in_=e_planes[:, :, :, P * m : P * (m + 1)].rearrange("p g c (b n) -> p g b c n", n=4),
+            )
+
+        def multiply_narrow(m, g):
+            products[m, g] = next_bank([P, PACK, P])
             for c in range(PACK):
-                multiply(bank[:, c, :], g * PACK + c, p_codes[1], P * chunk, HALF + P * chunk, P)
+                multiply(products[m, g][:, c, :], g * PACK + c, p_codes[1], P * m - HALF, P * m, P)
 
-        def scale_narrow(g, chunk):
-            if chunk == 0:
-                narrow[g] = narrow_pool.tile([P, CHUNKS, P, PACK], BF16, name="narrow", align_bytes=64)
+        def scale_narrow(m, g):
             factors = rt[:, R, g * PACK : (g + 1) * PACK]
             nc.vector.tensor_tensor(
-                out=narrow[g][:, chunk, :, :],
-                in0=products[g, chunk][:].rearrange("p c n -> p n c"),
+                out=woven_chunk(m)[:, g, :, :],
+                in0=products[m, g][:].rearrange("p c n -> p n c"),
                 in1=factors.unsqueeze(1).to_broadcast([P, P, PACK]),
                 op=MULT,
             )
 
-        def quantize_narrow(g, lo, hi):
-            cols = slice(HALF + P * lo, HALF + P * hi)
+        def quantize_e(m):
             nc.vector.quantize_mx(
-                out=e_codes[g][:, cols].bitcast(X4),
-                scales=e_code_scales[g][:, cols],
-                in_=narrow[g][:, lo:hi, :, :].rearrange("p b n c -> p (b n c)"),
+                out=e_codes[m][:].bitcast(X4),
+                scales=e_code_scales[m][:],
+                in_=woven_e[m][:].rearrange("p g n c -> p (g n c)"),
             )
 
-        sums = {}
+        sums, v_scaled = {}, {}
 
-        def contract(m, groups, lo=0, hi=K):
-            if (m, lo) not in sums:
-                bank = banks.tile([P, K], F32, name="bank")
-                sums[m, lo] = bank
-            cols = slice(P * m, P * (m + 1))
-            for g in groups:
+        def contract(m, lo=0, hi=K):
+            sums[m, lo] = next_bank([P, K])
+            for g in range(GROUPS):
+                cols = slice(P * g, P * (g + 1))
                 nc.tensor.matmul_mx(
                     out=sums[m, lo][:, 0 : hi - lo],
-                    lhsT=e_codes[g][:, cols].bitcast(X4),
-                    lhsT_scale=e_code_scales[g][:, cols],
+                    lhsT=e_codes[m][:, cols].bitcast(X4),
+                    lhsT_scale=e_code_scales[m][:, cols],
                     rhs=z_codes[g][:, lo:hi].bitcast(X4),
                     rhs_scale=z_code_scales[g][:, lo:hi],
                     start=(g == 0),
                     stop=(g == GROUPS - 1),
                 )
 
-        def finish(m):
-            difference = woven_pool.tile([P, K], F32, name="difference")
-            nc.vector.scalar_tensor_tensor(
-                out=difference[:], in0=sums[m, 0][:], scalar=1.0 / N, in1=v_in[:, m, :], op0=MULT, op1=SUBTRACT
-            )
-            result = result_pool.tile([P, K], F32, name="result")
-            nc.scalar.activation(out=result[:], in_=difference[:], func=COPY, scale=inv_psi[:, m : m + 1])
-            nc.sync.dma_start(out=out[P * m : P * (m + 1), :], in_=result[:])
-
         def scale_v(m):
-            nc.scalar.activation(
-                out=v_scaled[:, m - 2, :], in_=v_in[:, m, :], func=COPY, scale=inv_psi[:, m : m + 1]
-            )
+            v_scaled[m] = result_pool.tile([P, K], F32, name="v_scaled")
+            nc.scalar.activation(out=v_scaled[m][:], in_=v_in[:, m, :], func=COPY, scale=inv_psi[:, m : m + 1])
 
-        def finish_last(m, lo=0, hi=K):
+        def finish(m, lo=0, hi=K):
             result = result_pool.tile([P, K], F32, name="result")
             nc.vector.scalar_tensor_tensor(
                 out=result[:, lo:hi],
                 in0=sums[m, lo][:, 0 : hi - lo],
                 scalar=gain[:, m : m + 1],
-                in1=v_scaled[:, m - 2, lo:hi],
+                in1=v_scaled[m][:, lo:hi],
                 op0=MULT,
                 op1=SUBTRACT,
             )
             nc.sync.dma_start(out=out[P * m : P * (m + 1), lo:hi], in_=result[:, lo:hi])
 
         vector, scalar = nc.vector.tensor_copy, nc.scalar.copy
-        every = range(GROUPS)
-        last = GROUPS - 1
-        ctx.enter_context(tc.manual_schedule(engines={ENGINE.PE, ENGINE.Activation, ENGINE.DVE}))
 
-        keep_busy(5)
+        keep_busy(4)
+        spread_scales(0)
         widen(0, vector)
-        widen(1, scalar)
-        transpose(0)
-        keep_busy(1)
+        widen(1, vector)
+        copy_scales(0)
+        transpose(0, (0,))
+        transpose(0, (1,))
         transpose(1)
-        scale_out(0)
-        quantize_x(0)
         widen(2, scalar)
-        multiply_wide("z", 0)
+        widen(3, scalar)
+        keep_busy(2)
+        spread_scales(1)
+        scale_out(0)
+        quantize_x(0, 0, 1)
+        quantize_x(0, 1, 2)
         transpose(2)
         scale_out(1)
+        multiply_wide("z", 0)
+        turn_rt()
+        transpose(3)
+        copy_rt()
+        copy_scales(1)
+        scale_out(2, (0,))
         quantize_x(1)
-        nc.vector.tensor_copy(
-            out=rt[:].rearrange("p w i -> p (w i)"), in_=rt_in[:].rearrange("p w g c -> p (w g c)")
-        )
-        widen(3, scalar)
-        scale_out(2)
+        scale_out(2, (1,))
         scale_wide("z", 0)
         multiply_wide("z", 1)
-        transpose(3)
-        widen(4, scalar)
-        scale_out(3)
+        multiply_wide("e", 0)
+        multiply_wide("e", 1)
         scale_wide("z", 1)
-        widen(5, scalar)
-        quantize_x_pair(1)
-        for i in (0, 1):
-            multiply_wide("e", i)
-            scale_wide("e", i)
-
-        for s in range(1, STEPS):
-            g, h = divmod(s, 2)
-            a = 2 * s
-            if s == 1:
-                for i in range(6, LATE_TILES):
-                    widen(i, scalar)
-            ahead = (0, 2, 2, 4, 0, 4, 0, 0)[s]
-            for i in range(a + 2, a + 2 + ahead):
+        scale_wide("e", 0)
+        scale_wide("e", 1)
+        scale_out(3, (0,))
+        quantize_x(2)
+        scale_out(3, (1,))
+        widen_and_scale(4)
+        quantize_x(3)
+        widen_and_scale(5)
+        wide(2)
+        transpose(4)
+        copy_out(4)
+        wide(3)
+        transpose(5)
+        copy_out(5)
+        widen_and_scale(6, 0, HALF)
+        quantize_x(4)
+        widen_and_scale(6, HALF, D)
+        widen_and_scale(7)
+        wide(4)
+        for a in range(6, TILES, 2):
+            for i in (a, a + 1):
                 transpose(i)
-            for i in range(a + 2, a + 2 + ahead):
-                if i < LATE_TILES:
-                    scale_out(i)
-                else:
-                    copy_out(i)
-            if s == 1:
-                quantize_x_pair(2)
-            for i in range(a + 6, min(a + 8, TILES)):
-                widen_and_scale(i)
-            for kind in ("z", "e"):
-                if s == STEPS - 1 and kind == "e":
-                    multiply_narrow(g - 1, 2)
-                    multiply_narrow(g - 1, 3)
-                for i in (a, a + 1):
-                    multiply_wide(kind, i)
-                for i in (a, a + 1):
-                    scale_wide(kind, i)
-                if s == STEPS - 1 and kind == "z":
-                    weave("z", last, 256, 512, scalar)
-            if s == 6:
-                weave("z", 2, 0, 512, scalar)
-            elif 2 <= s <= 5:
-                weave("z", g - 1, 256 * h, 256 * h + 256, scalar)
-            if s == 4:
-                weave("e", 0, 0, 512, vector)
-            if s == 5:
-                quantize_wide("e", 0)
-            if s == 6:
-                weave("e", 1, 0, 512, vector)
-            if 1 < s < STEPS - 1:
-                quantize_x_pair(s + 1)
-            if s == STEPS - 1:
-                quantize_wide("e", 1)
-            if g > 0:
-                if s < STEPS - 1:
-                    multiply_narrow(g - 1, 2 * h)
-                    multiply_narrow(g - 1, 2 * h + 1)
-                if h == 0 and g > 1:
-                    quantize_wide("z", g - 2)
-                    quantize_narrow(g - 2, 0, CHUNKS)
-                scale_narrow(g - 1, 2 * h)
-                scale_narrow(g - 1, 2 * h + 1)
-            if s == 4:
-                nc.vector.reciprocal(out=inv_psi[:], in_=psi_in[:, :, 0])
-            if s == 5:
-                nc.vector.tensor_scalar(out=gain[:], in0=inv_psi[:], scalar1=1.0 / N, scalar2=None, op0=MULT)
+            for i in (a, a + 1):
+                copy_out(i)
+            quantize_x(a - 1)
+            if a + 2 < TILES:
+                widen_and_scale(a + 2)
+            else:
+                weave_z(1, 0, K, vector)
+            quantize_x(a)
+            if a + 2 < TILES:
+                widen_and_scale(a + 3)
+            if a == 8:
+                weave_z(0, 0, K // 2, vector)
+            if a == 10:
+                weave_z(0, K // 2, K, vector)
+            if a == 12:
+                quantize_z(0)
+            if a == 14:
+                quantize_x(15)
+                weave_z(2, 0, K, vector)
+                quantize_z(1)
+            wide(a - 1)
+            wide(a)
 
-        contract(4, (0, 1))
-        for chunk in range(CHUNKS):
-            multiply_narrow(last, chunk)
-        weave("e", 2, 0, 512, scalar)
-        weave("z", last, 0, 256, vector)
-        quantize_wide("z", last - 1)
-        quantize_narrow(last - 1, 0, CHUNKS)
-        scale_narrow(last, 0)
-        quantize_wide("z", last)
-        weave("e", last, 0, 256, scalar)
-        scale_narrow(last, 1)
-        scale_narrow(last, 2)
-        quantize_narrow(last, 0, 2)
-        scale_narrow(last, 3)
-        quantize_wide("e", 2)
-        quantize_narrow(last, 2, 4)
-        contract(4, (2,))
-        contract(5, (0, 1, 2))
-        contract(6, (0, 1, 2))
-        for m in (4, 5, 6):
-            contract(m, (last,))
-        scale_v(2)
-        scale_v(3)
+        multiply_wide("z", 15)
+        scale_wide("z", 15)
+        nc.vector.reciprocal(out=inv_psi[:], in_=psi_in[:, :, 0])
+        weave_z(3, 0, K, scalar)
+        for g in range(GROUPS):
+            multiply_narrow(4, g)
+        multiply_wide("e", 15)
+        quantize_z(2)
+        scale_narrow(4, 0)
+        nc.vector.tensor_scalar(out=gain[:], in0=inv_psi[:], scalar1=1.0 / N, scalar2=None, op0=MULT)
+        scale_wide("e", 15)
+        scale_v(4)
+        weave_e(0)
+        for g in range(1, GROUPS):
+            scale_narrow(4, g)
+        for g in range(GROUPS):
+            multiply_narrow(5, g)
+        quantize_z(3)
+        quantize_e(4)
+        for g in range(GROUPS):
+            scale_narrow(5, g)
+        contract(4)
+        quantize_e(0)
+        scale_v(0)
+        scale_v(5)
+        weave_e(1)
+        for g in range(GROUPS):
+            multiply_narrow(6, g)
+        quantize_e(5)
         finish(4)
-        finish(5)
-        weave("e", last, 256, 512, vector)
-        quantize_wide("e", last)
-        contract(7, every)
-        finish(6)
-        contract(0, every)
-        finish(7)
-        contract(1, every)
+        for g in range(GROUPS):
+            scale_narrow(6, g)
+        contract(0)
+        contract(5)
+        quantize_e(1)
+        weave_e(2)
+        scale_v(1)
         finish(0)
-        contract(2, every)
+        quantize_e(6)
+        for g in range(GROUPS):
+            multiply_narrow(7, g)
+        scale_v(6)
+        quantize_e(2)
+        contract(1)
+        for g in range(GROUPS):
+            scale_narrow(7, g)
+        contract(6)
+        weave_e(3)
+        scale_v(2)
+        finish(5)
+        quantize_e(7)
+        contract(2)
         finish(1)
-        contract(3, every, 0, 256)
-        finish_last(2)
-        contract(3, every, 256, 512)
-        finish_last(3, 0, 256)
-        finish_last(3, 256, 512)
+        quantize_e(3)
+        finish(6)
+        scale_v(7)
+        scale_v(3)
+        contract(7)
+        finish(2)
+        contract(3, 0, 256)
+        finish(7)
+        contract(3, 256, 512)
+        finish(3, 0, 256)
+        finish(3, 256, 512)

@@ -15,6 +15,7 @@ FP8 = mybir.dt.float8_e4m3fn
 X4 = mybir.dt.float8_e4m3fn_x4
 MULT = mybir.AluOpType.mult
 SUBTRACT = mybir.AluOpType.subtract
+ADD = mybir.AluOpType.add
 COPY = mybir.ActivationFunctionType.Copy
 ENGINE = mybir.EngineType
 
@@ -40,7 +41,7 @@ def tile_factoranalysisemloadinggradient_w8_kernel(
         keep = ctx.enter_context(tc.tile_pool(name="keep", bufs=1))
         widened_pool = ctx.enter_context(tc.tile_pool(name="widened_pool", bufs=6))
         woven_pool = ctx.enter_context(tc.tile_pool(name="woven_pool", bufs=3))
-        result_pool = ctx.enter_context(tc.tile_pool(name="result_pool", bufs=6))
+        result_pool = ctx.enter_context(tc.tile_pool(name="result_pool", bufs=8))
         psum = ctx.enter_context(tc.psum_pool(name="psum", bufs=1))
         ctx.enter_context(tc.manual_schedule(engines={ENGINE.PE, ENGINE.Activation, ENGINE.DVE, ENGINE.SP}))
 
@@ -273,8 +274,19 @@ def tile_factoranalysisemloadinggradient_w8_kernel(
 
         def woven_chunk(m):
             if m not in woven_e:
-                woven_e[m] = woven_pool.tile([P, GROUPS, P, PACK], BF16, name="woven_e", bufs=4, align_bytes=64)
+                name = "woven_e%d" % {4: 0, 0: 0, 1: 0, 5: 1, 7: 1, 6: 2, 3: 4, 2: 3}[m]
+                woven_e[m] = keep.tile([P, GROUPS, P, PACK], BF16, name=name, align_bytes=64)
             return woven_e[m]
+
+        def weave_e_gpsimd(m):
+            nc.gpsimd.tensor_scalar(
+                out=woven_chunk(m)[:],
+                in0=e_planes[:, :, :, P * m : P * (m + 1)].rearrange("p g c n -> p g n c"),
+                scalar1=1.0,
+                scalar2=0.0,
+                op0=MULT,
+                op1=ADD,
+            )
 
         def weave_e(m):
             nc.scalar.copy(
@@ -294,6 +306,21 @@ def tile_factoranalysisemloadinggradient_w8_kernel(
                 in0=products[m, g][:].rearrange("p c n -> p n c"),
                 in1=factors.unsqueeze(1).to_broadcast([P, P, PACK]),
                 op=MULT,
+            )
+
+        last_planes = keep.tile([P, GROUPS, PACK, P], BF16, name="last_planes")
+
+        def scale_last(g):
+            for c in range(PACK):
+                i = g * PACK + c
+                nc.scalar.activation(
+                    out=last_planes[:, g, c, :], in_=products[7, g][:, c, :], func=COPY, scale=rt[:, R, i : i + 1]
+                )
+
+        def weave_last():
+            nc.scalar.copy(
+                out=woven_chunk(7)[:].rearrange("p g (b n) c -> p g b c n", n=4),
+                in_=last_planes[:].rearrange("p g c (b n) -> p g b c n", n=4),
             )
 
         def quantize_e(m):
@@ -424,55 +451,64 @@ def tile_factoranalysisemloadinggradient_w8_kernel(
         nc.vector.tensor_scalar(out=gain[:], in0=inv_psi[:], scalar1=1.0 / N, scalar2=None, op0=MULT)
         scale_wide("e", 15)
         scale_v(4)
-        weave_e(0)
+        scale_v(5)
         for g in range(1, GROUPS):
             scale_narrow(4, g)
         for g in range(GROUPS):
             multiply_narrow(5, g)
         quantize_z(3)
         quantize_e(4)
+        weave_e_gpsimd(0)
         for g in range(GROUPS):
             scale_narrow(5, g)
+        multiply_narrow(7, 0)
+        multiply_narrow(6, 0)
+        multiply_narrow(7, 1)
         contract(4)
-        quantize_e(0)
-        scale_v(0)
-        scale_v(5)
-        weave_e(1)
-        for g in range(GROUPS):
-            multiply_narrow(6, g)
-        quantize_e(5)
-        finish(4)
-        for g in range(GROUPS):
-            scale_narrow(6, g)
-        contract(0)
-        contract(5)
-        quantize_e(1)
+        multiply_narrow(6, 1)
+        multiply_narrow(6, 2)
         weave_e(2)
-        scale_v(1)
-        finish(0)
-        quantize_e(6)
-        for g in range(GROUPS):
-            multiply_narrow(7, g)
-        scale_v(6)
-        quantize_e(2)
-        contract(1)
-        for g in range(GROUPS):
-            scale_narrow(7, g)
-        contract(6)
+        scale_last(0)
+        scale_last(1)
         weave_e(3)
-        scale_v(2)
-        finish(5)
-        quantize_e(7)
+        scale_narrow(6, 0)
+        quantize_e(5)
+        quantize_e(2)
+        quantize_e(0)
+        weave_e_gpsimd(1)
+        multiply_narrow(6, 3)
+        multiply_narrow(7, 2)
+        multiply_narrow(7, 3)
+        contract(5)
+        contract(0)
         contract(2)
-        finish(1)
+        scale_last(2)
+        scale_last(3)
+        scale_v(0)
+        weave_last()
+        finish(4)
+        scale_narrow(6, 1)
+        scale_narrow(6, 2)
+        scale_narrow(6, 3)
+        finish(5)
         quantize_e(3)
-        finish(6)
-        scale_v(7)
+        quantize_e(6)
+        quantize_e(1)
+        scale_v(2)
         scale_v(3)
-        contract(7)
+        scale_v(6)
+        scale_v(1)
+        scale_v(7)
+        finish(0)
+        contract(3)
+        quantize_e(7)
         finish(2)
-        contract(3, 0, 256)
-        finish(7)
-        contract(3, 256, 512)
-        finish(3, 0, 256)
-        finish(3, 256, 512)
+        contract(6)
+        finish(3)
+        contract(1)
+        finish(6)
+        contract(7, 0, 256)
+        finish(1)
+        contract(7, 256, 512)
+        finish(7, 0, 256)
+        finish(7, 256, 512)

@@ -29,7 +29,7 @@ HALF = D // 2
 OUT_TILES = D // P
 BANKS = 8
 
-LATE_TILES = 4
+WIDE = K + D
 R, T = 0, 1
 
 
@@ -39,7 +39,7 @@ def tile_factoranalysisemloadinggradient_w8_kernel(
     nc = tc.nc
     with ExitStack() as ctx:
         keep = ctx.enter_context(tc.tile_pool(name="keep", bufs=1))
-        widened_pool = ctx.enter_context(tc.tile_pool(name="widened_pool", bufs=6))
+        widened_pool = ctx.enter_context(tc.tile_pool(name="widened_pool", bufs=4))
         woven_pool = ctx.enter_context(tc.tile_pool(name="woven_pool", bufs=3))
         result_pool = ctx.enter_context(tc.tile_pool(name="result_pool", bufs=8))
         psum = ctx.enter_context(tc.psum_pool(name="psum", bufs=1))
@@ -59,16 +59,16 @@ def tile_factoranalysisemloadinggradient_w8_kernel(
         ident = keep.tile([P, P], F32, name="ident")
         make_identity(nc, ident[:])
 
-        def load_scales(scales, width, col):
+        def load_scales(scales, width, col, quadrants):
             rows_in = scales.bitcast(I32)
-            for q in range(4):
+            for q in quadrants:
                 nc.sync.dma_start(
                     out=w_scales[32 * q : 32 * q + 4 * HALVES, col : col + width].bitcast(I32),
                     in_=rows_in[:, 4 * q : 4 * q + 4, :],
                 )
 
         x_cases = x_bytes.rearrange("(g m c) k -> g m c k", m=P, c=PACK)
-        x_raw = {}
+        x_raw, x_rows = {}, {}
 
         def load_x(first, count):
             g, c = divmod(first, PACK)
@@ -76,6 +76,7 @@ def tile_factoranalysisemloadinggradient_w8_kernel(
             nc.sync.dma_start(out=raw[:], in_=x_cases[g][:, c : c + count, :])
             for n in range(count):
                 x_raw[first + n] = raw[:, n, :]
+                x_rows[first + n] = raw[:, n:count, :].rearrange("p c k -> p (c k)")
 
         scale_cols = keep.tile([P, HALVES, PACK], F32, name="scale_cols")
         beta_codes = keep.tile([P, HALVES, K * PACK], U8, name="beta_codes", align_bytes=64)
@@ -88,40 +89,38 @@ def tile_factoranalysisemloadinggradient_w8_kernel(
         psi_in = keep.tile([P, OUT_TILES, 2], BF16, name="psi_in")
         v_in = keep.tile([P, OUT_TILES, K], BF16, name="v_in")
 
+        nc.gpsimd.dma_start(out=rt_rows[T * GROUPS : (T + 1) * GROUPS, :], in_=t.rearrange("(g n) -> g n", g=GROUPS))
+        nc.gpsimd.dma_start(out=rt_rows[R * GROUPS : (R + 1) * GROUPS, :], in_=r.rearrange("(g n) -> g n", g=GROUPS))
         nc.scalar.dma_start(out=scale_cols[:], in_=x_scale.rearrange("o (j p c) -> p (o j) c", p=P, c=PACK))
         load_x(0, 1)
         load_x(1, 1)
-        load_scales(beta_scales, K, D)
         load_x(2, 2)
+        load_scales(beta_scales, K, D, range(4))
         nc.sync.dma_start(out=beta_codes[:], in_=beta_words.rearrange("g p n c -> p g (n c)"))
-        nc.sync.dma_start(out=rt_rows[T * GROUPS : (T + 1) * GROUPS, :], in_=t.rearrange("(g n) -> g n", g=GROUPS))
-        nc.sync.dma_start(out=rt_rows[R * GROUPS : (R + 1) * GROUPS, :], in_=r.rearrange("(g n) -> g n", g=GROUPS))
-        load_scales(p_scales, D, 0)
-        nc.sync.dma_start(out=p_codes[0][:], in_=p_rows[:, :, 0 : HALF * PACK])
         load_x(4, 2)
+        nc.sync.dma_start(out=p_codes[0][:], in_=p_rows[:, :, 0 : HALF * PACK])
+        load_scales(p_scales, D, 0, range(4))
         load_x(6, 2)
-        load_x(8, 4)
-        load_x(12, 4)
         nc.sync.dma_start(out=p_codes[1][:], in_=p_rows[:, :, HALF * PACK : D * PACK])
         with nc.allow_non_contiguous_dma(reason="vectors of one value a case or a row, laid on the partitions"):
             nc.sync.dma_start(out=psi_in[:, :, 0:1], in_=psi.rearrange("(m p o) -> p m o", p=P, o=1))
         nc.sync.dma_start(out=v_in[:], in_=v.rearrange("(m p) k -> p m k", p=P))
+        load_x(8, 4)
+        load_x(12, 4)
 
-        x_scales = keep.tile([P, D], F32, name="x_scales")
+        ones = keep.tile([P, 1], F32, name="ones")
+        nc.vector.memset(ones[:], 1.0)
         rt = keep.tile([P, 2, TILES], F32, name="rt")
         inv_psi = keep.tile([P, OUT_TILES], F32, name="inv_psi")
         gain = keep.tile([P, OUT_TILES], F32, name="gain")
 
-        x_codes, x_code_scales, z_codes, z_code_scales, e_codes, e_code_scales = [], [], [], [], [], []
+        x_codes, x_code_scales, codes, code_scales = [], [], [], []
         for s in range(STEPS):
             x_codes.append(keep.tile([P, 2, HALVES * P], U32, name="x_codes%d" % s, align_bytes=64))
             x_code_scales.append(keep.tile([P, 2, HALVES * P], U8, name="x_code_scales%d" % s, align_bytes=64))
         for g in range(GROUPS):
-            z_codes.append(keep.tile([P, K], U32, name="z_codes%d" % g, align_bytes=64))
-            z_code_scales.append(keep.tile([P, K], U8, name="z_code_scales%d" % g, align_bytes=64))
-        for m in range(OUT_TILES):
-            e_codes.append(keep.tile([P, GROUPS * P], U32, name="e_codes%d" % m, align_bytes=64))
-            e_code_scales.append(keep.tile([P, GROUPS * P], U8, name="e_code_scales%d" % m, align_bytes=64))
+            codes.append(keep.tile([P, WIDE], U32, name="codes%d" % g, align_bytes=64))
+            code_scales.append(keep.tile([P, WIDE], U8, name="code_scales%d" % g, align_bytes=64))
 
         idle_bank = next_bank([P, K])
 
@@ -137,18 +136,6 @@ def tile_factoranalysisemloadinggradient_w8_kernel(
 
         spread = {}
 
-        def spread_scales(j):
-            spread[j] = next_bank([P, PACK, P])
-            for c in range(PACK):
-                nc.tensor.transpose(spread[j][:, c, :], scale_cols[:, j, c : c + 1].to_broadcast([P, P]), ident[:])
-
-        def copy_scales(j):
-            nc.scalar.activation(
-                out=x_scales[:, j * HALF : (j + 1) * HALF].rearrange("p (q c) -> p q c", c=PACK),
-                in_=spread[j][:].rearrange("p c q -> p q c"),
-                func=COPY,
-            )
-
         def turn_rt():
             spread["rt"] = next_bank([P, 2, P])
             for u in range(2):
@@ -160,7 +147,7 @@ def tile_factoranalysisemloadinggradient_w8_kernel(
                 in_=spread["rt"][:, :, 0 : 2 * GROUPS].bitcast(BF16).rearrange("p u (k e) -> p u k e", e=2),
             )
 
-        widened, transposed, woven_x = {}, {}, {}
+        widened, words_of, transposed, woven_x = {}, {}, {}, {}
 
         def widen(i, copy, halves=range(HALVES)):
             if i not in widened:
@@ -168,26 +155,34 @@ def tile_factoranalysisemloadinggradient_w8_kernel(
             for j in halves:
                 cols = slice(j * HALF, (j + 1) * HALF)
                 copy(out=widened[i][:, cols], in_=x_raw[i][:, cols].bitcast(FP8))
+                for u in range(2):
+                    words_of[i, j, u] = widened[i][:, cols].bitcast(F32)[:, u : 2 * P : 2]
 
-        def widen_and_scale(i, lo=0, hi=D):
-            if i not in widened:
-                widened[i] = widened_pool.tile([P, D], BF16, name="widened")
-            nc.vector.tensor_tensor(
-                out=widened[i][:, lo:hi], in0=x_raw[i][:, lo:hi].bitcast(FP8), in1=x_scales[:, lo:hi], op=MULT
+        def widen_sorted(first, lo, hi):
+            tile = widened_pool.tile([P, 2, hi - lo, P, 2], BF16, name="sorted", bufs=3)
+            nc.vector.tensor_scalar(
+                out=tile[:].rearrange("p u b q e -> p (b q) u e"),
+                in0=x_rows[first][:, lo * HALF : hi * HALF].bitcast(FP8).rearrange("p (q u e) -> p q u e", u=2, e=2),
+                scalar1=ones[:],
+                scalar2=None,
+                op0=MULT,
             )
+            for b in range(lo, hi):
+                for u in range(2):
+                    words_of[first + b // 2, b % 2, u] = tile[:, u, b - lo, :, :].rearrange("p q e -> p (q e)").bitcast(F32)
 
         def transpose(i, halves=range(HALVES)):
-            words = widened[i][:].bitcast(F32)
             bank = next_bank([P, HALVES, 2, P])
             for j in halves:
                 transposed[i, j] = bank
                 for u in range(2):
-                    nc.tensor.transpose(bank[:, j, u, :], words[:, 256 * j + u : 256 * (j + 1) : 2], ident[:])
+                    nc.tensor.transpose(bank[:, j, u, :], words_of[i, j, u], ident[:])
 
         def woven_tile(i):
             s, h = divmod(i, 2)
             if s not in woven_x:
-                woven_x[s] = woven_pool.tile([P, 2, HALVES * P * PACK], BF16, name="woven_x", align_bytes=64)
+                pool, name = (keep, "woven_gpsimd") if s == 2 else (woven_pool, "woven_x")
+                woven_x[s] = pool.tile([P, 2, HALVES * P * PACK], BF16, name=name, align_bytes=64)
             return woven_x[s][:, h, :]
 
         def scale_out(i, halves=range(HALVES)):
@@ -200,12 +195,6 @@ def tile_factoranalysisemloadinggradient_w8_kernel(
                     in1=scales.unsqueeze(1).to_broadcast([P, P, 2, 2]),
                     op=MULT,
                 )
-
-        def copy_out(i):
-            nc.scalar.copy(
-                out=woven_tile(i).bitcast(F32).rearrange("p (j m u) -> p j m u", j=HALVES, u=2),
-                in_=transposed[i, 0][:].rearrange("p j u m -> p j m u"),
-            )
 
         def quantize_x(i, lo=0, hi=HALVES):
             s, h = divmod(i, 2)
@@ -236,118 +225,92 @@ def tile_factoranalysisemloadinggradient_w8_kernel(
                     stop=(j == HALVES - 1),
                 )
 
-        products, woven_z, woven_e = {}, {}, {}
-        z_planes = []
-        for g in range(GROUPS):
-            z_planes.append(keep.tile([P, PACK, K], BF16, name="z_planes%d" % g))
-        e_planes = keep.tile([P, GROUPS, PACK, HALF], BF16, name="e_planes")
+        products, planes, woven = {}, {}, {}
+        weights = (beta_codes, p_codes[0], p_codes[1])
 
-        def multiply_wide(kind, i):
-            products[kind, i] = next_bank([P, K])
-            if kind == "z":
-                multiply(products[kind, i][:], i, beta_codes, 0, D, K)
-            else:
-                multiply(products[kind, i][:], i, p_codes[0], 0, 0, HALF)
+        def multiply_wide(part, i):
+            products[part, i] = next_bank([P, K])
+            multiply(products[part, i][:], i, weights[part], 0, (D, 0, HALF)[part], K)
 
-        def scale_wide(kind, i):
+        def scale_wide(part, i):
             g, c = divmod(i, PACK)
-            plane, factor = (z_planes[g][:, c, :], T) if kind == "z" else (e_planes[:, g, c, :], R)
-            nc.scalar.activation(out=plane, in_=products[kind, i][:], func=COPY, scale=rt[:, factor, i : i + 1])
+            if (g, part) not in planes:
+                planes[g, part] = keep.tile([P, PACK, K], BF16, name="planes%d_%d" % (g, part))
+            nc.scalar.activation(
+                out=planes[g, part][:, c, :],
+                in_=products[part, i][:],
+                func=COPY,
+                scale=rt[:, R if part else T, i : i + 1],
+            )
 
-        def wide(i):
-            for kind in ("z", "e"):
-                multiply_wide(kind, i)
-                scale_wide(kind, i)
+        def wide(i, parts):
+            for part in parts:
+                multiply_wide(part, i)
+                scale_wide(part, i)
 
-        def weave_z(g, lo, hi, copy):
-            if g not in woven_z:
-                woven_z[g] = woven_pool.tile([P, K, PACK], BF16, name="woven_z", bufs=3, align_bytes=64)
+        def weave(g, lo, hi, copy):
+            woven[g, lo] = keep.tile([P, hi - lo, PACK], BF16, name="woven%d_%d" % (g, lo), align_bytes=64)
             copy(
-                out=woven_z[g][:, lo:hi, :].rearrange("p (b n) c -> p b c n", n=4),
-                in_=z_planes[g][:, :, lo:hi].rearrange("p c (b n) -> p b c n", n=4),
+                out=woven[g, lo][:].rearrange("p (b n) c -> p b c n", n=4),
+                in_=planes[g, lo // K][:, :, lo % K : lo % K + hi - lo].rearrange("p c (b n) -> p b c n", n=4),
             )
 
-        def quantize_z(g):
-            nc.vector.quantize_mx(
-                out=z_codes[g][:].bitcast(X4), scales=z_code_scales[g][:], in_=woven_z[g][:].rearrange("p n c -> p (n c)")
-            )
-
-        def woven_chunk(m):
-            if m not in woven_e:
-                name = "woven_e%d" % {4: 0, 0: 0, 1: 0, 5: 1, 7: 1, 6: 2, 3: 4, 2: 3}[m]
-                woven_e[m] = keep.tile([P, GROUPS, P, PACK], BF16, name=name, align_bytes=64)
-            return woven_e[m]
-
-        def weave_e_gpsimd(m):
+        def weave_gpsimd(g, lo, hi):
+            woven[g, lo] = keep.tile([P, hi - lo, PACK], BF16, name="woven_gpsimd", align_bytes=64)
             nc.gpsimd.tensor_scalar(
-                out=woven_chunk(m)[:],
-                in0=e_planes[:, :, :, P * m : P * (m + 1)].rearrange("p g c n -> p g n c"),
+                out=woven[g, lo][:],
+                in0=planes[g, lo // K][:, :, lo % K : lo % K + hi - lo].rearrange("p c n -> p n c"),
                 scalar1=1.0,
                 scalar2=0.0,
                 op0=MULT,
                 op1=ADD,
             )
 
-        def weave_e(m):
-            nc.scalar.copy(
-                out=woven_chunk(m)[:].rearrange("p g (b n) c -> p g b c n", n=4),
-                in_=e_planes[:, :, :, P * m : P * (m + 1)].rearrange("p g c (b n) -> p g b c n", n=4),
+        def quantize(g, lo):
+            hi = lo + woven[g, lo].shape[1]
+            nc.vector.quantize_mx(
+                out=codes[g][:, lo:hi].bitcast(X4),
+                scales=code_scales[g][:, lo:hi],
+                in_=woven[g, lo][:].rearrange("p n c -> p (n c)"),
             )
 
-        def multiply_narrow(m, g):
-            products[m, g] = next_bank([P, PACK, P])
+        def multiply_narrow(g, chunk):
+            products[g, chunk, "narrow"] = next_bank([P, PACK, P])
             for c in range(PACK):
-                multiply(products[m, g][:, c, :], g * PACK + c, p_codes[1], P * m - HALF, P * m, P)
+                multiply(products[g, chunk, "narrow"][:, c, :], g * PACK + c, p_codes[1], P * chunk, HALF + P * chunk, P)
 
-        def scale_narrow(m, g):
+        def scale_narrow(g, chunk):
+            if chunk == 0:
+                woven[g, D] = keep.tile([P, HALF, PACK], BF16, name="woven%d_%d" % (g, D), align_bytes=64)
             factors = rt[:, R, g * PACK : (g + 1) * PACK]
             nc.vector.tensor_tensor(
-                out=woven_chunk(m)[:, g, :, :],
-                in0=products[m, g][:].rearrange("p c n -> p n c"),
+                out=woven[g, D][:, P * chunk : P * (chunk + 1), :],
+                in0=products[g, chunk, "narrow"][:].rearrange("p c n -> p n c"),
                 in1=factors.unsqueeze(1).to_broadcast([P, P, PACK]),
                 op=MULT,
             )
 
-        last_planes = keep.tile([P, GROUPS, PACK, P], BF16, name="last_planes")
+        sums, added, v_scaled = {}, {}, {}
 
-        def scale_last(g):
-            for c in range(PACK):
-                i = g * PACK + c
-                nc.scalar.activation(
-                    out=last_planes[:, g, c, :], in_=products[7, g][:, c, :], func=COPY, scale=rt[:, R, i : i + 1]
-                )
-
-        def weave_last():
-            nc.scalar.copy(
-                out=woven_chunk(7)[:].rearrange("p g (b n) c -> p g b c n", n=4),
-                in_=last_planes[:].rearrange("p g c (b n) -> p g b c n", n=4),
-            )
-
-        def quantize_e(m):
-            nc.vector.quantize_mx(
-                out=e_codes[m][:].bitcast(X4),
-                scales=e_code_scales[m][:],
-                in_=woven_e[m][:].rearrange("p g n c -> p (g n c)"),
-            )
-
-        sums, v_scaled = {}, {}
-
-        def contract(m, lo=0, hi=K):
-            sums[m, lo] = next_bank([P, K])
-            for g in range(GROUPS):
-                cols = slice(P * g, P * (g + 1))
+        def contract(m, groups, lo=0, hi=K):
+            if (m, lo) not in sums:
+                sums[m, lo] = next_bank([P, K])
+                added[m, lo] = -1
+            cols = slice(K + P * m, K + P * (m + 1))
+            for g in groups:
+                added[m, lo] = added[m, lo] + 1
                 nc.tensor.matmul_mx(
                     out=sums[m, lo][:, 0 : hi - lo],
-                    lhsT=e_codes[m][:, cols].bitcast(X4),
-                    lhsT_scale=e_code_scales[m][:, cols],
-                    rhs=z_codes[g][:, lo:hi].bitcast(X4),
-                    rhs_scale=z_code_scales[g][:, lo:hi],
-                    start=(g == 0),
-                    stop=(g == GROUPS - 1),
+                    lhsT=codes[g][:, cols].bitcast(X4),
+                    lhsT_scale=code_scales[g][:, cols],
+                    rhs=codes[g][:, lo:hi].bitcast(X4),
+                    rhs_scale=code_scales[g][:, lo:hi],
+                    start=(added[m, lo] == 0),
+                    stop=(added[m, lo] == GROUPS - 1),
                 )
 
         def scale_v(m):
-            v_scaled[m] = result_pool.tile([P, K], F32, name="v_scaled")
+            v_scaled[m] = result_pool.tile([P, K], F32, name="v_scaled", bufs=8)
             nc.scalar.activation(out=v_scaled[m][:], in_=v_in[:, m, :], func=COPY, scale=inv_psi[:, m : m + 1])
 
         def finish(m, lo=0, hi=K):
@@ -364,151 +327,129 @@ def tile_factoranalysisemloadinggradient_w8_kernel(
 
         vector, scalar = nc.vector.tensor_copy, nc.scalar.copy
 
+        every = range(GROUPS)
         keep_busy(4)
-        spread_scales(0)
-        widen(0, vector)
-        widen(1, vector)
-        copy_scales(0)
+        widen_sorted(0, 0, 1)
+        widen_sorted(0, 1, 2)
+        widen_sorted(1, 0, 2)
+        for i in range(2, 6):
+            widen(i, scalar)
         transpose(0, (0,))
         transpose(0, (1,))
         transpose(1)
-        widen(2, scalar)
-        widen(3, scalar)
         keep_busy(2)
-        spread_scales(1)
         scale_out(0)
         quantize_x(0, 0, 1)
         quantize_x(0, 1, 2)
         transpose(2)
-        scale_out(1)
-        multiply_wide("z", 0)
-        turn_rt()
         transpose(3)
-        copy_rt()
-        copy_scales(1)
+        scale_out(1)
         scale_out(2, (0,))
         quantize_x(1)
         scale_out(2, (1,))
-        scale_wide("z", 0)
-        multiply_wide("z", 1)
-        multiply_wide("e", 0)
-        multiply_wide("e", 1)
-        scale_wide("z", 1)
-        scale_wide("e", 0)
-        scale_wide("e", 1)
+        multiply_wide(0, 0)
+        turn_rt()
+        transpose(4)
+        copy_rt()
+        multiply_wide(0, 1)
+        scale_wide(0, 0)
+        scale_wide(0, 1)
         scale_out(3, (0,))
         quantize_x(2)
         scale_out(3, (1,))
-        widen_and_scale(4)
-        quantize_x(3)
-        widen_and_scale(5)
-        wide(2)
-        transpose(4)
-        copy_out(4)
-        wide(3)
         transpose(5)
-        copy_out(5)
-        widen_and_scale(6, 0, HALF)
-        quantize_x(4)
-        widen_and_scale(6, HALF, D)
-        widen_and_scale(7)
-        wide(4)
-        for a in range(6, TILES, 2):
-            for i in (a, a + 1):
-                transpose(i)
-            for i in (a, a + 1):
-                copy_out(i)
-            quantize_x(a - 1)
-            if a + 2 < TILES:
-                widen_and_scale(a + 2)
+        wide(0, (1,))
+        wide(1, (1,))
+        scale_out(4, (0,))
+        quantize_x(3)
+        scale_out(4, (1,))
+        wide(2, (0, 1))
+        wide(3, (0, 1))
+        scale_out(5)
+        pieces = {2: (0, 0, 256), 3: (0, 256, 512), 4: (1, 0, 256), 5: (1, 256, 512), 6: (2, 0, 512)}
+        for s in range(2, STEPS):
+            a = 2 * s
+            g, h = divmod(s, 2)
+            more = s + 1 < STEPS
+            if more:
+                widen_sorted(a + 2, 0, 4)
+                transpose(a + 2)
+                transpose(a + 3)
+            quantize_x_pair(s)
+            if s == 2:
+                nc.vector.reciprocal(out=inv_psi[:], in_=psi_in[:, :, 0])
+                scale_v(0)
+                scale_v(1)
+            if s == 3:
+                nc.vector.tensor_scalar(out=gain[:], in0=inv_psi[:], scalar1=1.0 / N, scalar2=None, op0=MULT)
+            if s == 7:
+                quantize(0, K)
+                quantize(0, K + 256)
+            if 2 < s < 7:
+                quantize(*pieces[s - 1][0:2])
+            if s < 7:
+                weave_gpsimd(*pieces[s])
+            if g in (1, 2):
+                for part in (0, 1, 2):
+                    wide(a, (part,))
+                    wide(a + 1, (part,))
             else:
-                weave_z(1, 0, K, vector)
-            quantize_x(a)
-            if a + 2 < TILES:
-                widen_and_scale(a + 3)
-            if a == 8:
-                weave_z(0, 0, K // 2, vector)
-            if a == 10:
-                weave_z(0, K // 2, K, vector)
-            if a == 12:
-                quantize_z(0)
-            if a == 14:
-                quantize_x(15)
-                weave_z(2, 0, K, vector)
-                quantize_z(1)
-            wide(a - 1)
-            wide(a)
-
-        multiply_wide("z", 15)
-        scale_wide("z", 15)
-        nc.vector.reciprocal(out=inv_psi[:], in_=psi_in[:, :, 0])
-        weave_z(3, 0, K, scalar)
-        for g in range(GROUPS):
-            multiply_narrow(4, g)
-        multiply_wide("e", 15)
-        quantize_z(2)
-        scale_narrow(4, 0)
-        nc.vector.tensor_scalar(out=gain[:], in0=inv_psi[:], scalar1=1.0 / N, scalar2=None, op0=MULT)
-        scale_wide("e", 15)
-        scale_v(4)
-        scale_v(5)
-        for g in range(1, GROUPS):
-            scale_narrow(4, g)
-        for g in range(GROUPS):
-            multiply_narrow(5, g)
-        quantize_z(3)
-        quantize_e(4)
-        weave_e_gpsimd(0)
-        for g in range(GROUPS):
-            scale_narrow(5, g)
-        multiply_narrow(7, 0)
-        multiply_narrow(6, 0)
-        multiply_narrow(7, 1)
-        contract(4)
-        multiply_narrow(6, 1)
-        multiply_narrow(6, 2)
-        weave_e(2)
-        scale_last(0)
-        scale_last(1)
-        weave_e(3)
-        scale_narrow(6, 0)
-        quantize_e(5)
-        quantize_e(2)
-        quantize_e(0)
-        weave_e_gpsimd(1)
-        multiply_narrow(6, 3)
-        multiply_narrow(7, 2)
-        multiply_narrow(7, 3)
-        contract(5)
-        contract(0)
-        contract(2)
-        scale_last(2)
-        scale_last(3)
-        scale_v(0)
-        weave_last()
-        finish(4)
-        scale_narrow(6, 1)
-        scale_narrow(6, 2)
-        scale_narrow(6, 3)
-        finish(5)
-        quantize_e(3)
-        quantize_e(6)
-        quantize_e(1)
+                multiply_narrow(0, 2 * h)
+                multiply_narrow(0, 2 * h + 1)
+                for part in (0, 1):
+                    wide(a, (part,))
+                    wide(a + 1, (part,))
+            if more:
+                scale_out(a + 2)
+                scale_out(a + 3)
+            if g == 3:
+                scale_narrow(0, 2 * h)
+                scale_narrow(0, 2 * h + 1)
+            if s < 6:
+                weave(g - 1, K + 256 * h, K + 256 * (h + 1), scalar)
+        for chunk in range(4):
+            multiply_narrow(3, chunk)
+        weave(3, 0, K, scalar)
+        weave(3, K, D, scalar)
+        quantize(1, K)
+        quantize(1, K + 256)
+        weave(2, K, D, vector)
+        quantize(0, D)
+        quantize(2, K)
+        quantize(2, 0)
+        weave_gpsimd(1, D, D + 256)
+        for chunk in range(4):
+            scale_narrow(3, chunk)
+        for g in range(3):
+            for m in range(4):
+                contract(m, (g,))
+        weave(2, D, D + 256, scalar)
         scale_v(2)
         scale_v(3)
-        scale_v(6)
-        scale_v(1)
-        scale_v(7)
+        weave(2, D + 256, WIDE, scalar)
+        quantize(3, 0)
+        quantize(3, D)
+        quantize(3, K)
+        for m in range(4):
+            contract(m, (3,))
+        quantize(2, D)
+        quantize(1, D)
+        weave_gpsimd(1, D + 256, WIDE)
+        for m in range(4, 8):
+            scale_v(m)
         finish(0)
-        contract(3)
-        quantize_e(7)
-        finish(2)
-        contract(6)
-        finish(3)
-        contract(1)
-        finish(6)
-        contract(7, 0, 256)
         finish(1)
-        contract(7, 256, 512)
+        contract(4, (0, 3, 2, 1))
+        finish(2)
+        contract(5, every)
+        quantize(2, D + 256)
+        quantize(1, D + 256)
+        finish(3)
+        finish(4)
+        contract(6, (0, 3, 2, 1))
+        finish(5)
+        contract(7, every, 0, 256)
+        finish(6)
+        contract(7, every, 256, 512)
         finish(7, 0, 256)
         finish(7, 256, 512)

@@ -47,9 +47,9 @@ def tile_factoranalysisemloadinggradient_w8_kernel(
 
         taken = []
 
-        def next_bank(shape):
+        def next_bank(shape, dtype=F32):
             taken.append(len(taken) % BANKS)
-            return psum.tile(shape, F32, name="bank%d" % taken[-1])
+            return psum.tile(shape, dtype, name="bank%d" % taken[-1])
 
         w_scales = keep.tile([P, D + K], U8, name="w_scales", align_bytes=64)
         nc.vector.memset(w_scales[:].bitcast(I32), 0)
@@ -86,24 +86,26 @@ def tile_factoranalysisemloadinggradient_w8_kernel(
         p_rows = p_words.rearrange("g p n c -> p g (n c)")
         rt_rows = keep.tile([P, P * PACK], BF16, name="rt_rows")
         nc.vector.memset(rt_rows[:], 0.0)
-        psi_in = keep.tile([P, OUT_TILES, 2], BF16, name="psi_in")
         v_in = keep.tile([P, OUT_TILES, K], BF16, name="v_in")
 
         nc.gpsimd.dma_start(out=rt_rows[T * GROUPS : (T + 1) * GROUPS, :], in_=t.rearrange("(g n) -> g n", g=GROUPS))
         nc.gpsimd.dma_start(out=rt_rows[R * GROUPS : (R + 1) * GROUPS, :], in_=r.rearrange("(g n) -> g n", g=GROUPS))
+        psi_rows = keep.tile([P, P], BF16, name="psi_rows")
+        nc.vector.memset(psi_rows[:], 0.0)
+        ident_bf16 = keep.tile([P, P], BF16, name="ident_bf16")
+        nc.vector.tensor_copy(out=ident_bf16[:], in_=ident[:])
         nc.scalar.dma_start(out=scale_cols[:], in_=x_scale.rearrange("o (j p c) -> p (o j) c", p=P, c=PACK))
         load_x(0, 1)
         load_x(1, 1)
         load_x(2, 2)
         load_scales(beta_scales, K, D, range(4))
-        nc.sync.dma_start(out=beta_codes[:], in_=beta_words.rearrange("g p n c -> p g (n c)"))
         load_x(4, 2)
+        nc.sync.dma_start(out=beta_codes[:], in_=beta_words.rearrange("g p n c -> p g (n c)"))
         nc.sync.dma_start(out=p_codes[0][:], in_=p_rows[:, :, 0 : HALF * PACK])
         load_scales(p_scales, D, 0, range(4))
+        nc.sync.dma_start(out=psi_rows[0:OUT_TILES, :], in_=psi.rearrange("(m p) -> m p", p=P))
         load_x(6, 2)
         nc.sync.dma_start(out=p_codes[1][:], in_=p_rows[:, :, HALF * PACK : D * PACK])
-        with nc.allow_non_contiguous_dma(reason="vectors of one value a case or a row, laid on the partitions"):
-            nc.sync.dma_start(out=psi_in[:, :, 0:1], in_=psi.rearrange("(m p o) -> p m o", p=P, o=1))
         nc.sync.dma_start(out=v_in[:], in_=v.rearrange("(m p) k -> p m k", p=P))
         load_x(8, 4)
         load_x(12, 4)
@@ -141,6 +143,13 @@ def tile_factoranalysisemloadinggradient_w8_kernel(
             for u in range(2):
                 nc.tensor.transpose(spread["rt"][:, u, :], rt_rows[:].bitcast(F32)[:, u : 2 * P : 2], ident[:])
 
+        def turn_psi():
+            spread["psi"] = next_bank([P, P], BF16)
+            nc.tensor.transpose(spread["psi"][:], psi_rows[:], ident_bf16[:])
+
+        def invert_psi():
+            nc.vector.reciprocal(out=inv_psi[:], in_=spread["psi"][:, 0:OUT_TILES])
+
         def copy_rt():
             nc.scalar.copy(
                 out=rt[:].rearrange("p w (g u e) -> p u (w g) e", u=2, e=2),
@@ -159,7 +168,7 @@ def tile_factoranalysisemloadinggradient_w8_kernel(
                     words_of[i, j, u] = widened[i][:, cols].bitcast(F32)[:, u : 2 * P : 2]
 
         def widen_sorted(first, lo, hi):
-            tile = widened_pool.tile([P, 2, hi - lo, P, 2], BF16, name="sorted", bufs=3)
+            tile = widened_pool.tile([P, 2, hi - lo, P, 2], BF16, name="sorted", bufs=4)
             nc.vector.tensor_scalar(
                 out=tile[:].rearrange("p u b q e -> p (b q) u e"),
                 in0=x_rows[first][:, lo * HALF : hi * HALF].bitcast(FP8).rearrange("p (q u e) -> p q u e", u=2, e=2),
@@ -255,8 +264,9 @@ def tile_factoranalysisemloadinggradient_w8_kernel(
                 in_=planes[g, lo // K][:, :, lo % K : lo % K + hi - lo].rearrange("p c (b n) -> p b c n", n=4),
             )
 
-        def weave_gpsimd(g, lo, hi):
-            woven[g, lo] = keep.tile([P, hi - lo, PACK], BF16, name="woven_gpsimd", align_bytes=64)
+        def weave_gpsimd(g, lo, hi, after=None):
+            name = "woven%d_%d" % after if after else "woven_gpsimd"
+            woven[g, lo] = keep.tile([P, hi - lo, PACK], BF16, name=name, align_bytes=64)
             nc.gpsimd.tensor_scalar(
                 out=woven[g, lo][:],
                 in0=planes[g, lo // K][:, :, lo % K : lo % K + hi - lo].rearrange("p c n -> p n c"),
@@ -310,8 +320,14 @@ def tile_factoranalysisemloadinggradient_w8_kernel(
                 )
 
         def scale_v(m):
-            v_scaled[m] = result_pool.tile([P, K], F32, name="v_scaled", bufs=8)
+            v_scaled[m] = result_pool.tile([P, K], F32, name="v_scaled", bufs=7)
             nc.scalar.activation(out=v_scaled[m][:], in_=v_in[:, m, :], func=COPY, scale=inv_psi[:, m : m + 1])
+
+        def scale_v_gpsimd(m, name):
+            v_scaled[m] = keep.tile([P, K], F32, name=name, align_bytes=64)
+            nc.gpsimd.tensor_scalar(
+                out=v_scaled[m][:], in0=v_in[:, m, :], scalar1=inv_psi[:, m : m + 1], scalar2=0.0, op0=MULT, op1=ADD
+            )
 
         def finish(m, lo=0, hi=K):
             result = result_pool.tile([P, K], F32, name="result")
@@ -336,6 +352,7 @@ def tile_factoranalysisemloadinggradient_w8_kernel(
             widen(i, scalar)
         transpose(0, (0,))
         transpose(0, (1,))
+        keep_busy(1)
         transpose(1)
         keep_busy(2)
         scale_out(0)
@@ -343,21 +360,23 @@ def tile_factoranalysisemloadinggradient_w8_kernel(
         quantize_x(0, 1, 2)
         transpose(2)
         transpose(3)
+        turn_rt()
+        keep_busy(1)
         scale_out(1)
         scale_out(2, (0,))
         quantize_x(1)
         scale_out(2, (1,))
         multiply_wide(0, 0)
-        turn_rt()
-        transpose(4)
         copy_rt()
         multiply_wide(0, 1)
+        transpose(4)
         scale_wide(0, 0)
         scale_wide(0, 1)
         scale_out(3, (0,))
         quantize_x(2)
         scale_out(3, (1,))
         transpose(5)
+        turn_psi()
         wide(0, (1,))
         wide(1, (1,))
         scale_out(4, (0,))
@@ -365,26 +384,30 @@ def tile_factoranalysisemloadinggradient_w8_kernel(
         scale_out(4, (1,))
         wide(2, (0, 1))
         wide(3, (0, 1))
-        scale_out(5)
+        scale_out(5, (0,))
+        invert_psi()
+        scale_out(5, (1,))
+        scale_v(0)
         pieces = {2: (0, 0, 256), 3: (0, 256, 512), 4: (1, 0, 256), 5: (1, 256, 512), 6: (2, 0, 512)}
         for s in range(2, STEPS):
             a = 2 * s
             g, h = divmod(s, 2)
             more = s + 1 < STEPS
             if more:
-                widen_sorted(a + 2, 0, 4)
+                widen_sorted(a + 2, 0, 2)
+                widen_sorted(a + 3, 0, 2)
                 transpose(a + 2)
                 transpose(a + 3)
             quantize_x_pair(s)
             if s == 2:
-                nc.vector.reciprocal(out=inv_psi[:], in_=psi_in[:, :, 0])
-                scale_v(0)
-                scale_v(1)
-            if s == 3:
                 nc.vector.tensor_scalar(out=gain[:], in0=inv_psi[:], scalar1=1.0 / N, scalar2=None, op0=MULT)
             if s == 7:
                 quantize(0, K)
                 quantize(0, K + 256)
+                quantize(1, K)
+                quantize(1, K + 256)
+                quantize(2, 0)
+                weave_gpsimd(2, K, D)
             if 2 < s < 7:
                 quantize(*pieces[s - 1][0:2])
             if s < 7:
@@ -396,7 +419,13 @@ def tile_factoranalysisemloadinggradient_w8_kernel(
             else:
                 multiply_narrow(0, 2 * h)
                 multiply_narrow(0, 2 * h + 1)
+                if s == 7:
+                    weave(2, D, D + 256, scalar)
                 for part in (0, 1):
+                    if s == 7 and part == 1:
+                        weave(3, 0, K, scalar)
+                        for chunk in range(4):
+                            multiply_narrow(3, chunk)
                     wide(a, (part,))
                     wide(a + 1, (part,))
             if more:
@@ -408,43 +437,38 @@ def tile_factoranalysisemloadinggradient_w8_kernel(
             if s < 6:
                 weave(g - 1, K + 256 * h, K + 256 * (h + 1), scalar)
         for chunk in range(4):
-            multiply_narrow(3, chunk)
-        weave(3, 0, K, scalar)
-        weave(3, K, D, scalar)
-        quantize(1, K)
-        quantize(1, K + 256)
-        weave(2, K, D, vector)
-        quantize(0, D)
-        quantize(2, K)
-        quantize(2, 0)
-        weave_gpsimd(1, D, D + 256)
-        for chunk in range(4):
             scale_narrow(3, chunk)
+        weave(3, K, K + 256, scalar)
+        weave(1, D, D + 256, scalar)
+        quantize(2, K)
+        quantize(0, D)
+        quantize(3, 0)
+        quantize(3, D)
+        weave(3, K + 256, D, vector)
         for g in range(3):
             for m in range(4):
                 contract(m, (g,))
-        weave(2, D, D + 256, scalar)
-        scale_v(2)
-        scale_v(3)
+        for m in (1, 2, 3):
+            scale_v(m)
         weave(2, D + 256, WIDE, scalar)
-        quantize(3, 0)
-        quantize(3, D)
         quantize(3, K)
+        quantize(2, D)
+        quantize(3, K + 256)
+        quantize(1, D)
         for m in range(4):
             contract(m, (3,))
-        quantize(2, D)
-        quantize(1, D)
-        weave_gpsimd(1, D + 256, WIDE)
-        for m in range(4, 8):
+        weave_gpsimd(1, D + 256, WIDE, (1, D))
+        for m in (4, 5, 6):
             scale_v(m)
         finish(0)
         finish(1)
         contract(4, (0, 3, 2, 1))
         finish(2)
+        finish(3)
         contract(5, every)
         quantize(2, D + 256)
         quantize(1, D + 256)
-        finish(3)
+        scale_v_gpsimd(7, "woven%d_%d" % (1, D))
         finish(4)
         contract(6, (0, 3, 2, 1))
         finish(5)

@@ -103,12 +103,12 @@ def tile_factoranalysisemloadinggradient_w8_kernel(
         nc.sync.dma_start(out=beta_codes[:], in_=beta_words.rearrange("g p n c -> p g (n c)"))
         nc.sync.dma_start(out=p_codes[0][:], in_=p_rows[:, :, 0 : HALF * PACK])
         load_scales(p_scales, D, 0, range(4))
-        nc.sync.dma_start(out=psi_rows[0:OUT_TILES, :], in_=psi.rearrange("(m p) -> m p", p=P))
         load_x(6, 2)
+        nc.sync.dma_start(out=psi_rows[0:OUT_TILES, :], in_=psi.rearrange("(m p) -> m p", p=P))
         nc.sync.dma_start(out=p_codes[1][:], in_=p_rows[:, :, HALF * PACK : D * PACK])
-        nc.sync.dma_start(out=v_in[:], in_=v.rearrange("(m p) k -> p m k", p=P))
         load_x(8, 4)
         load_x(12, 4)
+        nc.sync.dma_start(out=v_in[:], in_=v.rearrange("(m p) k -> p m k", p=P))
 
         ones = keep.tile([P, 1], F32, name="ones")
         nc.vector.memset(ones[:], 1.0)
@@ -376,7 +376,6 @@ def tile_factoranalysisemloadinggradient_w8_kernel(
         quantize_x(2)
         scale_out(3, (1,))
         transpose(5)
-        turn_psi()
         wide(0, (1,))
         wide(1, (1,))
         scale_out(4, (0,))
@@ -385,9 +384,7 @@ def tile_factoranalysisemloadinggradient_w8_kernel(
         wide(2, (0, 1))
         wide(3, (0, 1))
         scale_out(5, (0,))
-        invert_psi()
         scale_out(5, (1,))
-        scale_v(0)
         pieces = {2: (0, 0, 256), 3: (0, 256, 512), 4: (1, 0, 256), 5: (1, 256, 512), 6: (2, 0, 512)}
         for s in range(2, STEPS):
             a = 2 * s
@@ -398,8 +395,12 @@ def tile_factoranalysisemloadinggradient_w8_kernel(
                 widen_sorted(a + 3, 0, 2)
                 transpose(a + 2)
                 transpose(a + 3)
-            quantize_x_pair(s)
             if s == 2:
+                turn_psi()
+            quantize_x_pair(s)
+            if s == 3:
+                invert_psi()
+            if s == 4:
                 nc.vector.tensor_scalar(out=gain[:], in0=inv_psi[:], scalar1=1.0 / N, scalar2=None, op0=MULT)
             if s == 7:
                 quantize(0, K)
@@ -412,18 +413,22 @@ def tile_factoranalysisemloadinggradient_w8_kernel(
                 quantize(*pieces[s - 1][0:2])
             if s < 7:
                 weave_gpsimd(*pieces[s])
+            if s == 2:
+                weave(0, K, K + 256, scalar)
             if g in (1, 2):
                 for part in (0, 1, 2):
                     wide(a, (part,))
                     wide(a + 1, (part,))
+                    if part == 0 and s > 2:
+                        weave(g - 1, K + 256 * h, K + 256 * (h + 1), scalar)
             else:
                 multiply_narrow(0, 2 * h)
                 multiply_narrow(0, 2 * h + 1)
-                if s == 7:
-                    weave(2, D, D + 256, scalar)
                 for part in (0, 1):
+                    if s == 6 and part == 1:
+                        weave(2, D, D + 256, scalar)
                     if s == 7 and part == 1:
-                        weave(3, 0, K, scalar)
+                        weave(3, 0, 256, scalar)
                         for chunk in range(4):
                             multiply_narrow(3, chunk)
                     wide(a, (part,))
@@ -434,26 +439,28 @@ def tile_factoranalysisemloadinggradient_w8_kernel(
             if g == 3:
                 scale_narrow(0, 2 * h)
                 scale_narrow(0, 2 * h + 1)
-            if s < 6:
-                weave(g - 1, K + 256 * h, K + 256 * (h + 1), scalar)
         for chunk in range(4):
             scale_narrow(3, chunk)
         weave(3, K, K + 256, scalar)
         weave(1, D, D + 256, scalar)
+        scale_v(0)
+        scale_v(1)
+        weave(3, 256, K, vector)
         quantize(2, K)
-        quantize(0, D)
         quantize(3, 0)
-        quantize(3, D)
         weave(3, K + 256, D, vector)
+        quantize(3, 256)
+        quantize(0, D)
         for g in range(3):
             for m in range(4):
                 contract(m, (g,))
-        for m in (1, 2, 3):
-            scale_v(m)
+        scale_v(2)
+        scale_v(3)
         weave(2, D + 256, WIDE, scalar)
         quantize(3, K)
-        quantize(2, D)
         quantize(3, K + 256)
+        quantize(3, D)
+        quantize(2, D)
         quantize(1, D)
         for m in range(4):
             contract(m, (3,))

@@ -103,8 +103,8 @@ def tile_factoranalysisemloadinggradient_w8_kernel(
         nc.sync.dma_start(out=beta_codes[:], in_=beta_words.rearrange("g p n c -> p g (n c)"))
         nc.sync.dma_start(out=p_codes[0][:], in_=p_rows[:, :, 0 : HALF * PACK])
         load_scales(p_scales, D, 0, range(4))
-        load_x(6, 2)
         nc.sync.dma_start(out=psi_rows[0:OUT_TILES, :], in_=psi.rearrange("(m p) -> m p", p=P))
+        load_x(6, 2)
         nc.sync.dma_start(out=p_codes[1][:], in_=p_rows[:, :, HALF * PACK : D * PACK])
         load_x(8, 4)
         load_x(12, 4)
@@ -135,6 +135,15 @@ def tile_factoranalysisemloadinggradient_w8_kernel(
                     start=True,
                     stop=True,
                 )
+
+        def keep_busy_long():
+            nc.tensor.matmul(
+                out=idle_bank[:].rearrange("p (a n) -> p a n", n=P),
+                lhsT=ident[:],
+                rhs=ident[:].unsqueeze(1).to_broadcast([P, K // P, P]),
+                start=True,
+                stop=True,
+            )
 
         spread = {}
 
@@ -344,7 +353,8 @@ def tile_factoranalysisemloadinggradient_w8_kernel(
         vector, scalar = nc.vector.tensor_copy, nc.scalar.copy
 
         every = range(GROUPS)
-        keep_busy(4)
+        keep_busy(2)
+        keep_busy_long()
         widen_sorted(0, 0, 1)
         widen_sorted(0, 1, 2)
         widen_sorted(1, 0, 2)
@@ -354,7 +364,7 @@ def tile_factoranalysisemloadinggradient_w8_kernel(
         transpose(0, (1,))
         keep_busy(1)
         transpose(1)
-        keep_busy(2)
+        keep_busy_long()
         scale_out(0)
         quantize_x(0, 0, 1)
         quantize_x(0, 1, 2)
@@ -376,6 +386,7 @@ def tile_factoranalysisemloadinggradient_w8_kernel(
         quantize_x(2)
         scale_out(3, (1,))
         transpose(5)
+        turn_psi()
         wide(0, (1,))
         wide(1, (1,))
         scale_out(4, (0,))
@@ -384,6 +395,7 @@ def tile_factoranalysisemloadinggradient_w8_kernel(
         wide(2, (0, 1))
         wide(3, (0, 1))
         scale_out(5, (0,))
+        invert_psi()
         scale_out(5, (1,))
         pieces = {2: (0, 0, 256), 3: (0, 256, 512), 4: (1, 0, 256), 5: (1, 256, 512), 6: (2, 0, 512)}
         for s in range(2, STEPS):
@@ -395,12 +407,8 @@ def tile_factoranalysisemloadinggradient_w8_kernel(
                 widen_sorted(a + 3, 0, 2)
                 transpose(a + 2)
                 transpose(a + 3)
-            if s == 2:
-                turn_psi()
             quantize_x_pair(s)
-            if s == 3:
-                invert_psi()
-            if s == 4:
+            if s == 2:
                 nc.vector.tensor_scalar(out=gain[:], in0=inv_psi[:], scalar1=1.0 / N, scalar2=None, op0=MULT)
             if s == 7:
                 quantize(0, K)

@@ -88,8 +88,6 @@ def tile_factoranalysisemloadinggradient_w8_kernel(
         nc.vector.memset(rt_rows[:], 0.0)
         v_in = keep.tile([P, OUT_TILES, K], BF16, name="v_in")
 
-        nc.gpsimd.dma_start(out=rt_rows[T * GROUPS : (T + 1) * GROUPS, :], in_=t.rearrange("(g n) -> g n", g=GROUPS))
-        nc.gpsimd.dma_start(out=rt_rows[R * GROUPS : (R + 1) * GROUPS, :], in_=r.rearrange("(g n) -> g n", g=GROUPS))
         psi_rows = keep.tile([P, P], BF16, name="psi_rows")
         nc.vector.memset(psi_rows[:], 0.0)
         ident_bf16 = keep.tile([P, P], BF16, name="ident_bf16")
@@ -101,10 +99,12 @@ def tile_factoranalysisemloadinggradient_w8_kernel(
         load_scales(beta_scales, K, D, range(4))
         load_x(4, 2)
         nc.sync.dma_start(out=beta_codes[:], in_=beta_words.rearrange("g p n c -> p g (n c)"))
+        nc.sync.dma_start(out=rt_rows[T * GROUPS : (T + 1) * GROUPS, :], in_=t.rearrange("(g n) -> g n", g=GROUPS))
+        nc.sync.dma_start(out=rt_rows[R * GROUPS : (R + 1) * GROUPS, :], in_=r.rearrange("(g n) -> g n", g=GROUPS))
         nc.sync.dma_start(out=p_codes[0][:], in_=p_rows[:, :, 0 : HALF * PACK])
         load_scales(p_scales, D, 0, range(4))
-        nc.sync.dma_start(out=psi_rows[0:OUT_TILES, :], in_=psi.rearrange("(m p) -> m p", p=P))
         load_x(6, 2)
+        nc.sync.dma_start(out=psi_rows[0:OUT_TILES, :], in_=psi.rearrange("(m p) -> m p", p=P))
         nc.sync.dma_start(out=p_codes[1][:], in_=p_rows[:, :, HALF * PACK : D * PACK])
         load_x(8, 4)
         load_x(12, 4)
@@ -370,15 +370,15 @@ def tile_factoranalysisemloadinggradient_w8_kernel(
         quantize_x(0, 1, 2)
         transpose(2)
         transpose(3)
-        turn_rt()
         keep_busy(1)
         scale_out(1)
         scale_out(2, (0,))
         quantize_x(1)
         scale_out(2, (1,))
         multiply_wide(0, 0)
-        copy_rt()
         multiply_wide(0, 1)
+        turn_rt()
+        copy_rt()
         transpose(4)
         scale_wide(0, 0)
         scale_wide(0, 1)
@@ -386,7 +386,6 @@ def tile_factoranalysisemloadinggradient_w8_kernel(
         quantize_x(2)
         scale_out(3, (1,))
         transpose(5)
-        turn_psi()
         wide(0, (1,))
         wide(1, (1,))
         scale_out(4, (0,))
@@ -395,13 +394,14 @@ def tile_factoranalysisemloadinggradient_w8_kernel(
         wide(2, (0, 1))
         wide(3, (0, 1))
         scale_out(5, (0,))
-        invert_psi()
         scale_out(5, (1,))
         pieces = {2: (0, 0, 256), 3: (0, 256, 512), 4: (1, 0, 256), 5: (1, 256, 512), 6: (2, 0, 512)}
         for s in range(2, STEPS):
             a = 2 * s
             g, h = divmod(s, 2)
             more = s + 1 < STEPS
+            if s == 2:
+                turn_psi()
             if more:
                 widen_sorted(a + 2, 0, 2)
                 widen_sorted(a + 3, 0, 2)
@@ -409,6 +409,8 @@ def tile_factoranalysisemloadinggradient_w8_kernel(
                 transpose(a + 3)
             quantize_x_pair(s)
             if s == 2:
+                invert_psi()
+            if s == 3:
                 nc.vector.tensor_scalar(out=gain[:], in0=inv_psi[:], scalar1=1.0 / N, scalar2=None, op0=MULT)
             if s == 7:
                 quantize(0, K)

@@ -41,7 +41,7 @@ def tile_factoranalysisemloadinggradient_w8_kernel(
         keep = ctx.enter_context(tc.tile_pool(name="keep", bufs=1))
         widened_pool = ctx.enter_context(tc.tile_pool(name="widened_pool", bufs=4))
         woven_pool = ctx.enter_context(tc.tile_pool(name="woven_pool", bufs=3))
-        result_pool = ctx.enter_context(tc.tile_pool(name="result_pool", bufs=8))
+        result_pool = ctx.enter_context(tc.tile_pool(name="result_pool", bufs=10))
         psum = ctx.enter_context(tc.psum_pool(name="psum", bufs=1))
         ctx.enter_context(tc.manual_schedule(engines={ENGINE.PE, ENGINE.Activation, ENGINE.DVE, ENGINE.SP}))
 
@@ -70,10 +70,12 @@ def tile_factoranalysisemloadinggradient_w8_kernel(
         x_cases = x_bytes.rearrange("(g m c) k -> g m c k", m=P, c=PACK)
         x_raw, x_rows = {}, {}
 
-        def load_x(first, count):
+        def load_x(first, count, pieces=1):
             g, c = divmod(first, PACK)
             raw = keep.tile([P, count, D], U8, name="x_raw%d" % first)
-            nc.sync.dma_start(out=raw[:], in_=x_cases[g][:, c : c + count, :])
+            for n in range(pieces):
+                cols = slice(n * D // pieces, (n + 1) * D // pieces)
+                nc.sync.dma_start(out=raw[:, :, cols], in_=x_cases[g][:, c : c + count, cols])
             for n in range(count):
                 x_raw[first + n] = raw[:, n, :]
                 x_rows[first + n] = raw[:, n:count, :].rearrange("p c k -> p (c k)")
@@ -165,16 +167,14 @@ def tile_factoranalysisemloadinggradient_w8_kernel(
                 in_=spread["rt"][:, :, 0 : 2 * GROUPS].bitcast(BF16).rearrange("p u (k e) -> p u k e", e=2),
             )
 
-        widened, words_of, transposed, woven_x = {}, {}, {}, {}
+        words_of, transposed, woven_x = {}, {}, {}
 
-        def widen(i, copy, halves=range(HALVES)):
-            if i not in widened:
-                widened[i] = widened_pool.tile([P, D], BF16, name="widened")
-            for j in halves:
-                cols = slice(j * HALF, (j + 1) * HALF)
-                copy(out=widened[i][:, cols], in_=x_raw[i][:, cols].bitcast(FP8))
+        def widen(i):
+            tile = widened_pool.tile([P, D], BF16, name="widened")
+            nc.scalar.copy(out=tile[:], in_=x_raw[i].bitcast(FP8))
+            for j in range(HALVES):
                 for u in range(2):
-                    words_of[i, j, u] = widened[i][:, cols].bitcast(F32)[:, u : 2 * P : 2]
+                    words_of[i, j, u] = tile[:].bitcast(F32)[:, 2 * P * j + u : 2 * P * (j + 1) : 2]
 
         def widen_sorted(first, lo, hi):
             tile = widened_pool.tile([P, 2, hi - lo, P, 2], BF16, name="sorted", bufs=4)
@@ -266,11 +266,14 @@ def tile_factoranalysisemloadinggradient_w8_kernel(
                 multiply_wide(part, i)
                 scale_wide(part, i)
 
-        def weave(g, lo, hi, copy):
-            woven[g, lo] = keep.tile([P, hi - lo, PACK], BF16, name="woven%d_%d" % (g, lo), align_bytes=64)
+        def weave(g, lo, hi, copy, part=None):
+            if (g, lo) not in woven:
+                woven[g, lo] = keep.tile([P, hi - lo, PACK], BF16, name="woven%d_%d" % (g, lo), align_bytes=64)
+            first, width = (0, hi - lo) if part is None else (part * (hi - lo) // 2, (hi - lo) // 2)
+            col = lo % K + first
             copy(
-                out=woven[g, lo][:].rearrange("p (b n) c -> p b c n", n=4),
-                in_=planes[g, lo // K][:, :, lo % K : lo % K + hi - lo].rearrange("p c (b n) -> p b c n", n=4),
+                out=woven[g, lo][:, first : first + width, :].rearrange("p (b n) c -> p b c n", n=4),
+                in_=planes[g, lo // K][:, :, col : col + width].rearrange("p c (b n) -> p b c n", n=4),
             )
 
         def weave_gpsimd(g, lo, hi, after=None):
@@ -359,22 +362,20 @@ def tile_factoranalysisemloadinggradient_w8_kernel(
         widen_sorted(0, 1, 2)
         widen_sorted(1, 0, 2)
         for i in range(2, 6):
-            widen(i, scalar)
+            widen(i)
         transpose(0, (0,))
         transpose(0, (1,))
         keep_busy(1)
         transpose(1)
         keep_busy_long()
         scale_out(0)
-        quantize_x(0, 0, 1)
-        quantize_x(0, 1, 2)
         transpose(2)
         transpose(3)
         keep_busy(1)
         scale_out(1)
-        scale_out(2, (0,))
+        quantize_x(0)
         quantize_x(1)
-        scale_out(2, (1,))
+        scale_out(2)
         multiply_wide(0, 0)
         multiply_wide(0, 1)
         turn_rt()
@@ -393,8 +394,8 @@ def tile_factoranalysisemloadinggradient_w8_kernel(
         scale_out(4, (1,))
         wide(2, (0, 1))
         wide(3, (0, 1))
-        scale_out(5, (0,))
-        scale_out(5, (1,))
+        widen_sorted(6, 0, 2)
+        scale_out(5)
         pieces = {2: (0, 0, 256), 3: (0, 256, 512), 4: (1, 0, 256), 5: (1, 256, 512), 6: (2, 0, 512)}
         for s in range(2, STEPS):
             a = 2 * s
@@ -403,7 +404,6 @@ def tile_factoranalysisemloadinggradient_w8_kernel(
             if s == 2:
                 turn_psi()
             if more:
-                widen_sorted(a + 2, 0, 2)
                 widen_sorted(a + 3, 0, 2)
                 transpose(a + 2)
                 transpose(a + 3)
@@ -414,23 +414,23 @@ def tile_factoranalysisemloadinggradient_w8_kernel(
                 nc.vector.tensor_scalar(out=gain[:], in0=inv_psi[:], scalar1=1.0 / N, scalar2=None, op0=MULT)
             if s == 7:
                 quantize(0, K)
-                quantize(0, K + 256)
                 quantize(1, K)
-                quantize(1, K + 256)
                 quantize(2, 0)
                 weave_gpsimd(2, K, D)
             if 2 < s < 7:
                 quantize(*pieces[s - 1][0:2])
             if s < 7:
                 weave_gpsimd(*pieces[s])
+            if s + 2 < STEPS:
+                widen_sorted(a + 4, 0, 2)
             if s == 2:
-                weave(0, K, K + 256, scalar)
+                weave(0, K, D, scalar, 0)
             if g in (1, 2):
                 for part in (0, 1, 2):
                     wide(a, (part,))
                     wide(a + 1, (part,))
                     if part == 0 and s > 2:
-                        weave(g - 1, K + 256 * h, K + 256 * (h + 1), scalar)
+                        weave(g - 1, K, D, scalar, h)
             else:
                 multiply_narrow(0, 2 * h)
                 multiply_narrow(0, 2 * h + 1)
@@ -438,7 +438,8 @@ def tile_factoranalysisemloadinggradient_w8_kernel(
                     if s == 6 and part == 1:
                         weave(2, D, D + 256, scalar)
                     if s == 7 and part == 1:
-                        weave(3, 0, 256, scalar)
+                        scale_v(0)
+                        weave(3, 0, K, scalar)
                         for chunk in range(4):
                             multiply_narrow(3, chunk)
                     wide(a, (part,))
@@ -453,23 +454,20 @@ def tile_factoranalysisemloadinggradient_w8_kernel(
             scale_narrow(3, chunk)
         weave(3, K, K + 256, scalar)
         weave(1, D, D + 256, scalar)
-        scale_v(0)
         scale_v(1)
-        weave(3, 256, K, vector)
         quantize(2, K)
+        quantize(0, D)
         quantize(3, 0)
         weave(3, K + 256, D, vector)
-        quantize(3, 256)
-        quantize(0, D)
         for g in range(3):
             for m in range(4):
                 contract(m, (g,))
         scale_v(2)
         scale_v(3)
         weave(2, D + 256, WIDE, scalar)
+        quantize(3, D)
         quantize(3, K)
         quantize(3, K + 256)
-        quantize(3, D)
         quantize(2, D)
         quantize(1, D)
         for m in range(4):
@@ -483,11 +481,11 @@ def tile_factoranalysisemloadinggradient_w8_kernel(
         finish(2)
         finish(3)
         contract(5, every)
-        quantize(2, D + 256)
         quantize(1, D + 256)
-        scale_v_gpsimd(7, "woven%d_%d" % (1, D))
+        quantize(2, D + 256)
+        scale_v_gpsimd(7, "woven%d_%d" % (2, D + 256))
         finish(4)
-        contract(6, (0, 3, 2, 1))
+        contract(6, (0, 3, 1, 2))
         finish(5)
         contract(7, every, 0, 256)
         finish(6)

@@ -31,6 +31,11 @@ BANKS = 8
 
 WIDE = K + D
 R, T = 0, 1
+ALIGN = 64
+VBUFS = 6
+RBUFS = 6
+SBUFS = 5
+WBUFS = 4
 
 
 def tile_factoranalysisemloadinggradient_w8_kernel(
@@ -39,94 +44,118 @@ def tile_factoranalysisemloadinggradient_w8_kernel(
     nc = tc.nc
     with ExitStack() as ctx:
         keep = ctx.enter_context(tc.tile_pool(name="keep", bufs=1))
-        widened_pool = ctx.enter_context(tc.tile_pool(name="widened_pool", bufs=4))
-        woven_pool = ctx.enter_context(tc.tile_pool(name="woven_pool", bufs=3))
-        result_pool = ctx.enter_context(tc.tile_pool(name="result_pool", bufs=10))
+        widened_pool = ctx.enter_context(tc.tile_pool(name="widened_pool", bufs=WBUFS))
+        result_pool = ctx.enter_context(tc.tile_pool(name="result_pool", bufs=RBUFS))
         psum = ctx.enter_context(tc.psum_pool(name="psum", bufs=1))
-        ctx.enter_context(tc.manual_schedule(engines={ENGINE.PE, ENGINE.Activation, ENGINE.DVE, ENGINE.SP}))
+        ctx.enter_context(tc.manual_schedule(engines={ENGINE.PE, ENGINE.Activation, ENGINE.DVE, ENGINE.SP, ENGINE.Pool}))
 
-        taken = []
+        free_banks = list(range(BANKS))
+        bank_of = {}
 
-        def next_bank(shape, dtype=F32):
-            taken.append(len(taken) % BANKS)
-            return psum.tile(shape, dtype, name="bank%d" % taken[-1])
+        def next_bank(key, shape, dtype=F32):
+            bank_of[key] = free_banks.pop(0)
+            return psum.tile(shape, dtype, name="bank%d" % bank_of[key])
 
-        w_scales = keep.tile([P, D + K], U8, name="w_scales", align_bytes=64)
-        nc.vector.memset(w_scales[:].bitcast(I32), 0)
+        def release(key):
+            free_banks.append(bank_of[key])
+
+        beta_rows = keep.tile([P, K], U8, name="beta_rows", align_bytes=64)
+        p_rows = keep.tile([P, D], U8, name="p_rows", align_bytes=64)
+        nc.vector.memset(beta_rows[:].bitcast(I32), 0)
+        nc.vector.memset(p_rows[:].bitcast(I32), 0)
+        ones = keep.tile([P, 1], F32, name="ones")
+        nc.vector.memset(ones[:], 1.0)
 
         zeros = keep.tile([P, P], BF16, name="zeros")
         nc.gpsimd.memset(zeros[:], 0.0)
         ident = keep.tile([P, P], F32, name="ident")
         make_identity(nc, ident[:])
 
-        def load_scales(scales, width, col, quadrants):
+        def load_scales(tile, scales):
             rows_in = scales.bitcast(I32)
-            for q in quadrants:
+            for q in range(4):
                 nc.sync.dma_start(
-                    out=w_scales[32 * q : 32 * q + 4 * HALVES, col : col + width].bitcast(I32),
-                    in_=rows_in[:, 4 * q : 4 * q + 4, :],
+                    out=tile[32 * q : 32 * q + 4 * HALVES, :].bitcast(I32), in_=rows_in[:, 4 * q : 4 * q + 4, :]
                 )
 
-        x_cases = x_bytes.rearrange("(g m c) k -> g m c k", m=P, c=PACK)
-        x_raw, x_rows = {}, {}
+        def slot(i):
+            g, n = divmod(i, PACK)
+            return g, (n + 2) % PACK if g == 1 else n
 
-        def load_x(first, count, pieces=1):
-            g, c = divmod(first, PACK)
+        x_cases = x_bytes.rearrange("(g m c) k -> g m c k", m=P, c=PACK)
+        x_raw = {}
+
+        def load_x(first, count):
+            g, c = slot(first)
             raw = keep.tile([P, count, D], U8, name="x_raw%d" % first)
-            for n in range(pieces):
-                cols = slice(n * D // pieces, (n + 1) * D // pieces)
-                nc.sync.dma_start(out=raw[:, :, cols], in_=x_cases[g][:, c : c + count, cols])
+            nc.sync.dma_start(out=raw[:], in_=x_cases[g][:, c : c + count, :])
             for n in range(count):
                 x_raw[first + n] = raw[:, n, :]
-                x_rows[first + n] = raw[:, n:count, :].rearrange("p c k -> p (c k)")
+
+        def load_x_2_to_5():
+            raw = keep.tile([P, 2, 2 * D], U8, name="x_raw2")
+            rows = x_bytes.rearrange("(g m h c) k -> m g h (c k)", m=P, h=2, c=2)
+            nc.sync.dma_start(out=raw[:], in_=rows[:, 0:2, 1, :])
+            for n in range(4):
+                x_raw[2 + n] = raw[:, n // 2, n % 2 * D : (n % 2 + 1) * D]
 
         scale_cols = keep.tile([P, HALVES, PACK], F32, name="scale_cols")
-        beta_codes = keep.tile([P, HALVES, K * PACK], U8, name="beta_codes", align_bytes=64)
+        beta_codes = keep.tile([P, HALVES, K * PACK], U8, name="beta_codes", align_bytes=ALIGN)
         p_codes = []
         for h in range(2):
-            p_codes.append(keep.tile([P, HALVES, HALF * PACK], U8, name="p_codes%d" % h, align_bytes=64))
-        p_rows = p_words.rearrange("g p n c -> p g (n c)")
+            p_codes.append(keep.tile([P, HALVES, HALF * PACK], U8, name="p_codes%d" % h, align_bytes=ALIGN))
+        p_by_partition = p_words.rearrange("g p n c -> p g (n c)")
+
+        def load_p(h):
+            nc.sync.dma_start(out=p_codes[h][:], in_=p_by_partition[:, :, h * HALF * PACK : (h + 1) * HALF * PACK])
+
         rt_rows = keep.tile([P, P * PACK], BF16, name="rt_rows")
         nc.vector.memset(rt_rows[:], 0.0)
-        v_in = keep.tile([P, OUT_TILES, K], BF16, name="v_in")
+        v_in = {}
+
+        def load_v(lo, hi):
+            rows = keep.tile([P, hi - lo, K], BF16, name="v_rows%d" % lo)
+            nc.sync.dma_start(out=rows[:], in_=v.rearrange("(m p) k -> p m k", p=P)[:, lo:hi, :])
+            for m in range(lo, hi):
+                v_in[m] = rows[:, m - lo, :]
 
         psi_rows = keep.tile([P, P], BF16, name="psi_rows")
         nc.vector.memset(psi_rows[:], 0.0)
         ident_bf16 = keep.tile([P, P], BF16, name="ident_bf16")
-        nc.vector.tensor_copy(out=ident_bf16[:], in_=ident[:])
-        nc.scalar.dma_start(out=scale_cols[:], in_=x_scale.rearrange("o (j p c) -> p (o j) c", p=P, c=PACK))
-        load_x(0, 1)
-        load_x(1, 1)
-        load_x(2, 2)
-        load_scales(beta_scales, K, D, range(4))
-        load_x(4, 2)
-        nc.sync.dma_start(out=beta_codes[:], in_=beta_words.rearrange("g p n c -> p g (n c)"))
-        nc.sync.dma_start(out=rt_rows[T * GROUPS : (T + 1) * GROUPS, :], in_=t.rearrange("(g n) -> g n", g=GROUPS))
-        nc.sync.dma_start(out=rt_rows[R * GROUPS : (R + 1) * GROUPS, :], in_=r.rearrange("(g n) -> g n", g=GROUPS))
-        nc.sync.dma_start(out=p_codes[0][:], in_=p_rows[:, :, 0 : HALF * PACK])
-        load_scales(p_scales, D, 0, range(4))
-        load_x(6, 2)
-        nc.sync.dma_start(out=psi_rows[0:OUT_TILES, :], in_=psi.rearrange("(m p) -> m p", p=P))
-        nc.sync.dma_start(out=p_codes[1][:], in_=p_rows[:, :, HALF * PACK : D * PACK])
-        load_x(8, 4)
-        load_x(12, 4)
-        nc.sync.dma_start(out=v_in[:], in_=v.rearrange("(m p) k -> p m k", p=P))
 
-        ones = keep.tile([P, 1], F32, name="ones")
-        nc.vector.memset(ones[:], 1.0)
+        def load_row_factor(w, vec):
+            nc.sync.dma_start(out=rt_rows[w * GROUPS : (w + 1) * GROUPS, :], in_=vec.rearrange("(g n) -> g n", g=GROUPS))
+
+        load_x(0, 2)
+        nc.scalar.dma_start(out=scale_cols[:], in_=x_scale.rearrange("o (j p c) -> p (o j) c", p=P, c=PACK))
+        load_x_2_to_5()
+        load_scales(beta_rows, beta_scales)
+        nc.sync.dma_start(out=beta_codes[:], in_=beta_words.rearrange("g p n c -> p g (n c)"))
+        load_row_factor(T, t)
+        load_row_factor(R, r)
+        load_p(0)
+        load_scales(p_rows, p_scales)
+        load_x(6, 2)
+        load_p(1)
+        nc.sync.dma_start(out=psi_rows[0:OUT_TILES, :], in_=psi.rearrange("(m p) -> m p", p=P))
+        load_x(8, 4)
+        load_v(0, 4)
+        load_x(12, 4)
+        load_v(4, 8)
+
         rt = keep.tile([P, 2, TILES], F32, name="rt")
         inv_psi = keep.tile([P, OUT_TILES], F32, name="inv_psi")
         gain = keep.tile([P, OUT_TILES], F32, name="gain")
 
         x_codes, x_code_scales, codes, code_scales = [], [], [], []
         for s in range(STEPS):
-            x_codes.append(keep.tile([P, 2, HALVES * P], U32, name="x_codes%d" % s, align_bytes=64))
-            x_code_scales.append(keep.tile([P, 2, HALVES * P], U8, name="x_code_scales%d" % s, align_bytes=64))
+            x_codes.append(keep.tile([P, 2, HALVES * P], U32, name="x_codes%d" % s, align_bytes=ALIGN))
+            x_code_scales.append(keep.tile([P, 2, HALVES * P], U8, name="x_code_scales%d" % s, align_bytes=ALIGN))
         for g in range(GROUPS):
-            codes.append(keep.tile([P, WIDE], U32, name="codes%d" % g, align_bytes=64))
-            code_scales.append(keep.tile([P, WIDE], U8, name="code_scales%d" % g, align_bytes=64))
+            codes.append(keep.tile([P, WIDE], U32, name="codes%d" % g, align_bytes=ALIGN))
+            code_scales.append(keep.tile([P, WIDE], U8, name="code_scales%d" % g, align_bytes=ALIGN))
 
-        idle_bank = next_bank([P, K])
+        idle_bank = next_bank("idle", [P, K])
 
         def keep_busy(count):
             for n in range(count):
@@ -138,81 +167,72 @@ def tile_factoranalysisemloadinggradient_w8_kernel(
                     stop=True,
                 )
 
-        def keep_busy_long():
-            nc.tensor.matmul(
-                out=idle_bank[:].rearrange("p (a n) -> p a n", n=P),
-                lhsT=ident[:],
-                rhs=ident[:].unsqueeze(1).to_broadcast([P, K // P, P]),
-                start=True,
-                stop=True,
-            )
-
         spread = {}
 
         def turn_rt():
-            spread["rt"] = next_bank([P, 2, P])
+            spread["rt"] = next_bank("rt", [P, 2, P])
             for u in range(2):
                 nc.tensor.transpose(spread["rt"][:, u, :], rt_rows[:].bitcast(F32)[:, u : 2 * P : 2], ident[:])
-
-        def turn_psi():
-            spread["psi"] = next_bank([P, P], BF16)
-            nc.tensor.transpose(spread["psi"][:], psi_rows[:], ident_bf16[:])
-
-        def invert_psi():
-            nc.vector.reciprocal(out=inv_psi[:], in_=spread["psi"][:, 0:OUT_TILES])
 
         def copy_rt():
             nc.scalar.copy(
                 out=rt[:].rearrange("p w (g u e) -> p u (w g) e", u=2, e=2),
                 in_=spread["rt"][:, :, 0 : 2 * GROUPS].bitcast(BF16).rearrange("p u (k e) -> p u k e", e=2),
             )
+            release("rt")
+
+        def turn_psi():
+            spread["psi"] = next_bank("psi", [P, P], BF16)
+            nc.tensor.transpose(spread["psi"][:], psi_rows[:], ident_bf16[:])
+
+        def invert_psi():
+            nc.vector.reciprocal(out=inv_psi[:], in_=spread["psi"][:, 0:OUT_TILES])
+            release("psi")
+
+        def make_gain():
+            nc.vector.tensor_scalar(out=gain[:], in0=inv_psi[:], scalar1=1.0 / N, scalar2=None, op0=MULT)
 
         words_of, transposed, woven_x = {}, {}, {}
 
-        def widen(i):
+        def widen(i, copy=None):
             tile = widened_pool.tile([P, D], BF16, name="widened")
-            nc.scalar.copy(out=tile[:], in_=x_raw[i].bitcast(FP8))
+            (copy or nc.scalar.copy)(out=tile[:], in_=x_raw[i].bitcast(FP8))
             for j in range(HALVES):
                 for u in range(2):
                     words_of[i, j, u] = tile[:].bitcast(F32)[:, 2 * P * j + u : 2 * P * (j + 1) : 2]
 
-        def widen_sorted(first, lo, hi):
-            tile = widened_pool.tile([P, 2, hi - lo, P, 2], BF16, name="sorted", bufs=4)
+        def widen_sorted(i, lo=0, hi=HALVES):
+            tile = widened_pool.tile([P, 2, hi - lo, P, 2], BF16, name="sorted", bufs=SBUFS)
             nc.vector.tensor_scalar(
                 out=tile[:].rearrange("p u b q e -> p (b q) u e"),
-                in0=x_rows[first][:, lo * HALF : hi * HALF].bitcast(FP8).rearrange("p (q u e) -> p q u e", u=2, e=2),
+                in0=x_raw[i][:, lo * HALF : hi * HALF].bitcast(FP8).rearrange("p (q u e) -> p q u e", u=2, e=2),
                 scalar1=ones[:],
                 scalar2=None,
                 op0=MULT,
             )
-            for b in range(lo, hi):
+            for j in range(lo, hi):
                 for u in range(2):
-                    words_of[first + b // 2, b % 2, u] = tile[:, u, b - lo, :, :].rearrange("p q e -> p (q e)").bitcast(F32)
+                    words_of[i, j, u] = tile[:, u, j - lo, :, :].rearrange("p q e -> p (q e)").bitcast(F32)
 
-        def transpose(i, halves=range(HALVES)):
-            bank = next_bank([P, HALVES, 2, P])
-            for j in halves:
+        def transpose(i, lo=0, hi=HALVES):
+            bank = next_bank(("x", i, hi), [P, 2, HALVES, P])
+            for j in range(lo, hi):
                 transposed[i, j] = bank
                 for u in range(2):
-                    nc.tensor.transpose(bank[:, j, u, :], words_of[i, j, u], ident[:])
+                    nc.tensor.transpose(bank[:, u, j, :], words_of[i, j, u], ident[:])
 
-        def woven_tile(i):
+        def scale_out(i, lo=0, hi=HALVES):
             s, h = divmod(i, 2)
             if s not in woven_x:
-                pool, name = (keep, "woven_gpsimd") if s == 2 else (woven_pool, "woven_x")
-                woven_x[s] = pool.tile([P, 2, HALVES * P * PACK], BF16, name=name, align_bytes=64)
-            return woven_x[s][:, h, :]
-
-        def scale_out(i, halves=range(HALVES)):
-            woven = woven_tile(i)
-            for j in halves:
-                scales = scale_cols[:, j, :].rearrange("p (u e) -> p u e", e=2)
-                nc.vector.tensor_tensor(
-                    out=woven[:, j * P * PACK : (j + 1) * P * PACK].rearrange("p (m u e) -> p m u e", u=2, e=2),
-                    in0=transposed[i, j][:, j, :, :].bitcast(BF16).rearrange("p u (m e) -> p m u e", e=2),
-                    in1=scales.unsqueeze(1).to_broadcast([P, P, 2, 2]),
-                    op=MULT,
-                )
+                woven_x[s] = keep.tile([P, 2, HALVES * P * PACK], BF16, name="woven_x%d" % s, align_bytes=64)
+            nc.vector.tensor_tensor(
+                out=woven_x[s][:, h, lo * P * PACK : hi * P * PACK].rearrange("p (j m u e) -> p j m u e", m=P, u=2, e=2),
+                in0=transposed[i, lo][:, :, lo:hi, :].bitcast(BF16).rearrange("p u j (m e) -> p j m u e", e=2),
+                in1=scale_cols[:, lo:hi, :].rearrange("p j (u e) -> p j u e", e=2).unsqueeze(2).to_broadcast([P, hi - lo, P, 2, 2]),
+                op=MULT,
+            )
+            if ("x", i, hi) in bank_of:
+                release(("x", i, hi))
 
         def quantize_x(i, lo=0, hi=HALVES):
             s, h = divmod(i, 2)
@@ -229,7 +249,10 @@ def tile_factoranalysisemloadinggradient_w8_kernel(
                 in_=woven_x[s][:].rearrange("p h w -> p (h w)"),
             )
 
-        def multiply(bank, i, codes, first, scale_col, width):
+        weights = (beta_codes, p_codes[0], p_codes[1])
+        weight_scales = (beta_rows[:, 0:K], p_rows[:, 0:HALF], p_rows[:, HALF:D])
+
+        def multiply(bank, i, part, first, width):
             s, h = divmod(i, 2)
             for j in range(HALVES):
                 cols = slice(j * P, (j + 1) * P)
@@ -237,51 +260,50 @@ def tile_factoranalysisemloadinggradient_w8_kernel(
                     out=bank,
                     lhsT=x_codes[s][:, h, cols].bitcast(X4),
                     lhsT_scale=x_code_scales[s][:, h, cols],
-                    rhs=codes[:, j, first * PACK : (first + width) * PACK].bitcast(X4),
-                    rhs_scale=w_scales[4 * j : P, scale_col : scale_col + width],
+                    rhs=weights[part][:, j, first * PACK : (first + width) * PACK].bitcast(X4),
+                    rhs_scale=weight_scales[part][4 * j : P, first : first + width],
                     start=(j == 0),
                     stop=(j == HALVES - 1),
                 )
 
         products, planes, woven = {}, {}, {}
-        weights = (beta_codes, p_codes[0], p_codes[1])
 
-        def multiply_wide(part, i):
-            products[part, i] = next_bank([P, K])
-            multiply(products[part, i][:], i, weights[part], 0, (D, 0, HALF)[part], K)
-
-        def scale_wide(part, i):
-            g, c = divmod(i, PACK)
+        def plane(g, lo, hi):
+            part = lo // K
             if (g, part) not in planes:
                 planes[g, part] = keep.tile([P, PACK, K], BF16, name="planes%d_%d" % (g, part))
+            return planes[g, part][:, :, lo - part * K : hi - part * K]
+
+        def multiply_wide(part, i, first=0):
+            products[part, i] = next_bank((part, i), [P, K - first])
+            multiply(products[part, i][:], i, part, first, K - first)
+
+        def scale_wide(part, i, first=0):
+            g, c = slot(i)
             nc.scalar.activation(
-                out=planes[g, part][:, c, :],
+                out=plane(g, part * K + first, (part + 1) * K)[:, c, :],
                 in_=products[part, i][:],
                 func=COPY,
-                scale=rt[:, R if part else T, i : i + 1],
+                scale=rt[:, R if part else T, g * PACK + c : g * PACK + c + 1],
             )
+            release((part, i))
 
-        def wide(i, parts):
-            for part in parts:
-                multiply_wide(part, i)
-                scale_wide(part, i)
+        def wide(part, i, first=0):
+            multiply_wide(part, i, first)
+            scale_wide(part, i, first)
 
-        def weave(g, lo, hi, copy, part=None):
-            if (g, lo) not in woven:
-                woven[g, lo] = keep.tile([P, hi - lo, PACK], BF16, name="woven%d_%d" % (g, lo), align_bytes=64)
-            first, width = (0, hi - lo) if part is None else (part * (hi - lo) // 2, (hi - lo) // 2)
-            col = lo % K + first
+        def weave(g, lo, hi, copy, buffer=None):
+            woven[g, lo] = keep.tile([P, hi - lo, PACK], BF16, name=buffer or "woven%d_%d" % (g, lo), align_bytes=64)
             copy(
-                out=woven[g, lo][:, first : first + width, :].rearrange("p (b n) c -> p b c n", n=4),
-                in_=planes[g, lo // K][:, :, col : col + width].rearrange("p c (b n) -> p b c n", n=4),
+                out=woven[g, lo][:].rearrange("p (b n) c -> p b c n", n=4),
+                in_=plane(g, lo, hi).rearrange("p c (b n) -> p b c n", n=4),
             )
 
-        def weave_gpsimd(g, lo, hi, after=None):
-            name = "woven%d_%d" % after if after else "woven_gpsimd"
-            woven[g, lo] = keep.tile([P, hi - lo, PACK], BF16, name=name, align_bytes=64)
+        def weave_gpsimd(g, lo, hi, buffer):
+            woven[g, lo] = keep.tile([P, hi - lo, PACK], BF16, name=buffer, align_bytes=64)
             nc.gpsimd.tensor_scalar(
                 out=woven[g, lo][:],
-                in0=planes[g, lo // K][:, :, lo % K : lo % K + hi - lo].rearrange("p c n -> p n c"),
+                in0=plane(g, lo, hi).rearrange("p c n -> p n c"),
                 scalar1=1.0,
                 scalar2=0.0,
                 op0=MULT,
@@ -296,27 +318,29 @@ def tile_factoranalysisemloadinggradient_w8_kernel(
                 in_=woven[g, lo][:].rearrange("p n c -> p (n c)"),
             )
 
-        def multiply_narrow(g, chunk):
-            products[g, chunk, "narrow"] = next_bank([P, PACK, P])
+        def multiply_narrow(g, part, chunk):
+            products[g, part, chunk] = next_bank((g, part, chunk), [P, PACK, P])
             for c in range(PACK):
-                multiply(products[g, chunk, "narrow"][:, c, :], g * PACK + c, p_codes[1], P * chunk, HALF + P * chunk, P)
+                multiply(products[g, part, chunk][:, c, :], g * PACK + c, part, P * chunk, P)
 
-        def scale_narrow(g, chunk):
-            if chunk == 0:
-                woven[g, D] = keep.tile([P, HALF, PACK], BF16, name="woven%d_%d" % (g, D), align_bytes=64)
-            factors = rt[:, R, g * PACK : (g + 1) * PACK]
+        def scale_narrow(g, part, chunk, width=K // P):
+            lo = part * K + chunk // width * width * P
+            if chunk % width == 0:
+                woven[g, lo] = keep.tile([P, width * P, PACK], BF16, name="woven%d_%d" % (g, lo), align_bytes=64)
+            factors = rt[:, R if part else T, g * PACK : (g + 1) * PACK]
             nc.vector.tensor_tensor(
-                out=woven[g, D][:, P * chunk : P * (chunk + 1), :],
-                in0=products[g, chunk, "narrow"][:].rearrange("p c n -> p n c"),
+                out=woven[g, lo][:, P * (chunk % width) : P * (chunk % width + 1), :],
+                in0=products[g, part, chunk][:].rearrange("p c n -> p n c"),
                 in1=factors.unsqueeze(1).to_broadcast([P, P, PACK]),
                 op=MULT,
             )
+            release((g, part, chunk))
 
-        sums, added, v_scaled = {}, {}, {}
+        sums, added, v_scaled, differences = {}, {}, {}, {}
 
         def contract(m, groups, lo=0, hi=K):
             if (m, lo) not in sums:
-                sums[m, lo] = next_bank([P, K])
+                sums[m, lo] = next_bank(("c", m, lo), [P, K])
                 added[m, lo] = -1
             cols = slice(K + P * m, K + P * (m + 1))
             for g in groups:
@@ -332,13 +356,13 @@ def tile_factoranalysisemloadinggradient_w8_kernel(
                 )
 
         def scale_v(m):
-            v_scaled[m] = result_pool.tile([P, K], F32, name="v_scaled", bufs=7)
-            nc.scalar.activation(out=v_scaled[m][:], in_=v_in[:, m, :], func=COPY, scale=inv_psi[:, m : m + 1])
+            v_scaled[m] = result_pool.tile([P, K], F32, name="v_scaled", bufs=VBUFS)
+            nc.scalar.activation(out=v_scaled[m][:], in_=v_in[m], func=COPY, scale=inv_psi[:, m : m + 1])
 
-        def scale_v_gpsimd(m, name):
-            v_scaled[m] = keep.tile([P, K], F32, name=name, align_bytes=64)
+        def scale_v_gpsimd(m):
+            v_scaled[m] = keep.tile([P, K], F32, name="v_scaled%d" % m)
             nc.gpsimd.tensor_scalar(
-                out=v_scaled[m][:], in0=v_in[:, m, :], scalar1=inv_psi[:, m : m + 1], scalar2=0.0, op0=MULT, op1=ADD
+                out=v_scaled[m][:], in0=v_in[m], scalar1=inv_psi[:, m : m + 1], scalar2=0.0, op0=MULT, op1=ADD
             )
 
         def finish(m, lo=0, hi=K):
@@ -351,141 +375,169 @@ def tile_factoranalysisemloadinggradient_w8_kernel(
                 op0=MULT,
                 op1=SUBTRACT,
             )
+            release(("c", m, lo))
             nc.sync.dma_start(out=out[P * m : P * (m + 1), lo:hi], in_=result[:, lo:hi])
 
         vector, scalar = nc.vector.tensor_copy, nc.scalar.copy
-
         every = range(GROUPS)
-        keep_busy(2)
-        keep_busy_long()
+        def products_of(pair, parts, first=0):
+            for part in parts:
+                for i in (2 * pair, 2 * pair + 1):
+                    wide(part, i, first if part == 2 else 0)
+
+        keep_busy(4)
         widen_sorted(0, 0, 1)
         widen_sorted(0, 1, 2)
-        widen_sorted(1, 0, 2)
-        for i in range(2, 6):
+        nc.vector.tensor_copy(out=ident_bf16[:], in_=ident[:])
+        for i in (1, 2, 3):
             widen(i)
-        transpose(0, (0,))
-        transpose(0, (1,))
-        keep_busy(1)
+        transpose(0, 0, 1)
+        transpose(0, 1, 2)
+        keep_busy(2)
         transpose(1)
-        keep_busy_long()
-        scale_out(0)
-        transpose(2)
-        transpose(3)
-        keep_busy(1)
-        scale_out(1)
-        quantize_x(0)
-        quantize_x(1)
-        scale_out(2)
-        multiply_wide(0, 0)
-        multiply_wide(0, 1)
+        release("idle")
+        scale_out(0, 0, 1)
+        scale_out(0, 1, 2)
+        quantize_x(0, 0, 1)
+        quantize_x(0, 1, 2)
         turn_rt()
         copy_rt()
-        transpose(4)
-        scale_wide(0, 0)
-        scale_wide(0, 1)
-        scale_out(3, (0,))
+        transpose(2)
+        widen(4)
+        wide(0, 0)
+        scale_out(1)
+        transpose(3)
+        widen(5)
+        wide(1, 0)
+        scale_out(2, 0, 1)
+        quantize_x(1)
+        scale_out(2, 1, 2)
+        wide(0, 1)
+        wide(1, 1)
+        wide(2, 0)
+        wide(2, 1)
+        scale_out(3, 0, 1)
         quantize_x(2)
-        scale_out(3, (1,))
-        transpose(5)
-        wide(0, (1,))
-        wide(1, (1,))
-        scale_out(4, (0,))
+        scale_out(3, 1, 2)
+        widen_sorted(6)
         quantize_x(3)
-        scale_out(4, (1,))
-        wide(2, (0, 1))
-        wide(3, (0, 1))
-        widen_sorted(6, 0, 2)
+        widen_sorted(7)
+        turn_psi()
+        for i in range(4, 8):
+            transpose(i)
+        invert_psi()
+        widen_sorted(8)
+        for m in range(2):
+            scale_v_gpsimd(m)
+        for m in range(2, 4):
+            scale_v(m)
+        scale_out(4)
         scale_out(5)
-        pieces = {2: (0, 0, 256), 3: (0, 256, 512), 4: (1, 0, 256), 5: (1, 256, 512), 6: (2, 0, 512)}
-        for s in range(2, STEPS):
-            a = 2 * s
-            g, h = divmod(s, 2)
-            more = s + 1 < STEPS
-            if s == 2:
-                turn_psi()
-            if more:
-                widen_sorted(a + 3, 0, 2)
-                transpose(a + 2)
-                transpose(a + 3)
-            quantize_x_pair(s)
-            if s == 2:
-                invert_psi()
-            if s == 3:
-                nc.vector.tensor_scalar(out=gain[:], in0=inv_psi[:], scalar1=1.0 / N, scalar2=None, op0=MULT)
-            if s == 7:
-                quantize(0, K)
-                quantize(1, K)
-                quantize(2, 0)
-                weave_gpsimd(2, K, D)
-            if 2 < s < 7:
-                quantize(*pieces[s - 1][0:2])
-            if s < 7:
-                weave_gpsimd(*pieces[s])
-            if s + 2 < STEPS:
-                widen_sorted(a + 4, 0, 2)
-            if s == 2:
-                weave(0, K, D, scalar, 0)
-            if g in (1, 2):
-                for part in (0, 1, 2):
-                    wide(a, (part,))
-                    wide(a + 1, (part,))
-                    if part == 0 and s > 2:
-                        weave(g - 1, K, D, scalar, h)
-            else:
-                multiply_narrow(0, 2 * h)
-                multiply_narrow(0, 2 * h + 1)
-                for part in (0, 1):
-                    if s == 6 and part == 1:
-                        weave(2, D, D + 256, scalar)
-                    if s == 7 and part == 1:
-                        scale_v(0)
-                        weave(3, 0, K, scalar)
-                        for chunk in range(4):
-                            multiply_narrow(3, chunk)
-                    wide(a, (part,))
-                    wide(a + 1, (part,))
-            if more:
-                scale_out(a + 2)
-                scale_out(a + 3)
-            if g == 3:
-                scale_narrow(0, 2 * h)
-                scale_narrow(0, 2 * h + 1)
+        products_of(1, (0,))
+        make_gain()
+        quantize_x_pair(2)
+        weave_gpsimd(0, 0, 384, "woven_x2")
+        widen_sorted(9)
+        products_of(1, (1, 2))
+        products_of(2, (0,))
+        scale_out(6)
+        scale_out(7)
+        products_of(2, (1, 2))
+        widen_sorted(10)
+        quantize_x_pair(3)
+        weave_gpsimd(0, 512, 896, "woven_x3")
+        widen_sorted(11)
+        quantize(0, 0)
+        for i in range(8, 12):
+            transpose(i)
+        scale_out(8)
+        scale_out(9)
+        weave(0, 384, 512, scalar)
+        weave(0, 896, 1024, scalar)
+        products_of(3, (0,))
+        widen_sorted(12)
+        quantize_x_pair(4)
+        weave_gpsimd(1, 0, 384, "woven_x4")
+        widen_sorted(13)
+        products_of(3, (1, 2))
+        products_of(4, (0,))
+        scale_out(10)
+        scale_out(11)
+        products_of(4, (1, 2), 256)
+        widen_sorted(14)
+        quantize_x_pair(5)
+        weave_gpsimd(1, 512, 896, "woven_x5")
+        widen_sorted(15)
+        for i in range(12, 16):
+            transpose(i)
+        scale_out(12)
+        scale_out(13)
+        weave(1, 384, 512, scalar)
+        weave(1, 896, 1024, scalar)
+        products_of(5, (0,))
+        quantize(0, 384)
+        quantize(0, 896)
+        quantize_x_pair(6)
+        weave_gpsimd(2, 0, 384, "woven_x6")
+        quantize(0, 512)
+        products_of(5, (1, 2), 256)
+        products_of(6, (0,))
+        scale_out(14)
+        scale_out(15)
+        products_of(6, (1,))
+        quantize(1, 0)
+        quantize_x_pair(7)
+        for chunk in range(2):
+            multiply_narrow(2, 2, chunk)
+        weave(2, 384, 512, scalar)
+        weave(2, 896, 1024, scalar)
+        quantize(1, 512)
+        quantize(1, 384)
+        quantize(1, 896)
+        weave(1, 1024, 1280, vector)
+        products_of(7, (0, 1))
+        quantize(2, 0)
+        weave_gpsimd(2, 512, 896, "woven_x6")
+        weave_gpsimd(3, 0, 256, "woven_x7")
+        quantize(2, 384)
+        quantize(2, 896)
+        quantize(1, 1024)
+        for chunk in range(2):
+            scale_narrow(2, 2, chunk, 2)
         for chunk in range(4):
-            scale_narrow(3, chunk)
-        weave(3, K, K + 256, scalar)
-        weave(1, D, D + 256, scalar)
-        scale_v(1)
-        quantize(2, K)
-        quantize(0, D)
-        quantize(3, 0)
-        weave(3, K + 256, D, vector)
+            multiply_narrow(3, 2, chunk)
+            scale_narrow(3, 2, chunk)
+        weave(3, 256, 512, scalar)
+        weave(3, 512, 768, scalar)
+        weave(3, 768, 1024, scalar)
+        quantize(2, 512)
         for g in range(3):
             for m in range(4):
                 contract(m, (g,))
-        scale_v(2)
-        scale_v(3)
-        weave(2, D + 256, WIDE, scalar)
-        quantize(3, D)
-        quantize(3, K)
-        quantize(3, K + 256)
-        quantize(2, D)
-        quantize(1, D)
+        quantize(3, 0)
+        quantize(3, 256)
+        quantize(3, 512)
+        quantize(2, 1024)
+        quantize(3, 768)
+        quantize(3, 1024)
+        weave(0, 1024, 1280, scalar, "woven_x0")
         for m in range(4):
             contract(m, (3,))
-        weave_gpsimd(1, D + 256, WIDE, (1, D))
-        for m in (4, 5, 6):
+        quantize(0, 1024)
+        weave_gpsimd(1, 1280, 1536, "woven_x0")
+        weave(0, 1280, 1536, scalar, "woven_x1")
+        weave(2, 1280, 1536, scalar, "woven_x2")
+        for m in range(4, 8):
             scale_v(m)
-        finish(0)
-        finish(1)
-        contract(4, (0, 3, 2, 1))
-        finish(2)
-        finish(3)
-        contract(5, every)
-        quantize(1, D + 256)
-        quantize(2, D + 256)
-        scale_v_gpsimd(7, "woven%d_%d" % (2, D + 256))
+        for m in range(4):
+            finish(m)
+        contract(4, (3, 2, 1, 0))
+        contract(5, (3, 2, 1, 0))
+        quantize(1, 1280)
+        quantize(0, 1280)
+        quantize(2, 1280)
         finish(4)
-        contract(6, (0, 3, 1, 2))
+        contract(6, (3, 1, 0, 2))
         finish(5)
         contract(7, every, 0, 256)
         finish(6)

@@ -34,8 +34,10 @@ R, T = 0, 1
 ALIGN = 64
 VBUFS = 6
 RBUFS = 6
-SBUFS = 5
+SBUFS = 4
 WBUFS = 4
+GW = 352
+ZW = 256
 
 
 def tile_factoranalysisemloadinggradient_w8_kernel(
@@ -62,12 +64,12 @@ def tile_factoranalysisemloadinggradient_w8_kernel(
         beta_rows = keep.tile([P, K], U8, name="beta_rows", align_bytes=64)
         p_rows = keep.tile([P, D], U8, name="p_rows", align_bytes=64)
         nc.vector.memset(beta_rows[:].bitcast(I32), 0)
-        nc.vector.memset(p_rows[:].bitcast(I32), 0)
         ones = keep.tile([P, 1], F32, name="ones")
         nc.vector.memset(ones[:], 1.0)
 
-        zeros = keep.tile([P, P], BF16, name="zeros")
-        nc.gpsimd.memset(zeros[:], 0.0)
+        zeros = keep.tile([P, P], F32, name="zeros")
+        nc.vector.memset(zeros[:], 0.0)
+        nc.vector.memset(p_rows[:].bitcast(I32), 0)
         ident = keep.tile([P, P], F32, name="ident")
         make_identity(nc, ident[:])
 
@@ -83,7 +85,7 @@ def tile_factoranalysisemloadinggradient_w8_kernel(
             return g, (n + 2) % PACK if g == 1 else n
 
         x_cases = x_bytes.rearrange("(g m c) k -> g m c k", m=P, c=PACK)
-        x_raw = {}
+        x_raw, x_rows = {}, {}
 
         def load_x(first, count):
             g, c = slot(first)
@@ -91,6 +93,7 @@ def tile_factoranalysisemloadinggradient_w8_kernel(
             nc.sync.dma_start(out=raw[:], in_=x_cases[g][:, c : c + count, :])
             for n in range(count):
                 x_raw[first + n] = raw[:, n, :]
+                x_rows[first + n] = raw[:, n:count, :].rearrange("p c k -> p (c k)")
 
         def load_x_2_to_5():
             raw = keep.tile([P, 2, 2 * D], U8, name="x_raw2")
@@ -98,6 +101,7 @@ def tile_factoranalysisemloadinggradient_w8_kernel(
             nc.sync.dma_start(out=raw[:], in_=rows[:, 0:2, 1, :])
             for n in range(4):
                 x_raw[2 + n] = raw[:, n // 2, n % 2 * D : (n % 2 + 1) * D]
+                x_rows[2 + n] = x_raw[2 + n]
 
         scale_cols = keep.tile([P, HALVES, PACK], F32, name="scale_cols")
         beta_codes = keep.tile([P, HALVES, K * PACK], U8, name="beta_codes", align_bytes=ALIGN)
@@ -131,15 +135,15 @@ def tile_factoranalysisemloadinggradient_w8_kernel(
         load_x_2_to_5()
         load_scales(beta_rows, beta_scales)
         nc.sync.dma_start(out=beta_codes[:], in_=beta_words.rearrange("g p n c -> p g (n c)"))
-        load_row_factor(T, t)
-        load_row_factor(R, r)
         load_p(0)
         load_scales(p_rows, p_scales)
+        load_row_factor(T, t)
+        load_row_factor(R, r)
         load_x(6, 2)
-        load_p(1)
         nc.sync.dma_start(out=psi_rows[0:OUT_TILES, :], in_=psi.rearrange("(m p) -> m p", p=P))
         load_x(8, 4)
         load_v(0, 4)
+        load_p(1)
         load_x(12, 4)
         load_v(4, 8)
 
@@ -155,14 +159,14 @@ def tile_factoranalysisemloadinggradient_w8_kernel(
             codes.append(keep.tile([P, WIDE], U32, name="codes%d" % g, align_bytes=ALIGN))
             code_scales.append(keep.tile([P, WIDE], U8, name="code_scales%d" % g, align_bytes=ALIGN))
 
-        idle_bank = next_bank("idle", [P, K])
+        idle_bank = next_bank("idle", [P, 2 * P])
 
-        def keep_busy(count):
+        def keep_busy(count, width=P):
             for n in range(count):
                 nc.tensor.matmul(
-                    out=idle_bank[:].rearrange("p (a n) -> p a n", n=P),
+                    out=idle_bank[:, 0 : 2 * width].rearrange("p (a n) -> p a n", a=2),
                     lhsT=zeros[:],
-                    rhs=zeros[:].unsqueeze(1).to_broadcast([P, K // P, P]),
+                    rhs=zeros[:, 0:width].unsqueeze(1).to_broadcast([P, 2, width]),
                     start=True,
                     stop=True,
                 )
@@ -205,14 +209,14 @@ def tile_factoranalysisemloadinggradient_w8_kernel(
             tile = widened_pool.tile([P, 2, hi - lo, P, 2], BF16, name="sorted", bufs=SBUFS)
             nc.vector.tensor_scalar(
                 out=tile[:].rearrange("p u b q e -> p (b q) u e"),
-                in0=x_raw[i][:, lo * HALF : hi * HALF].bitcast(FP8).rearrange("p (q u e) -> p q u e", u=2, e=2),
+                in0=x_rows[i][:, lo * HALF : hi * HALF].bitcast(FP8).rearrange("p (q u e) -> p q u e", u=2, e=2),
                 scalar1=ones[:],
                 scalar2=None,
                 op0=MULT,
             )
-            for j in range(lo, hi):
+            for b in range(lo, hi):
                 for u in range(2):
-                    words_of[i, j, u] = tile[:, u, j - lo, :, :].rearrange("p q e -> p (q e)").bitcast(F32)
+                    words_of[i + b // HALVES, b % HALVES, u] = tile[:, u, b - lo, :, :].rearrange("p q e -> p (q e)").bitcast(F32)
 
         def transpose(i, lo=0, hi=HALVES):
             bank = next_bank(("x", i, hi), [P, 2, HALVES, P])
@@ -240,13 +244,6 @@ def tile_factoranalysisemloadinggradient_w8_kernel(
                 out=x_codes[s][:, h, lo * P : hi * P].bitcast(X4),
                 scales=x_code_scales[s][:, h, lo * P : hi * P],
                 in_=woven_x[s][:, h, lo * P * PACK : hi * P * PACK],
-            )
-
-        def quantize_x_pair(s):
-            nc.vector.quantize_mx(
-                out=x_codes[s][:].rearrange("p h w -> p (h w)").bitcast(X4),
-                scales=x_code_scales[s][:].rearrange("p h w -> p (h w)"),
-                in_=woven_x[s][:].rearrange("p h w -> p (h w)"),
             )
 
         weights = (beta_codes, p_codes[0], p_codes[1])
@@ -292,17 +289,22 @@ def tile_factoranalysisemloadinggradient_w8_kernel(
             multiply_wide(part, i, first)
             scale_wide(part, i, first)
 
-        def weave(g, lo, hi, copy, buffer=None):
+        def new_woven(g, lo, hi, buffer=None):
             woven[g, lo] = keep.tile([P, hi - lo, PACK], BF16, name=buffer or "woven%d_%d" % (g, lo), align_bytes=64)
+
+        def woven_columns(g, lo, hi):
+            first = max(n for (h, n) in woven if h == g and n <= lo)
+            return woven[g, first][:, lo - first : hi - first, :]
+
+        def weave(g, lo, hi, copy):
             copy(
-                out=woven[g, lo][:].rearrange("p (b n) c -> p b c n", n=4),
+                out=woven_columns(g, lo, hi).rearrange("p (b n) c -> p b c n", n=4),
                 in_=plane(g, lo, hi).rearrange("p c (b n) -> p b c n", n=4),
             )
 
-        def weave_gpsimd(g, lo, hi, buffer):
-            woven[g, lo] = keep.tile([P, hi - lo, PACK], BF16, name=buffer, align_bytes=64)
+        def weave_gpsimd(g, lo, hi):
             nc.gpsimd.tensor_scalar(
-                out=woven[g, lo][:],
+                out=woven_columns(g, lo, hi),
                 in0=plane(g, lo, hi).rearrange("p c n -> p n c"),
                 scalar1=1.0,
                 scalar2=0.0,
@@ -385,148 +387,161 @@ def tile_factoranalysisemloadinggradient_w8_kernel(
                 for i in (2 * pair, 2 * pair + 1):
                     wide(part, i, first if part == 2 else 0)
 
-        keep_busy(4)
+        def shared_weave(g, part, buffer):
+            new_woven(g, part * K, (part + 1) * K, buffer)
+            weave_gpsimd(g, part * K, part * K + GW)
+
+        def rest_weave(g, part):
+            weave(g, part * K + GW, (part + 1) * K, scalar)
+
+        def weave_alone(g, lo, hi, copy, buffer=None):
+            new_woven(g, lo, hi, buffer)
+            weave(g, lo, hi, copy)
+
+        keep_busy(2)
         widen_sorted(0, 0, 1)
         widen_sorted(0, 1, 2)
         nc.vector.tensor_copy(out=ident_bf16[:], in_=ident[:])
-        for i in (1, 2, 3):
+        for i in (1, 2, 3, 4):
             widen(i)
         transpose(0, 0, 1)
         transpose(0, 1, 2)
-        keep_busy(2)
+        keep_busy(1)
         transpose(1)
+        keep_busy(1, 96)
         release("idle")
         scale_out(0, 0, 1)
         scale_out(0, 1, 2)
         quantize_x(0, 0, 1)
         quantize_x(0, 1, 2)
-        turn_rt()
-        copy_rt()
         transpose(2)
-        widen(4)
-        wide(0, 0)
+        multiply_wide(0, 0)
         scale_out(1)
         transpose(3)
-        widen(5)
-        wide(1, 0)
+        turn_rt()
+        multiply_wide(1, 0)
+        copy_rt()
+        scale_wide(0, 0)
+        scale_wide(1, 0)
         scale_out(2, 0, 1)
         quantize_x(1)
         scale_out(2, 1, 2)
         wide(0, 1)
         wide(1, 1)
-        wide(2, 0)
-        wide(2, 1)
         scale_out(3, 0, 1)
         quantize_x(2)
         scale_out(3, 1, 2)
-        widen_sorted(6)
+        wide(0, 2)
+        wide(1, 2)
+        widen_sorted(5)
         quantize_x(3)
-        widen_sorted(7)
+        widen_sorted(6, 0, 4)
         turn_psi()
-        for i in range(4, 8):
+        for i in (4, 5):
             transpose(i)
         invert_psi()
-        widen_sorted(8)
+        widen_sorted(8, 0, 4)
         for m in range(2):
             scale_v_gpsimd(m)
         for m in range(2, 4):
             scale_v(m)
         scale_out(4)
         scale_out(5)
-        products_of(1, (0,))
-        make_gain()
-        quantize_x_pair(2)
-        weave_gpsimd(0, 0, 384, "woven_x2")
-        widen_sorted(9)
-        products_of(1, (1, 2))
+        wide(0, 3)
+        wide(1, 3)
+        for i in (6, 7):
+            transpose(i)
+        quantize_x(4)
+        quantize_x(5)
+        shared_weave(0, 0, "woven_x2")
+        widen_sorted(10, 0, 4)
+        for i in range(4):
+            wide(2, i)
         products_of(2, (0,))
         scale_out(6)
         scale_out(7)
         products_of(2, (1, 2))
-        widen_sorted(10)
-        quantize_x_pair(3)
-        weave_gpsimd(0, 512, 896, "woven_x3")
-        widen_sorted(11)
-        quantize(0, 0)
+        make_gain()
+        quantize_x(6)
+        quantize_x(7)
+        shared_weave(0, 1, "woven_x3")
+        widen_sorted(12, 0, 4)
         for i in range(8, 12):
             transpose(i)
         scale_out(8)
         scale_out(9)
-        weave(0, 384, 512, scalar)
-        weave(0, 896, 1024, scalar)
+        rest_weave(0, 0)
+        rest_weave(0, 1)
         products_of(3, (0,))
-        widen_sorted(12)
-        quantize_x_pair(4)
-        weave_gpsimd(1, 0, 384, "woven_x4")
-        widen_sorted(13)
+        quantize_x(8)
+        quantize_x(9)
+        shared_weave(1, 0, "woven_x4")
+        widen_sorted(14, 0, 4)
         products_of(3, (1, 2))
         products_of(4, (0,))
         scale_out(10)
         scale_out(11)
         products_of(4, (1, 2), 256)
-        widen_sorted(14)
-        quantize_x_pair(5)
-        weave_gpsimd(1, 512, 896, "woven_x5")
-        widen_sorted(15)
+        quantize_x(10)
+        quantize_x(11)
+        shared_weave(1, 1, "woven_x5")
+        quantize(0, 0)
+        quantize(0, 512)
         for i in range(12, 16):
             transpose(i)
         scale_out(12)
         scale_out(13)
-        weave(1, 384, 512, scalar)
-        weave(1, 896, 1024, scalar)
+        rest_weave(1, 0)
+        rest_weave(1, 1)
         products_of(5, (0,))
-        quantize(0, 384)
-        quantize(0, 896)
-        quantize_x_pair(6)
-        weave_gpsimd(2, 0, 384, "woven_x6")
-        quantize(0, 512)
+        quantize_x(12)
+        quantize_x(13)
+        shared_weave(2, 0, "woven_x6")
+        weave_alone(1, 1024, 1280, vector)
+        quantize(1, 0)
         products_of(5, (1, 2), 256)
         products_of(6, (0,))
         scale_out(14)
         scale_out(15)
         products_of(6, (1,))
-        quantize(1, 0)
-        quantize_x_pair(7)
+        quantize_x(14)
+        quantize_x(15)
         for chunk in range(2):
             multiply_narrow(2, 2, chunk)
-        weave(2, 384, 512, scalar)
-        weave(2, 896, 1024, scalar)
+        rest_weave(2, 0)
         quantize(1, 512)
-        quantize(1, 384)
-        quantize(1, 896)
-        weave(1, 1024, 1280, vector)
-        products_of(7, (0, 1))
-        quantize(2, 0)
-        weave_gpsimd(2, 512, 896, "woven_x6")
-        weave_gpsimd(3, 0, 256, "woven_x7")
-        quantize(2, 384)
-        quantize(2, 896)
+        shared_weave(2, 1, "woven_x5")
+        rest_weave(2, 1)
         quantize(1, 1024)
+        quantize(2, 0)
+        products_of(7, (0, 1))
+        new_woven(3, 0, 512, "woven_x7")
+        weave_gpsimd(3, 0, ZW)
         for chunk in range(2):
             scale_narrow(2, 2, chunk, 2)
         for chunk in range(4):
             multiply_narrow(3, 2, chunk)
             scale_narrow(3, 2, chunk)
-        weave(3, 256, 512, scalar)
-        weave(3, 512, 768, scalar)
-        weave(3, 768, 1024, scalar)
+        weave(3, ZW, 512, scalar)
+        weave_alone(3, 512, 768, scalar)
+        weave_alone(3, 768, 1024, scalar)
         quantize(2, 512)
         for g in range(3):
             for m in range(4):
                 contract(m, (g,))
         quantize(3, 0)
-        quantize(3, 256)
         quantize(3, 512)
         quantize(2, 1024)
         quantize(3, 768)
-        quantize(3, 1024)
-        weave(0, 1024, 1280, scalar, "woven_x0")
+        weave_alone(0, 1024, 1280, scalar, "woven_x0")
         for m in range(4):
             contract(m, (3,))
         quantize(0, 1024)
-        weave_gpsimd(1, 1280, 1536, "woven_x0")
-        weave(0, 1280, 1536, scalar, "woven_x1")
-        weave(2, 1280, 1536, scalar, "woven_x2")
+        new_woven(1, 1280, 1536, "woven_x0")
+        weave_gpsimd(1, 1280, 1536)
+        quantize(3, 1024)
+        weave_alone(0, 1280, 1536, scalar, "woven_x1")
+        weave_alone(2, 1280, 1536, scalar, "woven_x2")
         for m in range(4, 8):
             scale_v(m)
         for m in range(4):

@@ -132,11 +132,11 @@ def tile_factoranalysisemloadinggradient_w8_kernel(
 
         load_x(0, 2)
         nc.scalar.dma_start(out=scale_cols[:], in_=x_scale.rearrange("o (j p c) -> p (o j) c", p=P, c=PACK))
-        load_x_2_to_5()
         load_scales(beta_rows, beta_scales)
+        load_x_2_to_5()
         nc.sync.dma_start(out=beta_codes[:], in_=beta_words.rearrange("g p n c -> p g (n c)"))
-        load_p(0)
         load_scales(p_rows, p_scales)
+        load_p(0)
         load_row_factor(T, t)
         load_row_factor(R, r)
         load_x(6, 2)
@@ -484,8 +484,8 @@ def tile_factoranalysisemloadinggradient_w8_kernel(
         products_of(4, (1, 2), 256)
         quantize_x(10)
         quantize_x(11)
-        shared_weave(1, 1, "woven_x5")
         quantize(0, 0)
+        shared_weave(1, 1, "woven_x2")
         quantize(0, 512)
         for i in range(12, 16):
             transpose(i)
@@ -496,9 +496,9 @@ def tile_factoranalysisemloadinggradient_w8_kernel(
         products_of(5, (0,))
         quantize_x(12)
         quantize_x(13)
-        shared_weave(2, 0, "woven_x6")
-        weave_alone(1, 1024, 1280, vector)
         quantize(1, 0)
+        shared_weave(2, 0, "woven_x4")
+        weave_alone(1, 1024, 1280, vector)
         products_of(5, (1, 2), 256)
         products_of(6, (0,))
         scale_out(14)
@@ -510,10 +510,9 @@ def tile_factoranalysisemloadinggradient_w8_kernel(
             multiply_narrow(2, 2, chunk)
         rest_weave(2, 0)
         quantize(1, 512)
-        shared_weave(2, 1, "woven_x5")
+        shared_weave(2, 1, "woven_x2")
         rest_weave(2, 1)
         quantize(1, 1024)
-        quantize(2, 0)
         products_of(7, (0, 1))
         new_woven(3, 0, 512, "woven_x7")
         weave_gpsimd(3, 0, ZW)
@@ -525,6 +524,7 @@ def tile_factoranalysisemloadinggradient_w8_kernel(
         weave(3, ZW, 512, scalar)
         weave_alone(3, 512, 768, scalar)
         weave_alone(3, 768, 1024, scalar)
+        quantize(2, 0)
         quantize(2, 512)
         for g in range(3):
             for m in range(4):
@@ -541,7 +541,7 @@ def tile_factoranalysisemloadinggradient_w8_kernel(
         weave_gpsimd(1, 1280, 1536)
         quantize(3, 1024)
         weave_alone(0, 1280, 1536, scalar, "woven_x1")
-        weave_alone(2, 1280, 1536, scalar, "woven_x2")
+        weave_alone(2, 1280, 1536, scalar, "woven_x3")
         for m in range(4, 8):
             scale_v(m)
         for m in range(4):

@@ -135,10 +135,10 @@ def tile_factoranalysisemloadinggradient_w8_kernel(
         load_scales(beta_rows, beta_scales)
         load_x_2_to_5()
         nc.sync.dma_start(out=beta_codes[:], in_=beta_words.rearrange("g p n c -> p g (n c)"))
-        load_scales(p_rows, p_scales)
-        load_p(0)
         load_row_factor(T, t)
         load_row_factor(R, r)
+        load_scales(p_rows, p_scales)
+        load_p(0)
         load_x(6, 2)
         nc.sync.dma_start(out=psi_rows[0:OUT_TILES, :], in_=psi.rearrange("(m p) -> m p", p=P))
         load_x(8, 4)
@@ -398,11 +398,11 @@ def tile_factoranalysisemloadinggradient_w8_kernel(
             new_woven(g, lo, hi, buffer)
             weave(g, lo, hi, copy)
 
-        keep_busy(2)
+        keep_busy(3)
         widen_sorted(0, 0, 1)
         widen_sorted(0, 1, 2)
         nc.vector.tensor_copy(out=ident_bf16[:], in_=ident[:])
-        for i in (1, 2, 3, 4):
+        for i in (1, 2, 3):
             widen(i)
         transpose(0, 0, 1)
         transpose(0, 1, 2)
@@ -415,18 +415,17 @@ def tile_factoranalysisemloadinggradient_w8_kernel(
         quantize_x(0, 0, 1)
         quantize_x(0, 1, 2)
         transpose(2)
-        multiply_wide(0, 0)
+        turn_rt()
+        copy_rt()
+        widen(4)
+        wide(0, 0)
         scale_out(1)
         transpose(3)
-        turn_rt()
-        multiply_wide(1, 0)
-        copy_rt()
-        scale_wide(0, 0)
-        scale_wide(1, 0)
         scale_out(2, 0, 1)
         quantize_x(1)
         scale_out(2, 1, 2)
         wide(0, 1)
+        wide(1, 0)
         wide(1, 1)
         scale_out(3, 0, 1)
         quantize_x(2)
@@ -437,8 +436,8 @@ def tile_factoranalysisemloadinggradient_w8_kernel(
         quantize_x(3)
         widen_sorted(6, 0, 4)
         turn_psi()
-        for i in (4, 5):
-            transpose(i)
+        transpose(4)
+        transpose(5)
         invert_psi()
         widen_sorted(8, 0, 4)
         for m in range(2):
@@ -449,8 +448,8 @@ def tile_factoranalysisemloadinggradient_w8_kernel(
         scale_out(5)
         wide(0, 3)
         wide(1, 3)
-        for i in (6, 7):
-            transpose(i)
+        transpose(6)
+        transpose(7)
         quantize_x(4)
         quantize_x(5)
         shared_weave(0, 0, "woven_x2")
@@ -466,18 +465,20 @@ def tile_factoranalysisemloadinggradient_w8_kernel(
         quantize_x(7)
         shared_weave(0, 1, "woven_x3")
         widen_sorted(12, 0, 4)
-        for i in range(8, 12):
-            transpose(i)
+        transpose(8)
+        transpose(9)
         scale_out(8)
         scale_out(9)
         rest_weave(0, 0)
-        rest_weave(0, 1)
         products_of(3, (0,))
         quantize_x(8)
         quantize_x(9)
         shared_weave(1, 0, "woven_x4")
         widen_sorted(14, 0, 4)
         products_of(3, (1, 2))
+        transpose(10)
+        transpose(11)
+        rest_weave(0, 1)
         products_of(4, (0,))
         scale_out(10)
         scale_out(11)
@@ -487,12 +488,11 @@ def tile_factoranalysisemloadinggradient_w8_kernel(
         quantize(0, 0)
         shared_weave(1, 1, "woven_x2")
         quantize(0, 512)
-        for i in range(12, 16):
-            transpose(i)
+        transpose(12)
+        transpose(13)
         scale_out(12)
         scale_out(13)
         rest_weave(1, 0)
-        rest_weave(1, 1)
         products_of(5, (0,))
         quantize_x(12)
         quantize_x(13)
@@ -500,6 +500,9 @@ def tile_factoranalysisemloadinggradient_w8_kernel(
         shared_weave(2, 0, "woven_x4")
         weave_alone(1, 1024, 1280, vector)
         products_of(5, (1, 2), 256)
+        transpose(14)
+        transpose(15)
+        rest_weave(1, 1)
         products_of(6, (0,))
         scale_out(14)
         scale_out(15)

@@ -31,7 +31,7 @@ BANKS = 8
 
 WIDE = K + D
 R, T = 0, 1
-ALIGN = 64
+ALIGN = 256
 VBUFS = 6
 RBUFS = 6
 SBUFS = 4
@@ -61,14 +61,14 @@ def tile_factoranalysisemloadinggradient_w8_kernel(
         def release(key):
             free_banks.append(bank_of[key])
 
-        beta_rows = keep.tile([P, K], U8, name="beta_rows", align_bytes=64)
-        p_rows = keep.tile([P, D], U8, name="p_rows", align_bytes=64)
+        beta_rows = keep.tile([P, K], U8, name="beta_rows", align_bytes=ALIGN)
+        p_rows = keep.tile([P, D], U8, name="p_rows", align_bytes=ALIGN)
+        zeros = keep.tile([P, P], F32, name="zeros")
+        nc.vector.memset(zeros[:], 0.0)
         nc.vector.memset(beta_rows[:].bitcast(I32), 0)
         ones = keep.tile([P, 1], F32, name="ones")
         nc.vector.memset(ones[:], 1.0)
 
-        zeros = keep.tile([P, P], F32, name="zeros")
-        nc.vector.memset(zeros[:], 0.0)
         nc.vector.memset(p_rows[:].bitcast(I32), 0)
         ident = keep.tile([P, P], F32, name="ident")
         make_identity(nc, ident[:])
@@ -159,14 +159,14 @@ def tile_factoranalysisemloadinggradient_w8_kernel(
             codes.append(keep.tile([P, WIDE], U32, name="codes%d" % g, align_bytes=ALIGN))
             code_scales.append(keep.tile([P, WIDE], U8, name="code_scales%d" % g, align_bytes=ALIGN))
 
-        idle_bank = next_bank("idle", [P, 2 * P])
+        idle_bank = next_bank("idle", [P, 3 * P])
 
-        def keep_busy(count, width=P):
+        def keep_busy(count, width=P, blocks=2):
             for n in range(count):
                 nc.tensor.matmul(
-                    out=idle_bank[:, 0 : 2 * width].rearrange("p (a n) -> p a n", a=2),
+                    out=idle_bank[:, 0 : blocks * width].rearrange("p (a n) -> p a n", a=blocks),
                     lhsT=zeros[:],
-                    rhs=zeros[:, 0:width].unsqueeze(1).to_broadcast([P, 2, width]),
+                    rhs=zeros[:, 0:width].unsqueeze(1).to_broadcast([P, blocks, width]),
                     start=True,
                     stop=True,
                 )
@@ -398,7 +398,8 @@ def tile_factoranalysisemloadinggradient_w8_kernel(
             new_woven(g, lo, hi, buffer)
             weave(g, lo, hi, copy)
 
-        keep_busy(3)
+        keep_busy(1)
+        keep_busy(1, P, 3)
         widen_sorted(0, 0, 1)
         widen_sorted(0, 1, 2)
         nc.vector.tensor_copy(out=ident_bf16[:], in_=ident[:])
@@ -406,9 +407,9 @@ def tile_factoranalysisemloadinggradient_w8_kernel(
             widen(i)
         transpose(0, 0, 1)
         transpose(0, 1, 2)
-        keep_busy(1)
-        transpose(1)
         keep_busy(1, 96)
+        transpose(1)
+        keep_busy(1)
         release("idle")
         scale_out(0, 0, 1)
         scale_out(0, 1, 2)
@@ -419,6 +420,7 @@ def tile_factoranalysisemloadinggradient_w8_kernel(
         copy_rt()
         widen(4)
         wide(0, 0)
+        widen(5)
         scale_out(1)
         transpose(3)
         scale_out(2, 0, 1)
@@ -432,7 +434,6 @@ def tile_factoranalysisemloadinggradient_w8_kernel(
         scale_out(3, 1, 2)
         wide(0, 2)
         wide(1, 2)
-        widen_sorted(5)
         quantize_x(3)
         widen_sorted(6, 0, 4)
         turn_psi()
@@ -465,44 +466,39 @@ def tile_factoranalysisemloadinggradient_w8_kernel(
         quantize_x(7)
         shared_weave(0, 1, "woven_x3")
         widen_sorted(12, 0, 4)
-        transpose(8)
-        transpose(9)
+        for i in range(8, 12):
+            transpose(i)
         scale_out(8)
         scale_out(9)
         rest_weave(0, 0)
+        rest_weave(0, 1)
         products_of(3, (0,))
         quantize_x(8)
         quantize_x(9)
         shared_weave(1, 0, "woven_x4")
         widen_sorted(14, 0, 4)
         products_of(3, (1, 2))
-        transpose(10)
-        transpose(11)
-        rest_weave(0, 1)
         products_of(4, (0,))
         scale_out(10)
         scale_out(11)
         products_of(4, (1, 2), 256)
+        quantize(0, 512)
         quantize_x(10)
         quantize_x(11)
+        shared_weave(1, 1, "woven_x5")
         quantize(0, 0)
-        shared_weave(1, 1, "woven_x2")
-        quantize(0, 512)
-        transpose(12)
-        transpose(13)
+        for i in range(12, 16):
+            transpose(i)
         scale_out(12)
         scale_out(13)
         rest_weave(1, 0)
+        rest_weave(1, 1)
         products_of(5, (0,))
         quantize_x(12)
         quantize_x(13)
+        shared_weave(2, 0, "woven_x6")
         quantize(1, 0)
-        shared_weave(2, 0, "woven_x4")
-        weave_alone(1, 1024, 1280, vector)
         products_of(5, (1, 2), 256)
-        transpose(14)
-        transpose(15)
-        rest_weave(1, 1)
         products_of(6, (0,))
         scale_out(14)
         scale_out(15)
@@ -513,10 +509,13 @@ def tile_factoranalysisemloadinggradient_w8_kernel(
             multiply_narrow(2, 2, chunk)
         rest_weave(2, 0)
         quantize(1, 512)
-        shared_weave(2, 1, "woven_x2")
-        rest_weave(2, 1)
+        weave_alone(1, 1024, 1280, vector)
+        weave_alone(0, 1024, 1280, vector)
+        quantize(2, 0)
+        shared_weave(2, 1, "woven_x6")
         quantize(1, 1024)
         products_of(7, (0, 1))
+        rest_weave(2, 1)
         new_woven(3, 0, 512, "woven_x7")
         weave_gpsimd(3, 0, ZW)
         for chunk in range(2):
@@ -527,7 +526,6 @@ def tile_factoranalysisemloadinggradient_w8_kernel(
         weave(3, ZW, 512, scalar)
         weave_alone(3, 512, 768, scalar)
         weave_alone(3, 768, 1024, scalar)
-        quantize(2, 0)
         quantize(2, 512)
         for g in range(3):
             for m in range(4):
@@ -535,12 +533,11 @@ def tile_factoranalysisemloadinggradient_w8_kernel(
         quantize(3, 0)
         quantize(3, 512)
         quantize(2, 1024)
+        quantize(0, 1024)
         quantize(3, 768)
-        weave_alone(0, 1024, 1280, scalar, "woven_x0")
         for m in range(4):
             contract(m, (3,))
-        quantize(0, 1024)
-        new_woven(1, 1280, 1536, "woven_x0")
+        new_woven(1, 1280, 1536, "woven3_768")
         weave_gpsimd(1, 1280, 1536)
         quantize(3, 1024)
         weave_alone(0, 1280, 1536, scalar, "woven_x1")

@@ -36,8 +36,8 @@ VBUFS = 6
 RBUFS = 6
 SBUFS = 4
 WBUFS = 4
-GW = 352
-ZW = 256
+GW = 384
+ZW = 320
 
 
 def tile_factoranalysisemloadinggradient_w8_kernel(
@@ -63,8 +63,8 @@ def tile_factoranalysisemloadinggradient_w8_kernel(
 
         beta_rows = keep.tile([P, K], U8, name="beta_rows", align_bytes=ALIGN)
         p_rows = keep.tile([P, D], U8, name="p_rows", align_bytes=ALIGN)
-        zeros = keep.tile([P, P], F32, name="zeros")
-        nc.vector.memset(zeros[:], 0.0)
+        zeros = keep.tile([P, P], BF16, name="zeros")
+        nc.gpsimd.memset(zeros[:], 0.0)
         nc.vector.memset(beta_rows[:].bitcast(I32), 0)
         ones = keep.tile([P, 1], F32, name="ones")
         nc.vector.memset(ones[:], 1.0)
@@ -132,13 +132,13 @@ def tile_factoranalysisemloadinggradient_w8_kernel(
 
         load_x(0, 2)
         nc.scalar.dma_start(out=scale_cols[:], in_=x_scale.rearrange("o (j p c) -> p (o j) c", p=P, c=PACK))
-        load_scales(beta_rows, beta_scales)
         load_x_2_to_5()
+        load_scales(beta_rows, beta_scales)
         nc.sync.dma_start(out=beta_codes[:], in_=beta_words.rearrange("g p n c -> p g (n c)"))
         load_row_factor(T, t)
         load_row_factor(R, r)
-        load_scales(p_rows, p_scales)
         load_p(0)
+        load_scales(p_rows, p_scales)
         load_x(6, 2)
         nc.sync.dma_start(out=psi_rows[0:OUT_TILES, :], in_=psi.rearrange("(m p) -> m p", p=P))
         load_x(8, 4)
@@ -159,9 +159,9 @@ def tile_factoranalysisemloadinggradient_w8_kernel(
             codes.append(keep.tile([P, WIDE], U32, name="codes%d" % g, align_bytes=ALIGN))
             code_scales.append(keep.tile([P, WIDE], U8, name="code_scales%d" % g, align_bytes=ALIGN))
 
-        idle_bank = next_bank("idle", [P, 3 * P])
+        idle_bank = next_bank("idle", [P, 4 * P])
 
-        def keep_busy(count, width=P, blocks=2):
+        def keep_busy(count, width=P, blocks=4):
             for n in range(count):
                 nc.tensor.matmul(
                     out=idle_bank[:, 0 : blocks * width].rearrange("p (a n) -> p a n", a=blocks),
@@ -387,27 +387,26 @@ def tile_factoranalysisemloadinggradient_w8_kernel(
                 for i in (2 * pair, 2 * pair + 1):
                     wide(part, i, first if part == 2 else 0)
 
-        def shared_weave(g, part, buffer):
+        def shared_weave(g, part, buffer, share=GW):
             new_woven(g, part * K, (part + 1) * K, buffer)
-            weave_gpsimd(g, part * K, part * K + GW)
+            weave_gpsimd(g, part * K, part * K + share)
 
-        def rest_weave(g, part):
-            weave(g, part * K + GW, (part + 1) * K, scalar)
+        def rest_weave(g, part, share=GW):
+            weave(g, part * K + share, (part + 1) * K, scalar)
 
         def weave_alone(g, lo, hi, copy, buffer=None):
             new_woven(g, lo, hi, buffer)
             weave(g, lo, hi, copy)
 
-        keep_busy(1)
-        keep_busy(1, P, 3)
+        keep_busy(4)
+        nc.vector.tensor_copy(out=ident_bf16[:], in_=ident[:])
         widen_sorted(0, 0, 1)
         widen_sorted(0, 1, 2)
-        nc.vector.tensor_copy(out=ident_bf16[:], in_=ident[:])
         for i in (1, 2, 3):
             widen(i)
         transpose(0, 0, 1)
         transpose(0, 1, 2)
-        keep_busy(1, 96)
+        keep_busy(1)
         transpose(1)
         keep_busy(1)
         release("idle")
@@ -423,11 +422,11 @@ def tile_factoranalysisemloadinggradient_w8_kernel(
         widen(5)
         scale_out(1)
         transpose(3)
+        wide(1, 0)
         scale_out(2, 0, 1)
         quantize_x(1)
         scale_out(2, 1, 2)
         wide(0, 1)
-        wide(1, 0)
         wide(1, 1)
         scale_out(3, 0, 1)
         quantize_x(2)
@@ -482,7 +481,6 @@ def tile_factoranalysisemloadinggradient_w8_kernel(
         scale_out(10)
         scale_out(11)
         products_of(4, (1, 2), 256)
-        quantize(0, 512)
         quantize_x(10)
         quantize_x(11)
         shared_weave(1, 1, "woven_x5")
@@ -508,48 +506,56 @@ def tile_factoranalysisemloadinggradient_w8_kernel(
         for chunk in range(2):
             multiply_narrow(2, 2, chunk)
         rest_weave(2, 0)
+        weave_alone(0, 1024, 1280, scalar)
         quantize(1, 512)
-        weave_alone(1, 1024, 1280, vector)
-        weave_alone(0, 1024, 1280, vector)
-        quantize(2, 0)
-        shared_weave(2, 1, "woven_x6")
-        quantize(1, 1024)
+        shared_weave(2, 1, "woven_x5")
+        quantize(0, 512)
         products_of(7, (0, 1))
         rest_weave(2, 1)
-        new_woven(3, 0, 512, "woven_x7")
-        weave_gpsimd(3, 0, ZW)
         for chunk in range(2):
             scale_narrow(2, 2, chunk, 2)
+        quantize(2, 0)
+        new_woven(3, 0, 512, "woven_x6")
+        weave_gpsimd(3, 0, ZW)
+        quantize(0, 1024)
         for chunk in range(4):
             multiply_narrow(3, 2, chunk)
             scale_narrow(3, 2, chunk)
         weave(3, ZW, 512, scalar)
         weave_alone(3, 512, 768, scalar)
         weave_alone(3, 768, 1024, scalar)
+        weave_alone(1, 1024, 1280, scalar, "woven_x0")
         quantize(2, 512)
-        for g in range(3):
-            for m in range(4):
-                contract(m, (g,))
         quantize(3, 0)
         quantize(3, 512)
+        for g in range(2):
+            for m in range(4):
+                contract(m, (g,))
+        for g in range(2, 4):
+            for m in (0, 1):
+                contract(m, (g,))
         quantize(2, 1024)
-        quantize(0, 1024)
-        quantize(3, 768)
-        for m in range(4):
-            contract(m, (3,))
-        new_woven(1, 1280, 1536, "woven3_768")
-        weave_gpsimd(1, 1280, 1536)
         quantize(3, 1024)
+        new_woven(1, 1280, 1536, "woven3_1024")
+        weave_gpsimd(1, 1280, 1536)
+        quantize(3, 768)
+        for g in range(2, 4):
+            for m in (2, 3):
+                contract(m, (g,))
         weave_alone(0, 1280, 1536, scalar, "woven_x1")
         weave_alone(2, 1280, 1536, scalar, "woven_x3")
         for m in range(4, 8):
             scale_v(m)
-        for m in range(4):
+        for m in range(3):
             finish(m)
-        contract(4, (3, 2, 1, 0))
-        contract(5, (3, 2, 1, 0))
+        for m in (4, 5):
+            contract(m, (3, 2, 0))
+        quantize(1, 1024)
         quantize(1, 1280)
         quantize(0, 1280)
+        for m in (4, 5):
+            contract(m, (1,))
+        finish(3)
         quantize(2, 1280)
         finish(4)
         contract(6, (3, 1, 0, 2))

@@ -63,8 +63,8 @@ def tile_factoranalysisemloadinggradient_w8_kernel(
 
         beta_rows = keep.tile([P, K], U8, name="beta_rows", align_bytes=ALIGN)
         p_rows = keep.tile([P, D], U8, name="p_rows", align_bytes=ALIGN)
-        zeros = keep.tile([P, P], BF16, name="zeros")
-        nc.gpsimd.memset(zeros[:], 0.0)
+        zeros = keep.tile([P, P], F32, name="zeros")
+        nc.vector.memset(zeros[:], 0.0)
         nc.vector.memset(beta_rows[:].bitcast(I32), 0)
         ones = keep.tile([P, 1], F32, name="ones")
         nc.vector.memset(ones[:], 1.0)
@@ -159,9 +159,9 @@ def tile_factoranalysisemloadinggradient_w8_kernel(
             codes.append(keep.tile([P, WIDE], U32, name="codes%d" % g, align_bytes=ALIGN))
             code_scales.append(keep.tile([P, WIDE], U8, name="code_scales%d" % g, align_bytes=ALIGN))
 
-        idle_bank = next_bank("idle", [P, 4 * P])
+        idle_bank = next_bank("idle", [P, 3 * P])
 
-        def keep_busy(count, width=P, blocks=4):
+        def keep_busy(count, width=P, blocks=2):
             for n in range(count):
                 nc.tensor.matmul(
                     out=idle_bank[:, 0 : blocks * width].rearrange("p (a n) -> p a n", a=blocks),
@@ -398,7 +398,8 @@ def tile_factoranalysisemloadinggradient_w8_kernel(
             new_woven(g, lo, hi, buffer)
             weave(g, lo, hi, copy)
 
-        keep_busy(4)
+        keep_busy(1)
+        keep_busy(1, P, 3)
         nc.vector.tensor_copy(out=ident_bf16[:], in_=ident[:])
         widen_sorted(0, 0, 1)
         widen_sorted(0, 1, 2)
@@ -406,7 +407,7 @@ def tile_factoranalysisemloadinggradient_w8_kernel(
             widen(i)
         transpose(0, 0, 1)
         transpose(0, 1, 2)
-        keep_busy(1)
+        keep_busy(1, 96)
         transpose(1)
         keep_busy(1)
         release("idle")

@@ -361,8 +361,8 @@ def tile_factoranalysisemloadinggradient_w8_kernel(
             v_scaled[m] = result_pool.tile([P, K], F32, name="v_scaled", bufs=VBUFS)
             nc.scalar.activation(out=v_scaled[m][:], in_=v_in[m], func=COPY, scale=inv_psi[:, m : m + 1])
 
-        def scale_v_gpsimd(m):
-            v_scaled[m] = keep.tile([P, K], F32, name="v_scaled%d" % m)
+        def scale_v_gpsimd(m, buffer=None):
+            v_scaled[m] = keep.tile([P, K], F32, name=buffer or "v_scaled%d" % m, align_bytes=64)
             nc.gpsimd.tensor_scalar(
                 out=v_scaled[m][:], in0=v_in[m], scalar1=inv_psi[:, m : m + 1], scalar2=0.0, op0=MULT, op1=ADD
             )
@@ -417,12 +417,13 @@ def tile_factoranalysisemloadinggradient_w8_kernel(
         quantize_x(0, 1, 2)
         transpose(2)
         turn_rt()
-        copy_rt()
         widen(4)
+        copy_rt()
         wide(0, 0)
         widen(5)
         scale_out(1)
         transpose(3)
+        transpose(4)
         wide(1, 0)
         scale_out(2, 0, 1)
         quantize_x(1)
@@ -437,10 +438,11 @@ def tile_factoranalysisemloadinggradient_w8_kernel(
         quantize_x(3)
         widen_sorted(6, 0, 4)
         turn_psi()
-        transpose(4)
-        transpose(5)
+        for i in (5, 6, 7):
+            transpose(i)
+        widen_sorted(8)
         invert_psi()
-        widen_sorted(8, 0, 4)
+        widen_sorted(9)
         for m in range(2):
             scale_v_gpsimd(m)
         for m in range(2, 4):
@@ -449,8 +451,6 @@ def tile_factoranalysisemloadinggradient_w8_kernel(
         scale_out(5)
         wide(0, 3)
         wide(1, 3)
-        transpose(6)
-        transpose(7)
         quantize_x(4)
         quantize_x(5)
         shared_weave(0, 0, "woven_x2")

@@ -24,20 +24,18 @@ PACK = 4
 GROUPS = N // (P * PACK)
 HALVES = D // (P * PACK)
 TILES = GROUPS * PACK
-STEPS = TILES // 2
+PAIRS = TILES // 2
 HALF = D // 2
 OUT_TILES = D // P
 BANKS = 8
 
 WIDE = K + D
 R, T = 0, 1
+Z, E0, E1 = 0, 1, 2
+QUARTER = K // 2
 ALIGN = 256
-VBUFS = 6
-RBUFS = 6
-SBUFS = 4
-WBUFS = 4
-GW = 384
-ZW = 320
+SHARE = 384
+LAST_SHARE = 320
 
 
 def tile_factoranalysisemloadinggradient_w8_kernel(
@@ -46,8 +44,8 @@ def tile_factoranalysisemloadinggradient_w8_kernel(
     nc = tc.nc
     with ExitStack() as ctx:
         keep = ctx.enter_context(tc.tile_pool(name="keep", bufs=1))
-        widened_pool = ctx.enter_context(tc.tile_pool(name="widened_pool", bufs=WBUFS))
-        result_pool = ctx.enter_context(tc.tile_pool(name="result_pool", bufs=RBUFS))
+        widened_pool = ctx.enter_context(tc.tile_pool(name="widened_pool", bufs=4))
+        result_pool = ctx.enter_context(tc.tile_pool(name="result_pool", bufs=6))
         psum = ctx.enter_context(tc.psum_pool(name="psum", bufs=1))
         ctx.enter_context(tc.manual_schedule(engines={ENGINE.PE, ENGINE.Activation, ENGINE.DVE, ENGINE.SP, ENGINE.Pool}))
 
@@ -68,7 +66,6 @@ def tile_factoranalysisemloadinggradient_w8_kernel(
         nc.vector.memset(beta_rows[:].bitcast(I32), 0)
         ones = keep.tile([P, 1], F32, name="ones")
         nc.vector.memset(ones[:], 1.0)
-
         nc.vector.memset(p_rows[:].bitcast(I32), 0)
         ident = keep.tile([P, P], F32, name="ident")
         make_identity(nc, ident[:])
@@ -142,17 +139,17 @@ def tile_factoranalysisemloadinggradient_w8_kernel(
         load_x(6, 2)
         nc.sync.dma_start(out=psi_rows[0:OUT_TILES, :], in_=psi.rearrange("(m p) -> m p", p=P))
         load_x(8, 4)
-        load_v(0, 4)
+        load_v(0, 5)
         load_p(1)
         load_x(12, 4)
-        load_v(4, 8)
+        load_v(5, 8)
 
         rt = keep.tile([P, 2, TILES], F32, name="rt")
         inv_psi = keep.tile([P, OUT_TILES], F32, name="inv_psi")
         gain = keep.tile([P, OUT_TILES], F32, name="gain")
 
         x_codes, x_code_scales, codes, code_scales = [], [], [], []
-        for s in range(STEPS):
+        for s in range(PAIRS):
             x_codes.append(keep.tile([P, 2, HALVES * P], U32, name="x_codes%d" % s, align_bytes=ALIGN))
             x_code_scales.append(keep.tile([P, 2, HALVES * P], U8, name="x_code_scales%d" % s, align_bytes=ALIGN))
         for g in range(GROUPS):
@@ -161,15 +158,14 @@ def tile_factoranalysisemloadinggradient_w8_kernel(
 
         idle_bank = next_bank("idle", [P, 3 * P])
 
-        def keep_busy(count, width=P, blocks=2):
-            for n in range(count):
-                nc.tensor.matmul(
-                    out=idle_bank[:, 0 : blocks * width].rearrange("p (a n) -> p a n", a=blocks),
-                    lhsT=zeros[:],
-                    rhs=zeros[:, 0:width].unsqueeze(1).to_broadcast([P, blocks, width]),
-                    start=True,
-                    stop=True,
-                )
+        def keep_busy(blocks, width=P):
+            nc.tensor.matmul(
+                out=idle_bank[:, 0 : blocks * width].rearrange("p (a n) -> p a n", a=blocks),
+                lhsT=zeros[:],
+                rhs=zeros[:, 0:width].unsqueeze(1).to_broadcast([P, blocks, width]),
+                start=True,
+                stop=True,
+            )
 
         spread = {}
 
@@ -198,15 +194,15 @@ def tile_factoranalysisemloadinggradient_w8_kernel(
 
         words_of, transposed, woven_x = {}, {}, {}
 
-        def widen(i, copy=None):
+        def widen(i):
             tile = widened_pool.tile([P, D], BF16, name="widened")
-            (copy or nc.scalar.copy)(out=tile[:], in_=x_raw[i].bitcast(FP8))
+            nc.scalar.copy(out=tile[:], in_=x_raw[i].bitcast(FP8))
             for j in range(HALVES):
                 for u in range(2):
                     words_of[i, j, u] = tile[:].bitcast(F32)[:, 2 * P * j + u : 2 * P * (j + 1) : 2]
 
         def widen_sorted(i, lo=0, hi=HALVES):
-            tile = widened_pool.tile([P, 2, hi - lo, P, 2], BF16, name="sorted", bufs=SBUFS)
+            tile = widened_pool.tile([P, 2, hi - lo, P, 2], BF16, name="sorted", bufs=4)
             nc.vector.tensor_scalar(
                 out=tile[:].rearrange("p u b q e -> p (b q) u e"),
                 in0=x_rows[i][:, lo * HALF : hi * HALF].bitcast(FP8).rearrange("p (q u e) -> p q u e", u=2, e=2),
@@ -296,8 +292,8 @@ def tile_factoranalysisemloadinggradient_w8_kernel(
             first = max(n for (h, n) in woven if h == g and n <= lo)
             return woven[g, first][:, lo - first : hi - first, :]
 
-        def weave(g, lo, hi, copy):
-            copy(
+        def weave(g, lo, hi):
+            nc.scalar.copy(
                 out=woven_columns(g, lo, hi).rearrange("p (b n) c -> p b c n", n=4),
                 in_=plane(g, lo, hi).rearrange("p c (b n) -> p b c n", n=4),
             )
@@ -338,7 +334,7 @@ def tile_factoranalysisemloadinggradient_w8_kernel(
             )
             release((g, part, chunk))
 
-        sums, added, v_scaled, differences = {}, {}, {}, {}
+        sums, added, v_scaled = {}, {}, {}
 
         def contract(m, groups, lo=0, hi=K):
             if (m, lo) not in sums:
@@ -358,7 +354,7 @@ def tile_factoranalysisemloadinggradient_w8_kernel(
                 )
 
         def scale_v(m):
-            v_scaled[m] = result_pool.tile([P, K], F32, name="v_scaled", bufs=VBUFS)
+            v_scaled[m] = result_pool.tile([P, K], F32, name="v_scaled", bufs=6)
             nc.scalar.activation(out=v_scaled[m][:], in_=v_in[m], func=COPY, scale=inv_psi[:, m : m + 1])
 
         def scale_v_gpsimd(m, buffer=None):
@@ -380,189 +376,192 @@ def tile_factoranalysisemloadinggradient_w8_kernel(
             release(("c", m, lo))
             nc.sync.dma_start(out=out[P * m : P * (m + 1), lo:hi], in_=result[:, lo:hi])
 
-        vector, scalar = nc.vector.tensor_copy, nc.scalar.copy
-        every = range(GROUPS)
         def products_of(pair, parts, first=0):
             for part in parts:
                 for i in (2 * pair, 2 * pair + 1):
-                    wide(part, i, first if part == 2 else 0)
+                    wide(part, i, first if part == E1 else 0)
 
-        def shared_weave(g, part, buffer, share=GW):
+        def weave_share(g, part, buffer):
             new_woven(g, part * K, (part + 1) * K, buffer)
-            weave_gpsimd(g, part * K, part * K + share)
+            weave_gpsimd(g, part * K, part * K + SHARE)
 
-        def rest_weave(g, part, share=GW):
-            weave(g, part * K + share, (part + 1) * K, scalar)
+        def weave_rest(g, part):
+            weave(g, part * K + SHARE, (part + 1) * K)
 
-        def weave_alone(g, lo, hi, copy, buffer=None):
-            new_woven(g, lo, hi, buffer)
-            weave(g, lo, hi, copy)
+        def weave_quarter(g, lo, buffer=None):
+            new_woven(g, lo, lo + QUARTER, buffer)
+            weave(g, lo, lo + QUARTER)
 
-        keep_busy(1)
-        keep_busy(1, P, 3)
+        keep_busy(2)
+        keep_busy(3)
         nc.vector.tensor_copy(out=ident_bf16[:], in_=ident[:])
-        widen_sorted(0, 0, 1)
-        widen_sorted(0, 1, 2)
-        for i in (1, 2, 3):
+        for j in range(HALVES):
+            widen_sorted(0, j, j + 1)
+        for i in (1, 2, 4, 5):
             widen(i)
-        transpose(0, 0, 1)
-        transpose(0, 1, 2)
-        keep_busy(1, 96)
-        transpose(1)
-        keep_busy(1)
+        for j in range(HALVES):
+            transpose(0, j, j + 1)
+        keep_busy(3, 112)
         release("idle")
-        scale_out(0, 0, 1)
-        scale_out(0, 1, 2)
+        transpose(1)
+        for j in range(HALVES):
+            scale_out(0, j, j + 1)
         quantize_x(0, 0, 1)
+        widen_sorted(3, 0, 1)
         quantize_x(0, 1, 2)
         transpose(2)
+        multiply_wide(Z, 0)
         turn_rt()
-        widen(4)
         copy_rt()
-        wide(0, 0)
-        widen(5)
+        scale_wide(Z, 0)
         scale_out(1)
-        transpose(3)
-        transpose(4)
-        wide(1, 0)
-        scale_out(2, 0, 1)
+        widen_sorted(3, 1, 2)
         quantize_x(1)
-        scale_out(2, 1, 2)
-        wide(0, 1)
-        wide(1, 1)
+        transpose(4)
+        transpose(3)
+        wide(Z, 1)
+        wide(E0, 0)
+        wide(E0, 1)
+        scale_out(2)
         scale_out(3, 0, 1)
         quantize_x(2)
         scale_out(3, 1, 2)
-        wide(0, 2)
-        wide(1, 2)
+        wide(Z, 2)
+        wide(E0, 2)
+        widen_sorted(6, 0, 2 * HALVES)
         quantize_x(3)
-        widen_sorted(6, 0, 4)
+
         turn_psi()
         for i in (5, 6, 7):
             transpose(i)
-        widen_sorted(8)
         invert_psi()
-        widen_sorted(9)
-        for m in range(2):
+        widen_sorted(8, 0, 2 * HALVES)
+        for m in (0, 1):
             scale_v_gpsimd(m)
-        for m in range(2, 4):
+        for m in (2, 3, 4):
             scale_v(m)
         scale_out(4)
         scale_out(5)
-        wide(0, 3)
-        wide(1, 3)
+        wide(Z, 3)
+        wide(E0, 3)
         quantize_x(4)
         quantize_x(5)
-        shared_weave(0, 0, "woven_x2")
-        widen_sorted(10, 0, 4)
-        for i in range(4):
-            wide(2, i)
-        products_of(2, (0,))
+        weave_share(0, Z, "woven_x2")
+        widen_sorted(10, 0, 2 * HALVES)
+        for i in range(PACK):
+            wide(E1, i)
+        products_of(2, (Z,))
         scale_out(6)
         scale_out(7)
-        products_of(2, (1, 2))
+        products_of(2, (E0, E1))
         make_gain()
         quantize_x(6)
         quantize_x(7)
-        shared_weave(0, 1, "woven_x3")
-        widen_sorted(12, 0, 4)
+        weave_share(0, E0, "woven_x3")
+        widen_sorted(12, 0, 2 * HALVES)
+
         for i in range(8, 12):
             transpose(i)
         scale_out(8)
         scale_out(9)
-        rest_weave(0, 0)
-        rest_weave(0, 1)
-        products_of(3, (0,))
+        weave_rest(0, Z)
+        weave_rest(0, E0)
+        products_of(3, (Z,))
         quantize_x(8)
         quantize_x(9)
-        shared_weave(1, 0, "woven_x4")
-        widen_sorted(14, 0, 4)
-        products_of(3, (1, 2))
-        products_of(4, (0,))
+        weave_share(1, Z, "woven_x4")
+        widen_sorted(14, 0, 2 * HALVES)
+        products_of(3, (E0, E1))
+        products_of(4, (Z,))
         scale_out(10)
         scale_out(11)
-        products_of(4, (1, 2), 256)
+        products_of(4, (E0, E1), QUARTER)
         quantize_x(10)
         quantize_x(11)
-        shared_weave(1, 1, "woven_x5")
-        quantize(0, 0)
+        weave_share(1, E0, "woven_x5")
+        quantize(0, Z * K)
+
         for i in range(12, 16):
             transpose(i)
         scale_out(12)
         scale_out(13)
-        rest_weave(1, 0)
-        rest_weave(1, 1)
-        products_of(5, (0,))
+        weave_rest(1, Z)
+        weave_rest(1, E0)
+        products_of(5, (Z,))
         quantize_x(12)
         quantize_x(13)
-        shared_weave(2, 0, "woven_x6")
-        quantize(1, 0)
-        products_of(5, (1, 2), 256)
-        products_of(6, (0,))
+        weave_share(2, Z, "woven_x6")
+        quantize(1, Z * K)
+        products_of(5, (E0, E1), QUARTER)
+        products_of(6, (Z,))
         scale_out(14)
         scale_out(15)
-        products_of(6, (1,))
+        products_of(6, (E0,))
         quantize_x(14)
         quantize_x(15)
+
         for chunk in range(2):
-            multiply_narrow(2, 2, chunk)
-        rest_weave(2, 0)
-        weave_alone(0, 1024, 1280, scalar)
-        quantize(1, 512)
-        shared_weave(2, 1, "woven_x5")
-        quantize(0, 512)
-        products_of(7, (0, 1))
-        rest_weave(2, 1)
+            multiply_narrow(2, E1, chunk)
+        weave_rest(2, Z)
+        weave_quarter(0, E1 * K)
+        quantize(1, E0 * K)
+        new_woven(2, E0 * K, E1 * K, "woven_x5")
+        weave_gpsimd(2, E0 * K, E0 * K + 320)
+        quantize(0, E0 * K)
+        products_of(7, (Z, E0))
+        weave(2, E0 * K + 320, E1 * K)
         for chunk in range(2):
-            scale_narrow(2, 2, chunk, 2)
-        quantize(2, 0)
-        new_woven(3, 0, 512, "woven_x6")
-        weave_gpsimd(3, 0, ZW)
-        quantize(0, 1024)
+            scale_narrow(2, E1, chunk, 2)
+        quantize(2, Z * K)
+        new_woven(3, 0, K, "woven_x6")
+        weave_gpsimd(3, 0, LAST_SHARE)
+        quantize(0, E1 * K)
         for chunk in range(4):
-            multiply_narrow(3, 2, chunk)
-            scale_narrow(3, 2, chunk)
-        weave(3, ZW, 512, scalar)
-        weave_alone(3, 512, 768, scalar)
-        weave_alone(3, 768, 1024, scalar)
-        weave_alone(1, 1024, 1280, scalar, "woven_x0")
-        quantize(2, 512)
-        quantize(3, 0)
-        quantize(3, 512)
-        for g in range(2):
+            multiply_narrow(3, E1, chunk)
+            scale_narrow(3, E1, chunk)
+        weave(3, LAST_SHARE, K)
+        weave_quarter(3, E0 * K)
+        weave_quarter(3, E0 * K + QUARTER)
+        weave_quarter(1, E1 * K, "woven_x0")
+
+        quantize(2, E0 * K)
+        quantize(3, Z * K)
+        quantize(3, E0 * K)
+        for g in (0, 1):
             for m in range(4):
                 contract(m, (g,))
-        for g in range(2, 4):
+        for g in (2, 3):
             for m in (0, 1):
                 contract(m, (g,))
-        quantize(2, 1024)
-        quantize(3, 1024)
-        new_woven(1, 1280, 1536, "woven3_1024")
-        weave_gpsimd(1, 1280, 1536)
-        quantize(3, 768)
-        for g in range(2, 4):
+        quantize(2, E1 * K)
+        quantize(3, E1 * K)
+        new_woven(1, E1 * K + QUARTER, WIDE, "woven3_1024")
+        weave_gpsimd(1, E1 * K + QUARTER, WIDE)
+        quantize(3, E0 * K + QUARTER)
+        for g in (2, 3):
             for m in (2, 3):
                 contract(m, (g,))
-        weave_alone(0, 1280, 1536, scalar, "woven_x1")
-        weave_alone(2, 1280, 1536, scalar, "woven_x3")
-        for m in range(4, 8):
+        weave_quarter(0, E1 * K + QUARTER, "woven_x1")
+        weave_quarter(2, E1 * K + QUARTER, "woven_x3")
+        for m in range(5, OUT_TILES):
             scale_v(m)
         for m in range(3):
             finish(m)
         for m in (4, 5):
             contract(m, (3, 2, 0))
-        quantize(1, 1024)
-        quantize(1, 1280)
-        quantize(0, 1280)
+        quantize(1, E1 * K)
+        quantize(1, E1 * K + QUARTER)
+        quantize(0, E1 * K + QUARTER)
         for m in (4, 5):
             contract(m, (1,))
         finish(3)
-        quantize(2, 1280)
+        quantize(2, E1 * K + QUARTER)
         finish(4)
         contract(6, (3, 1, 0, 2))
         finish(5)
-        contract(7, every, 0, 256)
+
+        contract(7, range(GROUPS), 0, QUARTER)
         finish(6)
-        contract(7, every, 256, 512)
-        finish(7, 0, 256)
-        finish(7, 256, 512)
+        contract(7, range(GROUPS), QUARTER, K)
+        finish(7, 0, QUARTER)
+        finish(7, QUARTER, K)

@@ -35,7 +35,7 @@ Z, E0, E1 = 0, 1, 2
 QUARTER = K // 2
 ALIGN = 256
 SHARE = 384
-LAST_SHARE = 320
+EARLY_V = 5
 
 
 def tile_factoranalysisemloadinggradient_w8_kernel(
@@ -77,28 +77,16 @@ def tile_factoranalysisemloadinggradient_w8_kernel(
                     out=tile[32 * q : 32 * q + 4 * HALVES, :].bitcast(I32), in_=rows_in[:, 4 * q : 4 * q + 4, :]
                 )
 
-        def slot(i):
-            g, n = divmod(i, PACK)
-            return g, (n + 2) % PACK if g == 1 else n
-
         x_cases = x_bytes.rearrange("(g m c) k -> g m c k", m=P, c=PACK)
         x_raw, x_rows = {}, {}
 
         def load_x(first, count):
-            g, c = slot(first)
+            g, c = divmod(first, PACK)
             raw = keep.tile([P, count, D], U8, name="x_raw%d" % first)
             nc.sync.dma_start(out=raw[:], in_=x_cases[g][:, c : c + count, :])
             for n in range(count):
                 x_raw[first + n] = raw[:, n, :]
                 x_rows[first + n] = raw[:, n:count, :].rearrange("p c k -> p (c k)")
-
-        def load_x_2_to_5():
-            raw = keep.tile([P, 2, 2 * D], U8, name="x_raw2")
-            rows = x_bytes.rearrange("(g m h c) k -> m g h (c k)", m=P, h=2, c=2)
-            nc.sync.dma_start(out=raw[:], in_=rows[:, 0:2, 1, :])
-            for n in range(4):
-                x_raw[2 + n] = raw[:, n // 2, n % 2 * D : (n % 2 + 1) * D]
-                x_rows[2 + n] = x_raw[2 + n]
 
         scale_cols = keep.tile([P, HALVES, PACK], F32, name="scale_cols")
         beta_codes = keep.tile([P, HALVES, K * PACK], U8, name="beta_codes", align_bytes=ALIGN)
@@ -129,9 +117,10 @@ def tile_factoranalysisemloadinggradient_w8_kernel(
 
         load_x(0, 2)
         nc.scalar.dma_start(out=scale_cols[:], in_=x_scale.rearrange("o (j p c) -> p (o j) c", p=P, c=PACK))
-        load_x_2_to_5()
+        load_x(2, 2)
         load_scales(beta_rows, beta_scales)
         nc.sync.dma_start(out=beta_codes[:], in_=beta_words.rearrange("g p n c -> p g (n c)"))
+        load_x(4, 2)
         load_row_factor(T, t)
         load_row_factor(R, r)
         load_p(0)
@@ -139,10 +128,10 @@ def tile_factoranalysisemloadinggradient_w8_kernel(
         load_x(6, 2)
         nc.sync.dma_start(out=psi_rows[0:OUT_TILES, :], in_=psi.rearrange("(m p) -> m p", p=P))
         load_x(8, 4)
-        load_v(0, 5)
+        load_v(0, EARLY_V)
         load_p(1)
         load_x(12, 4)
-        load_v(5, 8)
+        load_v(EARLY_V, OUT_TILES)
 
         rt = keep.tile([P, 2, TILES], F32, name="rt")
         inv_psi = keep.tile([P, OUT_TILES], F32, name="inv_psi")
@@ -190,16 +179,16 @@ def tile_factoranalysisemloadinggradient_w8_kernel(
             release("psi")
 
         def make_gain():
-            nc.vector.tensor_scalar(out=gain[:], in0=inv_psi[:], scalar1=1.0 / N, scalar2=None, op0=MULT)
+            nc.scalar.activation(out=gain[:], in_=inv_psi[:], func=COPY, scale=1.0 / N)
 
         words_of, transposed, woven_x = {}, {}, {}
 
-        def widen(i):
-            tile = widened_pool.tile([P, D], BF16, name="widened")
-            nc.scalar.copy(out=tile[:], in_=x_raw[i].bitcast(FP8))
-            for j in range(HALVES):
+        def widen(i, lo=0, hi=HALVES):
+            tile = widened_pool.tile([P, (hi - lo) * HALF], BF16, name="widened", bufs=5)
+            nc.scalar.copy(out=tile[:], in_=x_raw[i][:, lo * HALF : hi * HALF].bitcast(FP8))
+            for j in range(lo, hi):
                 for u in range(2):
-                    words_of[i, j, u] = tile[:].bitcast(F32)[:, 2 * P * j + u : 2 * P * (j + 1) : 2]
+                    words_of[i, j, u] = tile[:].bitcast(F32)[:, 2 * P * (j - lo) + u : 2 * P * (j - lo + 1) : 2]
 
         def widen_sorted(i, lo=0, hi=HALVES):
             tile = widened_pool.tile([P, 2, hi - lo, P, 2], BF16, name="sorted", bufs=4)
@@ -245,9 +234,9 @@ def tile_factoranalysisemloadinggradient_w8_kernel(
         weights = (beta_codes, p_codes[0], p_codes[1])
         weight_scales = (beta_rows[:, 0:K], p_rows[:, 0:HALF], p_rows[:, HALF:D])
 
-        def multiply(bank, i, part, first, width):
+        def multiply(bank, i, part, first, width, halves=range(HALVES)):
             s, h = divmod(i, 2)
-            for j in range(HALVES):
+            for j in halves:
                 cols = slice(j * P, (j + 1) * P)
                 nc.tensor.matmul_mx(
                     out=bank,
@@ -272,7 +261,7 @@ def tile_factoranalysisemloadinggradient_w8_kernel(
             multiply(products[part, i][:], i, part, first, K - first)
 
         def scale_wide(part, i, first=0):
-            g, c = slot(i)
+            g, c = divmod(i, PACK)
             nc.scalar.activation(
                 out=plane(g, part * K + first, (part + 1) * K)[:, c, :],
                 in_=products[part, i][:],
@@ -316,10 +305,13 @@ def tile_factoranalysisemloadinggradient_w8_kernel(
                 in_=woven[g, lo][:].rearrange("p n c -> p (n c)"),
             )
 
-        def multiply_narrow(g, part, chunk):
-            products[g, part, chunk] = next_bank((g, part, chunk), [P, PACK, P])
+        def multiply_narrow(g, part, chunks):
+            for chunk in chunks:
+                products[g, part, chunk] = next_bank((g, part, chunk), [P, PACK, P])
             for c in range(PACK):
-                multiply(products[g, part, chunk][:, c, :], g * PACK + c, part, P * chunk, P)
+                for j in range(HALVES):
+                    for chunk in chunks:
+                        multiply(products[g, part, chunk][:, c, :], g * PACK + c, part, P * chunk, P, (j,))
 
         def scale_narrow(g, part, chunk, width=K // P):
             lo = part * K + chunk // width * width * P
@@ -357,8 +349,8 @@ def tile_factoranalysisemloadinggradient_w8_kernel(
             v_scaled[m] = result_pool.tile([P, K], F32, name="v_scaled", bufs=6)
             nc.scalar.activation(out=v_scaled[m][:], in_=v_in[m], func=COPY, scale=inv_psi[:, m : m + 1])
 
-        def scale_v_gpsimd(m, buffer=None):
-            v_scaled[m] = keep.tile([P, K], F32, name=buffer or "v_scaled%d" % m, align_bytes=64)
+        def scale_v_gpsimd(m):
+            v_scaled[m] = keep.tile([P, K], F32, name="v_scaled%d" % m, align_bytes=64)
             nc.gpsimd.tensor_scalar(
                 out=v_scaled[m][:], in0=v_in[m], scalar1=inv_psi[:, m : m + 1], scalar2=0.0, op0=MULT, op1=ADD
             )
@@ -381,12 +373,12 @@ def tile_factoranalysisemloadinggradient_w8_kernel(
                 for i in (2 * pair, 2 * pair + 1):
                     wide(part, i, first if part == E1 else 0)
 
-        def weave_share(g, part, buffer):
+        def weave_share(g, part, buffer, share=SHARE):
             new_woven(g, part * K, (part + 1) * K, buffer)
-            weave_gpsimd(g, part * K, part * K + SHARE)
+            weave_gpsimd(g, part * K, part * K + share)
 
-        def weave_rest(g, part):
-            weave(g, part * K + SHARE, (part + 1) * K)
+        def weave_rest(g, part, share=SHARE):
+            weave(g, part * K + share, (part + 1) * K)
 
         def weave_quarter(g, lo, buffer=None):
             new_woven(g, lo, lo + QUARTER, buffer)
@@ -397,48 +389,49 @@ def tile_factoranalysisemloadinggradient_w8_kernel(
         nc.vector.tensor_copy(out=ident_bf16[:], in_=ident[:])
         for j in range(HALVES):
             widen_sorted(0, j, j + 1)
-        for i in (1, 2, 4, 5):
+        widen_sorted(1, 0, 1)
+        widen(1, 1, 2)
+        for i in range(2, 6):
             widen(i)
         for j in range(HALVES):
             transpose(0, j, j + 1)
-        keep_busy(3, 112)
+        keep_busy(2)
         release("idle")
         transpose(1)
         for j in range(HALVES):
             scale_out(0, j, j + 1)
-        quantize_x(0, 0, 1)
-        widen_sorted(3, 0, 1)
-        quantize_x(0, 1, 2)
+        for j in range(HALVES):
+            quantize_x(0, j, j + 1)
         transpose(2)
         multiply_wide(Z, 0)
         turn_rt()
         copy_rt()
         scale_wide(Z, 0)
+        widen(6, 0, 1)
         scale_out(1)
-        widen_sorted(3, 1, 2)
-        quantize_x(1)
-        transpose(4)
         transpose(3)
+        transpose(4)
+        for i in (1, 2):
+            scale_out(i + 1, 0, 1)
+            quantize_x(i)
+            scale_out(i + 1, 1, 2)
         wide(Z, 1)
         wide(E0, 0)
         wide(E0, 1)
-        scale_out(2)
-        scale_out(3, 0, 1)
-        quantize_x(2)
-        scale_out(3, 1, 2)
         wide(Z, 2)
         wide(E0, 2)
-        widen_sorted(6, 0, 2 * HALVES)
+        widen_sorted(6, 1, 2 * HALVES)
         quantize_x(3)
 
         turn_psi()
         for i in (5, 6, 7):
             transpose(i)
+        widen_sorted(8)
         invert_psi()
-        widen_sorted(8, 0, 2 * HALVES)
+        widen_sorted(9)
         for m in (0, 1):
             scale_v_gpsimd(m)
-        for m in (2, 3, 4):
+        for m in range(2, EARLY_V):
             scale_v(m)
         scale_out(4)
         scale_out(5)
@@ -454,7 +447,6 @@ def tile_factoranalysisemloadinggradient_w8_kernel(
         scale_out(6)
         scale_out(7)
         products_of(2, (E0, E1))
-        make_gain()
         quantize_x(6)
         quantize_x(7)
         weave_share(0, E0, "woven_x3")
@@ -466,6 +458,7 @@ def tile_factoranalysisemloadinggradient_w8_kernel(
         scale_out(9)
         weave_rest(0, Z)
         weave_rest(0, E0)
+        make_gain()
         products_of(3, (Z,))
         quantize_x(8)
         quantize_x(9)
@@ -500,26 +493,24 @@ def tile_factoranalysisemloadinggradient_w8_kernel(
         quantize_x(14)
         quantize_x(15)
 
-        for chunk in range(2):
-            multiply_narrow(2, E1, chunk)
+        multiply_narrow(2, E1, (0, 1))
         weave_rest(2, Z)
         weave_quarter(0, E1 * K)
         quantize(1, E0 * K)
-        new_woven(2, E0 * K, E1 * K, "woven_x5")
-        weave_gpsimd(2, E0 * K, E0 * K + 320)
+        weave_share(2, E0, "woven_x5", QUARTER)
         quantize(0, E0 * K)
         products_of(7, (Z, E0))
-        weave(2, E0 * K + 320, E1 * K)
+        weave_rest(2, E0, QUARTER)
         for chunk in range(2):
             scale_narrow(2, E1, chunk, 2)
-        quantize(2, Z * K)
-        new_woven(3, 0, K, "woven_x6")
-        weave_gpsimd(3, 0, LAST_SHARE)
         quantize(0, E1 * K)
+        quantize(2, Z * K)
+        weave_share(3, Z, "woven_x6")
+        quantize(2, E1 * K)
         for chunk in range(4):
-            multiply_narrow(3, E1, chunk)
+            multiply_narrow(3, E1, (chunk,))
             scale_narrow(3, E1, chunk)
-        weave(3, LAST_SHARE, K)
+        weave_rest(3, Z)
         weave_quarter(3, E0 * K)
         weave_quarter(3, E0 * K + QUARTER)
         weave_quarter(1, E1 * K, "woven_x0")
@@ -533,7 +524,6 @@ def tile_factoranalysisemloadinggradient_w8_kernel(
         for g in (2, 3):
             for m in (0, 1):
                 contract(m, (g,))
-        quantize(2, E1 * K)
         quantize(3, E1 * K)
         new_woven(1, E1 * K + QUARTER, WIDE, "woven3_1024")
         weave_gpsimd(1, E1 * K + QUARTER, WIDE)
@@ -543,7 +533,7 @@ def tile_factoranalysisemloadinggradient_w8_kernel(
                 contract(m, (g,))
         weave_quarter(0, E1 * K + QUARTER, "woven_x1")
         weave_quarter(2, E1 * K + QUARTER, "woven_x3")
-        for m in range(5, OUT_TILES):
+        for m in range(EARLY_V, OUT_TILES):
             scale_v(m)
         for m in range(3):
             finish(m)

from contextlib import ExitStack

import concourse.mybir as mybir
from concourse.masks import make_identity

N, D, K = 2048, 1024, 512
FLOPS = 2 * N * D * (D + K) + 2 * N * D * K

F32 = mybir.dt.float32
BF16 = mybir.dt.bfloat16
U32 = mybir.dt.uint32
I32 = mybir.dt.int32
U8 = mybir.dt.uint8
FP8 = mybir.dt.float8_e4m3fn
X4 = mybir.dt.float8_e4m3fn_x4
MULT = mybir.AluOpType.mult
SUBTRACT = mybir.AluOpType.subtract
ADD = mybir.AluOpType.add
COPY = mybir.ActivationFunctionType.Copy
ENGINE = mybir.EngineType

P = 128
PACK = 4
GROUPS = N // (P * PACK)
HALVES = D // (P * PACK)
TILES = GROUPS * PACK
PAIRS = TILES // 2
HALF = D // 2
OUT_TILES = D // P
BANKS = 8

WIDE = K + D
R, T = 0, 1
Z, E0, E1 = 0, 1, 2
QUARTER = K // 2
ALIGN = 256
SHARE = 384
EARLY_V = 5


def tile_factoranalysisemloadinggradient_w8_kernel(
    tc, x_bytes, x_scale, p_words, p_scales, beta_words, beta_scales, r, t, v, psi, out
):
    nc = tc.nc
    with ExitStack() as ctx:
        keep = ctx.enter_context(tc.tile_pool(name="keep", bufs=1))
        widened_pool = ctx.enter_context(tc.tile_pool(name="widened_pool", bufs=4))
        result_pool = ctx.enter_context(tc.tile_pool(name="result_pool", bufs=6))
        psum = ctx.enter_context(tc.psum_pool(name="psum", bufs=1))
        ctx.enter_context(tc.manual_schedule(engines={ENGINE.PE, ENGINE.Activation, ENGINE.DVE, ENGINE.SP, ENGINE.Pool}))

        free_banks = list(range(BANKS))
        bank_of = {}

        def next_bank(key, shape, dtype=F32):
            bank_of[key] = free_banks.pop(0)
            return psum.tile(shape, dtype, name="bank%d" % bank_of[key])

        def release(key):
            free_banks.append(bank_of[key])

        beta_rows = keep.tile([P, K], U8, name="beta_rows", align_bytes=ALIGN)
        p_rows = keep.tile([P, D], U8, name="p_rows", align_bytes=ALIGN)
        zeros = keep.tile([P, P], F32, name="zeros")
        nc.vector.memset(zeros[:], 0.0)
        nc.vector.memset(beta_rows[:].bitcast(I32), 0)
        ones = keep.tile([P, 1], F32, name="ones")
        nc.vector.memset(ones[:], 1.0)
        nc.vector.memset(p_rows[:].bitcast(I32), 0)
        ident = keep.tile([P, P], F32, name="ident")
        make_identity(nc, ident[:])

        def load_scales(tile, scales):
            rows_in = scales.bitcast(I32)
            for q in range(4):
                nc.sync.dma_start(
                    out=tile[32 * q : 32 * q + 4 * HALVES, :].bitcast(I32), in_=rows_in[:, 4 * q : 4 * q + 4, :]
                )

        x_cases = x_bytes.rearrange("(g m c) k -> g m c k", m=P, c=PACK)
        x_raw, x_rows = {}, {}

        def load_x(first, count):
            g, c = divmod(first, PACK)
            raw = keep.tile([P, count, D], U8, name="x_raw%d" % first)
            nc.sync.dma_start(out=raw[:], in_=x_cases[g][:, c : c + count, :])
            for n in range(count):
                x_raw[first + n] = raw[:, n, :]
                x_rows[first + n] = raw[:, n:count, :].rearrange("p c k -> p (c k)")

        scale_cols = keep.tile([P, HALVES, PACK], F32, name="scale_cols")
        beta_codes = keep.tile([P, HALVES, K * PACK], U8, name="beta_codes", align_bytes=ALIGN)
        p_codes = []
        for h in range(2):
            p_codes.append(keep.tile([P, HALVES, HALF * PACK], U8, name="p_codes%d" % h, align_bytes=ALIGN))
        p_by_partition = p_words.rearrange("g p n c -> p g (n c)")

        def load_p(h):
            nc.sync.dma_start(out=p_codes[h][:], in_=p_by_partition[:, :, h * HALF * PACK : (h + 1) * HALF * PACK])

        rt_rows = keep.tile([P, P * PACK], BF16, name="rt_rows")
        nc.vector.memset(rt_rows[:], 0.0)
        v_in = {}

        def load_v(lo, hi):
            rows = keep.tile([P, hi - lo, K], BF16, name="v_rows%d" % lo)
            nc.sync.dma_start(out=rows[:], in_=v.rearrange("(m p) k -> p m k", p=P)[:, lo:hi, :])
            for m in range(lo, hi):
                v_in[m] = rows[:, m - lo, :]

        psi_rows = keep.tile([P, P], BF16, name="psi_rows")
        nc.vector.memset(psi_rows[:], 0.0)
        ident_bf16 = keep.tile([P, P], BF16, name="ident_bf16")

        def load_row_factor(w, vec):
            nc.sync.dma_start(out=rt_rows[w * GROUPS : (w + 1) * GROUPS, :], in_=vec.rearrange("(g n) -> g n", g=GROUPS))

        load_x(0, 2)
        nc.scalar.dma_start(out=scale_cols[:], in_=x_scale.rearrange("o (j p c) -> p (o j) c", p=P, c=PACK))
        load_x(2, 2)
        load_scales(beta_rows, beta_scales)
        nc.sync.dma_start(out=beta_codes[:], in_=beta_words.rearrange("g p n c -> p g (n c)"))
        load_x(4, 2)
        load_row_factor(T, t)
        load_row_factor(R, r)
        load_p(0)
        load_scales(p_rows, p_scales)
        load_x(6, 2)
        nc.sync.dma_start(out=psi_rows[0:OUT_TILES, :], in_=psi.rearrange("(m p) -> m p", p=P))
        load_x(8, 4)
        load_v(0, EARLY_V)
        load_p(1)
        load_x(12, 4)
        load_v(EARLY_V, OUT_TILES)

        rt = keep.tile([P, 2, TILES], F32, name="rt")
        inv_psi = keep.tile([P, OUT_TILES], F32, name="inv_psi")
        gain = keep.tile([P, OUT_TILES], F32, name="gain")

        x_codes, x_code_scales, codes, code_scales = [], [], [], []
        for s in range(PAIRS):
            x_codes.append(keep.tile([P, 2, HALVES * P], U32, name="x_codes%d" % s, align_bytes=ALIGN))
            x_code_scales.append(keep.tile([P, 2, HALVES * P], U8, name="x_code_scales%d" % s, align_bytes=ALIGN))
        for g in range(GROUPS):
            codes.append(keep.tile([P, WIDE], U32, name="codes%d" % g, align_bytes=ALIGN))
            code_scales.append(keep.tile([P, WIDE], U8, name="code_scales%d" % g, align_bytes=ALIGN))

        idle_bank = next_bank("idle", [P, 3 * P])

        def keep_busy(blocks, width=P):
            nc.tensor.matmul(
                out=idle_bank[:, 0 : blocks * width].rearrange("p (a n) -> p a n", a=blocks),
                lhsT=zeros[:],
                rhs=zeros[:, 0:width].unsqueeze(1).to_broadcast([P, blocks, width]),
                start=True,
                stop=True,
            )

        spread = {}

        def turn_rt():
            spread["rt"] = next_bank("rt", [P, 2, P])
            for u in range(2):
                nc.tensor.transpose(spread["rt"][:, u, :], rt_rows[:].bitcast(F32)[:, u : 2 * P : 2], ident[:])

        def copy_rt():
            nc.scalar.copy(
                out=rt[:].rearrange("p w (g u e) -> p u (w g) e", u=2, e=2),
                in_=spread["rt"][:, :, 0 : 2 * GROUPS].bitcast(BF16).rearrange("p u (k e) -> p u k e", e=2),
            )
            release("rt")

        def turn_psi():
            spread["psi"] = next_bank("psi", [P, P], BF16)
            nc.tensor.transpose(spread["psi"][:], psi_rows[:], ident_bf16[:])

        def invert_psi():
            nc.vector.reciprocal(out=inv_psi[:], in_=spread["psi"][:, 0:OUT_TILES])
            release("psi")

        def make_gain():
            nc.scalar.activation(out=gain[:], in_=inv_psi[:], func=COPY, scale=1.0 / N)

        words_of, transposed, woven_x = {}, {}, {}

        def widen(i, lo=0, hi=HALVES):
            tile = widened_pool.tile([P, (hi - lo) * HALF], BF16, name="widened", bufs=5)
            nc.scalar.copy(out=tile[:], in_=x_raw[i][:, lo * HALF : hi * HALF].bitcast(FP8))
            for j in range(lo, hi):
                for u in range(2):
                    words_of[i, j, u] = tile[:].bitcast(F32)[:, 2 * P * (j - lo) + u : 2 * P * (j - lo + 1) : 2]

        def widen_sorted(i, lo=0, hi=HALVES):
            tile = widened_pool.tile([P, 2, hi - lo, P, 2], BF16, name="sorted", bufs=4)
            nc.vector.tensor_scalar(
                out=tile[:].rearrange("p u b q e -> p (b q) u e"),
                in0=x_rows[i][:, lo * HALF : hi * HALF].bitcast(FP8).rearrange("p (q u e) -> p q u e", u=2, e=2),
                scalar1=ones[:],
                scalar2=None,
                op0=MULT,
            )
            for b in range(lo, hi):
                for u in range(2):
                    words_of[i + b // HALVES, b % HALVES, u] = tile[:, u, b - lo, :, :].rearrange("p q e -> p (q e)").bitcast(F32)

        def transpose(i, lo=0, hi=HALVES):
            bank = next_bank(("x", i, hi), [P, 2, HALVES, P])
            for j in range(lo, hi):
                transposed[i, j] = bank
                for u in range(2):
                    nc.tensor.transpose(bank[:, u, j, :], words_of[i, j, u], ident[:])

        def scale_out(i, lo=0, hi=HALVES):
            s, h = divmod(i, 2)
            if s not in woven_x:
                woven_x[s] = keep.tile([P, 2, HALVES * P * PACK], BF16, name="woven_x%d" % s, align_bytes=64)
            nc.vector.tensor_tensor(
                out=woven_x[s][:, h, lo * P * PACK : hi * P * PACK].rearrange("p (j m u e) -> p j m u e", m=P, u=2, e=2),
                in0=transposed[i, lo][:, :, lo:hi, :].bitcast(BF16).rearrange("p u j (m e) -> p j m u e", e=2),
                in1=scale_cols[:, lo:hi, :].rearrange("p j (u e) -> p j u e", e=2).unsqueeze(2).to_broadcast([P, hi - lo, P, 2, 2]),
                op=MULT,
            )
            if ("x", i, hi) in bank_of:
                release(("x", i, hi))

        def quantize_x(i, lo=0, hi=HALVES):
            s, h = divmod(i, 2)
            nc.vector.quantize_mx(
                out=x_codes[s][:, h, lo * P : hi * P].bitcast(X4),
                scales=x_code_scales[s][:, h, lo * P : hi * P],
                in_=woven_x[s][:, h, lo * P * PACK : hi * P * PACK],
            )

        weights = (beta_codes, p_codes[0], p_codes[1])
        weight_scales = (beta_rows[:, 0:K], p_rows[:, 0:HALF], p_rows[:, HALF:D])

        def multiply(bank, i, part, first, width, halves=range(HALVES)):
            s, h = divmod(i, 2)
            for j in halves:
                cols = slice(j * P, (j + 1) * P)
                nc.tensor.matmul_mx(
                    out=bank,
                    lhsT=x_codes[s][:, h, cols].bitcast(X4),
                    lhsT_scale=x_code_scales[s][:, h, cols],
                    rhs=weights[part][:, j, first * PACK : (first + width) * PACK].bitcast(X4),
                    rhs_scale=weight_scales[part][4 * j : P, first : first + width],
                    start=(j == 0),
                    stop=(j == HALVES - 1),
                )

        products, planes, woven = {}, {}, {}

        def plane(g, lo, hi):
            part = lo // K
            if (g, part) not in planes:
                planes[g, part] = keep.tile([P, PACK, K], BF16, name="planes%d_%d" % (g, part))
            return planes[g, part][:, :, lo - part * K : hi - part * K]

        def multiply_wide(part, i, first=0):
            products[part, i] = next_bank((part, i), [P, K - first])
            multiply(products[part, i][:], i, part, first, K - first)

        def scale_wide(part, i, first=0):
            g, c = divmod(i, PACK)
            nc.scalar.activation(
                out=plane(g, part * K + first, (part + 1) * K)[:, c, :],
                in_=products[part, i][:],
                func=COPY,
                scale=rt[:, R if part else T, g * PACK + c : g * PACK + c + 1],
            )
            release((part, i))

        def wide(part, i, first=0):
            multiply_wide(part, i, first)
            scale_wide(part, i, first)

        def new_woven(g, lo, hi, buffer=None):
            woven[g, lo] = keep.tile([P, hi - lo, PACK], BF16, name=buffer or "woven%d_%d" % (g, lo), align_bytes=64)

        def woven_columns(g, lo, hi):
            first = max(n for (h, n) in woven if h == g and n <= lo)
            return woven[g, first][:, lo - first : hi - first, :]

        def weave(g, lo, hi):
            nc.scalar.copy(
                out=woven_columns(g, lo, hi).rearrange("p (b n) c -> p b c n", n=4),
                in_=plane(g, lo, hi).rearrange("p c (b n) -> p b c n", n=4),
            )

        def weave_gpsimd(g, lo, hi):
            nc.gpsimd.tensor_scalar(
                out=woven_columns(g, lo, hi),
                in0=plane(g, lo, hi).rearrange("p c n -> p n c"),
                scalar1=1.0,
                scalar2=0.0,
                op0=MULT,
                op1=ADD,
            )

        def quantize(g, lo):
            hi = lo + woven[g, lo].shape[1]
            nc.vector.quantize_mx(
                out=codes[g][:, lo:hi].bitcast(X4),
                scales=code_scales[g][:, lo:hi],
                in_=woven[g, lo][:].rearrange("p n c -> p (n c)"),
            )

        def multiply_narrow(g, part, chunks):
            for chunk in chunks:
                products[g, part, chunk] = next_bank((g, part, chunk), [P, PACK, P])
            for c in range(PACK):
                for j in range(HALVES):
                    for chunk in chunks:
                        multiply(products[g, part, chunk][:, c, :], g * PACK + c, part, P * chunk, P, (j,))

        def scale_narrow(g, part, chunk, width=K // P):
            lo = part * K + chunk // width * width * P
            if chunk % width == 0:
                woven[g, lo] = keep.tile([P, width * P, PACK], BF16, name="woven%d_%d" % (g, lo), align_bytes=64)
            factors = rt[:, R if part else T, g * PACK : (g + 1) * PACK]
            nc.vector.tensor_tensor(
                out=woven[g, lo][:, P * (chunk % width) : P * (chunk % width + 1), :],
                in0=products[g, part, chunk][:].rearrange("p c n -> p n c"),
                in1=factors.unsqueeze(1).to_broadcast([P, P, PACK]),
                op=MULT,
            )
            release((g, part, chunk))

        sums, added, v_scaled = {}, {}, {}

        def contract(m, groups, lo=0, hi=K):
            if (m, lo) not in sums:
                sums[m, lo] = next_bank(("c", m, lo), [P, K])
                added[m, lo] = -1
            cols = slice(K + P * m, K + P * (m + 1))
            for g in groups:
                added[m, lo] = added[m, lo] + 1
                nc.tensor.matmul_mx(
                    out=sums[m, lo][:, 0 : hi - lo],
                    lhsT=codes[g][:, cols].bitcast(X4),
                    lhsT_scale=code_scales[g][:, cols],
                    rhs=codes[g][:, lo:hi].bitcast(X4),
                    rhs_scale=code_scales[g][:, lo:hi],
                    start=(added[m, lo] == 0),
                    stop=(added[m, lo] == GROUPS - 1),
                )

        def scale_v(m):
            v_scaled[m] = result_pool.tile([P, K], F32, name="v_scaled", bufs=6)
            nc.scalar.activation(out=v_scaled[m][:], in_=v_in[m], func=COPY, scale=inv_psi[:, m : m + 1])

        def scale_v_gpsimd(m):
            v_scaled[m] = keep.tile([P, K], F32, name="v_scaled%d" % m, align_bytes=64)
            nc.gpsimd.tensor_scalar(
                out=v_scaled[m][:], in0=v_in[m], scalar1=inv_psi[:, m : m + 1], scalar2=0.0, op0=MULT, op1=ADD
            )

        def finish(m, lo=0, hi=K):
            result = result_pool.tile([P, K], F32, name="result")
            nc.vector.scalar_tensor_tensor(
                out=result[:, lo:hi],
                in0=sums[m, lo][:, 0 : hi - lo],
                scalar=gain[:, m : m + 1],
                in1=v_scaled[m][:, lo:hi],
                op0=MULT,
                op1=SUBTRACT,
            )
            release(("c", m, lo))
            nc.sync.dma_start(out=out[P * m : P * (m + 1), lo:hi], in_=result[:, lo:hi])

        def products_of(pair, parts, first=0):
            for part in parts:
                for i in (2 * pair, 2 * pair + 1):
                    wide(part, i, first if part == E1 else 0)

        def weave_share(g, part, buffer, share=SHARE):
            new_woven(g, part * K, (part + 1) * K, buffer)
            weave_gpsimd(g, part * K, part * K + share)

        def weave_rest(g, part, share=SHARE):
            weave(g, part * K + share, (part + 1) * K)

        def weave_quarter(g, lo, buffer=None):
            new_woven(g, lo, lo + QUARTER, buffer)
            weave(g, lo, lo + QUARTER)

        keep_busy(2)
        keep_busy(3)
        nc.vector.tensor_copy(out=ident_bf16[:], in_=ident[:])
        for j in range(HALVES):
            widen_sorted(0, j, j + 1)
        widen_sorted(1, 0, 1)
        widen(1, 1, 2)
        for i in range(2, 6):
            widen(i)
        for j in range(HALVES):
            transpose(0, j, j + 1)
        keep_busy(2)
        release("idle")
        transpose(1)
        for j in range(HALVES):
            scale_out(0, j, j + 1)
        for j in range(HALVES):
            quantize_x(0, j, j + 1)
        transpose(2)
        multiply_wide(Z, 0)
        turn_rt()
        copy_rt()
        scale_wide(Z, 0)
        widen(6, 0, 1)
        scale_out(1)
        transpose(3)
        transpose(4)
        for i in (1, 2):
            scale_out(i + 1, 0, 1)
            quantize_x(i)
            scale_out(i + 1, 1, 2)
        wide(Z, 1)
        wide(E0, 0)
        wide(E0, 1)
        wide(Z, 2)
        wide(E0, 2)
        widen_sorted(6, 1, 2 * HALVES)
        quantize_x(3)

        turn_psi()
        for i in (5, 6, 7):
            transpose(i)
        widen_sorted(8)
        invert_psi()
        widen_sorted(9)
        for m in (0, 1):
            scale_v_gpsimd(m)
        for m in range(2, EARLY_V):
            scale_v(m)
        scale_out(4)
        scale_out(5)
        wide(Z, 3)
        wide(E0, 3)
        quantize_x(4)
        quantize_x(5)
        weave_share(0, Z, "woven_x2")
        widen_sorted(10, 0, 2 * HALVES)
        for i in range(PACK):
            wide(E1, i)
        products_of(2, (Z,))
        scale_out(6)
        scale_out(7)
        products_of(2, (E0, E1))
        quantize_x(6)
        quantize_x(7)
        weave_share(0, E0, "woven_x3")
        widen_sorted(12, 0, 2 * HALVES)

        for i in range(8, 12):
            transpose(i)
        scale_out(8)
        scale_out(9)
        weave_rest(0, Z)
        weave_rest(0, E0)
        make_gain()
        products_of(3, (Z,))
        quantize_x(8)
        quantize_x(9)
        weave_share(1, Z, "woven_x4")
        widen_sorted(14, 0, 2 * HALVES)
        products_of(3, (E0, E1))
        products_of(4, (Z,))
        scale_out(10)
        scale_out(11)
        products_of(4, (E0, E1), QUARTER)
        quantize_x(10)
        quantize_x(11)
        weave_share(1, E0, "woven_x5")
        quantize(0, Z * K)

        for i in range(12, 16):
            transpose(i)
        scale_out(12)
        scale_out(13)
        weave_rest(1, Z)
        weave_rest(1, E0)
        products_of(5, (Z,))
        quantize_x(12)
        quantize_x(13)
        weave_share(2, Z, "woven_x6")
        quantize(1, Z * K)
        products_of(5, (E0, E1), QUARTER)
        products_of(6, (Z,))
        scale_out(14)
        scale_out(15)
        products_of(6, (E0,))
        quantize_x(14)
        quantize_x(15)

        multiply_narrow(2, E1, (0, 1))
        weave_rest(2, Z)
        weave_quarter(0, E1 * K)
        quantize(1, E0 * K)
        weave_share(2, E0, "woven_x5", QUARTER)
        quantize(0, E0 * K)
        products_of(7, (Z, E0))
        weave_rest(2, E0, QUARTER)
        for chunk in range(2):
            scale_narrow(2, E1, chunk, 2)
        quantize(0, E1 * K)
        quantize(2, Z * K)
        weave_share(3, Z, "woven_x6")
        quantize(2, E1 * K)
        for chunk in range(4):
            multiply_narrow(3, E1, (chunk,))
            scale_narrow(3, E1, chunk)
        weave_rest(3, Z)
        weave_quarter(3, E0 * K)
        weave_quarter(3, E0 * K + QUARTER)
        weave_quarter(1, E1 * K, "woven_x0")

        quantize(2, E0 * K)
        quantize(3, Z * K)
        quantize(3, E0 * K)
        for g in (0, 1):
            for m in range(4):
                contract(m, (g,))
        for g in (2, 3):
            for m in (0, 1):
                contract(m, (g,))
        quantize(3, E1 * K)
        new_woven(1, E1 * K + QUARTER, WIDE, "woven3_1024")
        weave_gpsimd(1, E1 * K + QUARTER, WIDE)
        quantize(3, E0 * K + QUARTER)
        for g in (2, 3):
            for m in (2, 3):
                contract(m, (g,))
        weave_quarter(0, E1 * K + QUARTER, "woven_x1")
        weave_quarter(2, E1 * K + QUARTER, "woven_x3")
        for m in range(EARLY_V, OUT_TILES):
            scale_v(m)
        for m in range(3):
            finish(m)
        for m in (4, 5):
            contract(m, (3, 2, 0))
        quantize(1, E1 * K)
        quantize(1, E1 * K + QUARTER)
        quantize(0, E1 * K + QUARTER)
        for m in (4, 5):
            contract(m, (1,))
        finish(3)
        quantize(2, E1 * K + QUARTER)
        finish(4)
        contract(6, (3, 1, 0, 2))
        finish(5)

        contract(7, range(GROUPS), 0, QUARTER)
        finish(6)
        contract(7, range(GROUPS), QUARTER, K)
        finish(7, 0, QUARTER)
        finish(7, QUARTER, K)
